import numpy as np, ml_dtypes
CORES = [2,6,10,14,18,22,26,30]
N = 8
BF = ml_dtypes.bfloat16
W, L, ST = 4096, 512, 8
STEPS = (5, 2, 7)
def look(X, J, z, w, A):
    u = np.sum(w * z, axis=2) & 1023
    h = (((J * (2 * u + 1)[:, :, None, :]) >> 5) + J + A[:, None, None, None]) & (W - 1)
    x = np.take_along_axis(X, h.reshape(N, 8, 1, 16 * L), 3).reshape(N, 8, 16, 16, L)
    m = np.minimum(x, z[:, :, :, None, :])
    return u, x, np.sum(m, axis=2), 1 + np.sum(x - m, axis=2)
def parts(rng):
    top = rng.integers(6, 16, (N, 8, 1, W))
    X = rng.integers(0, top + 1, (N, 8, 16, W)); J = rng.integers(0, W, (N, 8, 16, L))
    return X, J, rng.integers(1, 16, (N, 8, 16, L)), rng.integers(0, 64, (N, 8, 16, 1))
def pack(X, J, z, w):
    return {"xt": X.reshape(N, 128, W).astype(np.float32).astype(BF), "jn": np.ascontiguousarray(J.reshape(N, 128, L)).astype(np.int32),
            "zd": z.reshape(N, 128, L).astype(np.float32).astype(BF), "wt": w.reshape(N, 128, 1).astype(np.float32)}
def setup_inputs(rng):
    return pack(*parts(rng))
def uphill(X, J, z, w):
    u, x, g, s = look(X, J, z, w, np.zeros(N, np.int64))
    o = np.argsort(g * np.power(s.astype(np.float64), -1.0), axis=2, kind="stable")
    return np.take_along_axis(J, o, 2)
def setup_inputs_corners(rng):
    X, J, z, w = parts(rng)
    w[:, 2] = 0; w[:, 2, :4] = 63; w[:, 2, 4] = 21; J[:, 2] = rng.integers(W - 120, W, (N, 16, L))
    w[:, 3] = 63; X[:, 3, :, 0] = 15; J[:, 3, 1:8] = W - 1 - 32 * rng.integers(0, 12, (N, 7, L)); J[:, 3, 15] = 0
    J[:, :, 0, :4] = 0; J[:, :, 1, :4] = W - 1
    c = W - 1 - 32 * np.arange(12); h = ((c * 2017 >> 5) + c + 128 * L) & (W - 1)
    X[0, 3][:, h] = 1; X[0, 3][:, (h + 1) & (W - 1)] = 15
    lead = np.concatenate([J[STEPS[0], 3, 1:], J[STEPS[0], 3, :1]], axis=0)
    strong = np.zeros((N, 8, 1, L), bool); short = np.zeros((N, 8, 1, L), bool); near = np.zeros((N, 8, 1, L), bool); m = 0
    for r in range(N):
        q = r ^ STEPS[0]
        if r > q: continue
        if m == 0: strong[r] = True
        elif m == 1:
            strong[q] = True; near[q, 7, 0, L - 1] = True
        else:
            strong[r, ::2] = True; strong[q, 1::2] = True
            strong[q, 1, 0, 0] = False; strong[r, 1, 0, 0] = True; strong[r, 6, 0, L - 1] = False; strong[q, 6, 0, L - 1] = True
            if m == 3:
                short[r] = True; short[q] = True
        m += 1
    z = np.where(strong, 15, 1) + np.zeros((1, 1, 16, 1), np.int64)
    up = uphill(X, J, z, w); down = up[:, :, ::-1]; most = np.concatenate([up[:, :, 1:], up[:, :, :1]], axis=2)
    J = np.where(strong, np.where(short, down, np.where(near, most, up)), J)
    for r in range(N):
        for g in range(8): J[r, g] = np.where(strong[r, g], J[r, g], up[r, g]) if g == 3 and r != STEPS[0] else J[r, g]
    J[STEPS[0], 3] = lead
    return pack(X, J, z, w)
def setup_inputs_crowd(rng):
    X, J, z, w = parts(rng); c = rng.integers(0, W, (N, 8)); c[0, 0] = 0; c[1, 0] = W - 1
    for g in (0, 4, 1, 5):
        J[:, g] = c[:, g][:, None, None]; z[:, g] = z[:, g, :, :1].copy()
    for g, o in ((1, int(rng.integers(0, L))), (5, L - 1)):
        J[:, g, :, o] = rng.integers(0, W, (N, 16)); z[:, g, :, o] = rng.integers(1, 16, (N, 16))
    for g in (2, 6): J[:, g] = rng.choice(np.array([0, 3, W // 2, W - 1]), (N, 16, L))
    for g in (3, 7): J[:, g] = J[:, g, :1].copy()
    for a in (X, J, z, w): a[:, 4] = a[0, 4].copy()
    return pack(X, J, z, w)
def setup_inputs_ends(rng):
    X = 15 * rng.integers(0, 2, (N, 8, 16, W)); X[:, 1::2] = 15 * rng.integers(0, 2, (N, 4, 1, W))
    J = (W - 1) * rng.integers(0, 2, (N, 8, 16, L)); kind = rng.integers(0, 3, (N, 8, 1, L))
    z = np.where(kind == 0, 1, np.where(kind == 1, 15, 1 + 14 * rng.integers(0, 2, (N, 8, 16, L))))
    w = 63 * rng.integers(0, 2, (N, 8, 16, 1)); w[:, 5] = 63
    for g in (0, 3, 7): w[:, g] = 0
    c = W // 32 - 2
    X[:, 0, :, 0] = 0; X[:, 0, :, c] = 0
    X[:, 3, :, 0] = 15; X[:, 3, :, c] = 15; X[:, 3, 0, c] = 0
    J[:, 3, :, -8:] = 0; J[:, 3, 0, -8:] = W - 1; z[:, 3, :, -8:] = 15
    X[:, 7, :, 0] = 15; X[:, 7, :, c] = 15; X[:, 7, 0, c] = 0
    duo = np.array([[0, 0], [0, 1], [1, 0], [1, 1], [2, 2], [2, 3], [3, 2], [3, 3], [4, 4]])
    pn = rng.integers(0, 9, L); pn[:9] = rng.permutation(9); pn[L - 1] = 8; pn[L - 2] = 5; pn[L - 3] = 0; pn[L - 4] = 7; pn[L - 5] = 6
    for r in range(N):
        if r < (r ^ STEPS[0]): X[r, 3, 1, c] = 14
        kd = duo[pn, int(r > (r ^ STEPS[0]))]
        J[r, 7] = 0; J[r, 7, 0] = np.where(kd >= 2, W - 1, 0)
        z[r, 7] = np.where((kd == 0) | (kd == 2), 15, 1)
        z[r, 7, :7] = np.where(kd == 4, 15, z[r, 7, :7])
    return pack(X, J, z, w)
def setup_inputs_spread(rng):
    def e(*shape): return np.exp2(rng.integers(-2, 4, shape))
    X = np.minimum((16 * rng.random((N, 8, 16, W)) ** e(N, 8, 1, W)).astype(np.int64), 15)
    J = np.minimum((W * rng.random((N, 8, 16, L)) ** e(N, 8, 1, L)).astype(np.int64), W - 1)
    z = np.minimum(1 + (15 * rng.random((N, 8, 16, L)) ** e(N, 8, 1, L)).astype(np.int64), 15)
    w = np.minimum((64 * rng.random((N, 8, 16, 1)) ** e(N, 8, 16, 1)).astype(np.int64), 63)
    high = [r for r in range(N) if r > (r ^ STEPS[0])]; few = 1 + rng.permutation(3)
    for r, n in zip(high[1:], few):
        at = np.array([L - 1, 0, L // 2])[:int(n)]
        X[r, :, :, ::4] = 0; J[r] = J[r] & -128
        w[r, 7] = 0; X[r, 7, :, 1] = 15
        J[r, 7, 0][at] = 1; z[r, 7][:, at] = 15; z[r ^ STEPS[0], 7][:, at] = 1
    return pack(X, J, z, w)
def setup_inputs_ties(rng):
    X, J, z, w = parts(rng); v = rng.integers(0, 16, (8, 16)); v[:, 0] = 15; v[:, 1] = 0
    ix = (np.arange(16)[None, None, :, None] + rng.integers(0, 16, (N, 8, 1, W))) & 15
    X = np.where(rng.random((N, 8, 1, W)) < 0.0625, X, v[np.arange(8)[None, :, None, None], ix])
    one = rng.integers(1, 16, (N, 8, 1, L)); one[:, ::2] = one[0, ::2].copy(); one[:, 7] = one[0, 7].copy()
    w[:, 6] = 0; kd = rng.integers(0, 4, L); kd[:4] = rng.permutation(4); kd[L - 4:] = rng.permutation(4)
    for c, g, s, d, n in ((1, 100, 61, 8, 9), (2, 120, 57, 8, 9), (3, 110, 51, 8, 9), (4, 108, 50, 8, 9), (5, 113, 53, 8, 9), (6, 56, 131, 4, 12), (7, 60, 87, 4, 12), (8, 60, 86, 4, 12)):
        X[:, 6, :n, c] = d + (s - 1 + np.arange(n)) // n
        X[:, 6, n:, c] = (g - d * n + np.arange(16 - n)) // (16 - n)
    for m, d, p, lo, hi in ((0, 8, 1, 2, 3), (1, 8, 1, 4, 5), (2, 4, 6, 7, 8)):
        at = kd == m; one[:, 6, 0, at] = d
        for r in range(N):
            J[r, 6][:, at] = p; J[r, 6, 15, at] = hi if r > (r ^ STEPS[0]) else lo
    return pack(X, J, one + np.zeros((1, 1, 16, 1), np.int64), w)
def check_inputs(d):
    bad = []
    for k, lo, hi in (("xt", 0, 15), ("jn", 0, W - 1), ("zd", 1, 15), ("wt", 0, 63)):
        a = np.asarray(d[k]).astype(np.float64)
        if not np.all((a >= lo) & (a <= hi)): bad.append("range of " + k)
        if not np.all(a == np.floor(a)): bad.append("whole numbers of " + k)
    return bad
def reference(xt, jn, zd, wt):
    X = xt.astype(np.float32).astype(np.int64).reshape(N, 8, 16, W); J = jn.astype(np.int64).reshape(N, 8, 16, L)
    z = zd.astype(np.float32).astype(np.int64).reshape(N, 8, 16, L); w = wt.astype(np.int64).reshape(N, 8, 16, 1)
    A = np.zeros(N, np.int64); r = np.arange(N); k16 = np.arange(16)
    for step in STEPS:
        q = r ^ step
        u, x, g, s = look(X, J, z, w, A)
        G = np.add.accumulate(g, axis=2); S = np.add.accumulate(s, axis=2)
        bG, bS, b = G[:, :, 0], S[:, :, 0], np.zeros((N, 8, L), np.int64)
        for k in range(1, 16):
            up = G[:, :, k] * bS > bG * S[:, :, k]
            bG = np.where(up, G[:, :, k], bG); bS = np.where(up, S[:, :, k], bS); b = np.where(up, k, b)
        y = np.max(np.where(k16[None, None, None, :, None] <= b[:, :, None, None, :], x, 0), axis=3)
        mine = bG * bS[q]; other = bG[q] * bS
        win = (mine > other) | ((mine == other) & (r < q)[:, None, None]); ww = win[:, :, None, :]
        both = np.concatenate([J, J[q]], axis=2)
        spliced = np.take_along_axis(both, k16[None, None, :, None] + (b + 1)[:, :, None, :], 2)
        col = (ST * np.arange(L)[None, None, :] + (u & (ST - 1)))[:, :, None, :]
        old = np.take_along_axis(X, col, 3)
        np.put_along_axis(X, np.broadcast_to(col, old.shape), np.where(ww, (old + y) >> 1, old), 3)
        z = np.where(ww, np.maximum(np.abs(z - y), 1), np.maximum((z + y[q]) >> 1, 1))
        J = np.where(ww, spliced, J)
        A = np.sum(np.where(win, b + 1, 0), axis=(1, 2))
    out = X[..., :W // 2] + 16 * X[..., W // 2:]
    return {"yx": out.reshape(N, 128, W // 2).astype(np.float32).astype(BF), "yj": J.reshape(N, 128, L).astype(np.float32), "yz": z.reshape(N, 128, L).astype(np.float32).astype(BF)}

@@ -1,0 +1,423 @@
+from concourse.mybir import AluOpType as OP, AxisListType as AX, ActivationFunctionType as AF
+
+STEPS = (5, 2, 7)
+BIG = 8192.0
+F, B, I, U = "float32", "bfloat16", "int32", "uint16"
+
+SCRATCH = {
+    "X": ("sbuf", [128, 4608], B),
+    "xg": ("sbuf", [128, 8192], B), "mg": ("sbuf", [128, 8192], B), "pg": ("sbuf", [128, 8192], B),
+    "ji": ("sbuf", [128, 512], I), "z": ("sbuf", [128, 512], B), "w": ("sbuf", [128, 1], F),
+    "jo": ("sbuf", [128, 512], F), "pi": ("sbuf", [128, 512], I), "hu": ("sbuf", [128, 512], U),
+    "yy": ("sbuf", [128, 512], B), "vv": ("sbuf", [128, 512], B), "nv": ("sbuf", [128, 512], B),
+    "t1": ("sbuf", [128, 512], B), "t2": ("sbuf", [128, 512], B), "nb": ("sbuf", [128, 512], B),
+    "cz": ("sbuf", [128, 1024], B), "yo": ("sbuf", [128, 2048], B),
+    "s0": ("sbuf", [128, 256], F), "s1": ("sbuf", [128, 128], F), "s2": ("sbuf", [128, 64], F), "s3": ("sbuf", [128, 32], F),
+    "p1": ("sbuf", [128, 128], F), "cc": ("sbuf", [128, 128], F), "cgk": ("sbuf", [128, 128], F),
+    "fin": ("sbuf", [128, 96], F), "wa": ("sbuf", [128, 48], F), "sig": ("sbuf", [128, 32], F), "a1": ("sbuf", [128, 1], F),
+    "zz": ("sbuf", [128, 128], B), "oy": ("sbuf", [128, 32], U), "of": ("sbuf", [128, 48], F), "ou": ("sbuf", [128, 96], U),
+    "ri": ("sbuf", [128, 32], I), "cu": ("sbuf", [128, 32], U),
+    "one": ("sbuf", [128, 256], B), "idb": ("sbuf", [128, 128], B), "idn": ("sbuf", [128, 128], B), "id16": ("sbuf", [128, 128], B),
+    "idm": ("sbuf", [128, 128], B), "idf": ("sbuf", [128, 128], F), "o32": ("sbuf", [128, 128], F), "bd": ("sbuf", [128, 128], B),
+    "bdw": ("sbuf", [128, 128], B), "bdw2": ("sbuf", [128, 128], B), "qw": ("sbuf", [128, 144], B), "cst": ("sbuf", [128, 128], B),
+    "rx": ("sbuf", [128, 32], B), "pat": ("sbuf", [128, 512], B), "mp": ("sbuf", [128, 2048], B),
+    "m192": ("sbuf", [128, 256], B), "zo": ("sbuf", [128, 8], U), "zm": ("sbuf", [128, 128], B), "ro": ("sbuf", [128, 112], B),
+    "co": ("sbuf", [128, 112], F), "cm": ("sbuf", [128, 96], F), "c8": ("sbuf", [128, 32], F),
+    "i1": ("sbuf", [128, 128], I), "i2": ("sbuf", [128, 128], I), "i3": ("sbuf", [128, 16], I), "i4": ("sbuf", [128, 16], I),
+    "i5": ("sbuf", [128, 16], I), "pc": ("sbuf", [128, 2], F), "il": ("sbuf", [128, 16], F),
+    "ZU0": ("psum", [128, 512], F), "ZU1": ("psum", [128, 512], F), "GS0": ("psum", [128, 512], F), "GS1": ("psum", [128, 512], F),
+    "TV": ("psum", [128, 512], F), "DZ": ("psum", [128, 512], F), "SR": ("psum", [128, 512], F), "LL": ("psum", [128, 512], F),
+}
+SEMAPHORES = ["cv", "cs", "cp", "cg", "ldx", "ldj", "ldz", "ldw", "sy0", "sy1", "sj0", "sj1", "sz0", "sz1"]
+for _t in range(3):
+    for _c in range(2):
+        SCRATCH["W%d%d" % (_t, _c)] = ("sbuf", [128, 17 * 256], F)
+        SCRATCH["D%d%d" % (_t, _c)] = ("dram", [8, 32, 256], F)
+        SCRATCH["RG%d%d" % (_t, _c)] = ("sbuf", [128, 32], F)
+        SCRATCH["RY%d%d" % (_t, _c)] = ("sbuf", [128, 256], B)
+        for _k in ("aj", "ag", "ay", "lj", "lg", "ly", "do", "dr", "dt"):
+            SEMAPHORES.append("%s%d%d" % (_k, _t, _c))
+BANKS = ("ZU0", "ZU1", "GS0", "GS1", "TV", "DZ", "SR", "LL")
+ESEM = {"v": "cv", "s": "cs", "p": "cp", "g": "cg"}
+
+
+def weave(a, b):
+    out, n = [], max(len(a), 1)
+    done = 0
+    for i, o in enumerate(a):
+        out.append(o)
+        upto = (i + 1) * len(b) // n
+        out.extend(b[done:upto])
+        done = upto
+    return out + b[done:]
+
+
+def emit(g, T, ops):
+    Q = {"v": g.vector, "s": g.scalar, "p": g.tensor, "g": g, "y": g.sync}
+    cnt = {e: 0 for e in ESEM}
+    know = {e: {} for e in Q}
+    clock = {}
+    lastw, readers, bank, total = {}, {}, {}, {}
+    for eng, fn, rd, wr, tok in ops:
+        deps = []
+        for k in rd:
+            if k not in BANKS:
+                deps += lastw.get(k, [])
+        for k in wr:
+            if k not in BANKS:
+                deps += lastw.get(k, []) + readers.get(k, [])
+        for k in rd + wr:
+            if k in BANKS:
+                deps += [t for e, t in bank.get(k, {}).items() if e != eng]
+        if eng == "p":
+            deps = [d for d in deps if d[0] != "cp"]
+        if fn is not None:
+            kn = know[eng]
+            for d in sorted(set(deps), key=lambda d: -d[1]):
+                if kn.get(d[0], 0) < d[1] and d != tok:
+                    Q[eng].wait_ge(T.sem[d[0]], d[1])
+                    kn[d[0]] = d[1]
+                    for s, v in clock.get(d, {}).items():
+                        kn[s] = max(kn.get(s, 0), v)
+            ins = fn(Q[eng])
+            if tok is None:
+                cnt[eng] += 1
+                tok = (ESEM[eng], cnt[eng])
+                ins.then_inc(T.sem[tok[0]], 1)
+            elif ins is not None:
+                ins.then_inc(T.sem[tok[0]], 16)
+            ck = clock.setdefault(tok, {})
+            for s, v in kn.items():
+                ck[s] = max(ck.get(s, 0), v)
+        total[tok[0]] = max(total.get(tok[0], 0), tok[1])
+        for k in rd:
+            if k not in BANKS:
+                readers.setdefault(k, []).append(tok)
+        for k in wr:
+            if k not in BANKS:
+                lastw[k] = [tok]
+                readers[k] = []
+        for k in rd + wr:
+            if k in BANKS:
+                bank.setdefault(k, {})[eng] = tok
+    for s, v in total.items():
+        if know["g"].get(s, 0) < v:
+            g.wait_ge(T.sem[s], v)
+
+
+def rank_program(g, core, T, topo):
+    rank = T.rank_of(core)
+    if rank is None:
+        return
+    ops = []
+
+    def o(eng, fn, rd, wr, tok=None):
+        return (eng, fn, list(rd), list(wr), tok)
+
+    def tt(out, a, b, op, rd, wr):
+        return o("v", lambda q: q.tensor_tensor(out, a, b, op), rd, wr)
+
+    def ts(out, a, s1, op0, rd, wr, s2=None, op1=None):
+        if op1 is None:
+            return o("v", lambda q: q.tensor_scalar(out, a, s1, None, op0), rd, wr)
+        return o("v", lambda q: q.tensor_scalar(out, a, s1, s2, op0, op1), rd, wr)
+
+    def cp(out, a, rd, wr):
+        return o("v", lambda q: q.tensor_copy(out, a), rd, wr)
+
+    def ms(ap, c, wr):
+        return o("v", lambda q: q.memset(ap, c), [], wr)
+
+    def act(out, a, fn, rd, wr, bias=0.0, scale=1.0):
+        return o("s", lambda q: q.activation(out, a, fn, bias=bias, scale=scale), rd, wr)
+
+    def mm(out, l, r, st, sp, rd, wr):
+        return o("p", lambda q: q.matmul(out, l, r, st, sp), rd, wr)
+
+    def dma(eng, out, a, rd, wr, sem, n=1):
+        return o(eng, lambda q: q.dma_start(out, a), rd, wr, (sem, 16 * n))
+
+    def send(t, c, kind, dst, src, rd, land):
+        peer = T.cores[rank ^ STEPS[t]]
+        assert topo.may_write(core, peer)
+        rid, pid, _ = topo.addr(peer)
+        n = len(topo.engines(core, peer))
+        back = len(topo.engines(peer, core))
+        a, l = "a%s%d%d" % (kind, t, c), "l%s%d%d" % (kind, t, c)
+
+        def f(q):
+            q.remote_dma(dst, src, T.sem[a], T.sem[l], pid, rid, topo.mask(core, peer))
+        return [o("g", f, rd, [], (l, n)), o("g", None, [], [land], (a, back))]
+
+    def iota(out, pat, base, cm, wr):
+        return o("g", lambda q: q.iota(out, pat, base, cm), [], wr)
+
+    def asel(out, a, pat, cmp, base, cm, rd, wr):
+        return o("g", lambda q: q.affine_select(out, a, pat, cmp, 0.0, base, cm), rd, wr)
+
+    def W(t, c):
+        return T["W%d%d" % (t, c)]
+
+    def ln(c):
+        return slice(256 * c, 256 * c + 256)
+
+    XW = (T.X[:, 0:2304], T.X[:, 2304:4608])
+    XK = ["X0", "X1"]
+    OJ, OZ, OS = (0, 80), (16, 64), (32, 48)
+    CL, CW = (0, 768), (256, 512)
+
+    ops += [dma("s", T.z[:], T.zd[:], [], ["z0", "z1"], "ldz"), dma("s", T.w[:], T.wt[:], [], ["w"], "ldw"),
+            dma("y", T.ji[:], T.jn[:], [], ["ji"], "ldj"), dma("y", T.X[:, 256:4352], T.xt[:], [], ["Xl"], "ldx")]
+    ops += [ms(T.one[:], 1.0, ["one"]),
+            asel(T.bd[:], T.one[:, 0:128], [[-16, 8], [0, 16]], OP.is_ge, 0, 1, ["one"], ["bd"]),
+            asel(T.bd[:], T.bd[:], [[16, 8], [0, 16]], OP.is_ge, 15, -1, ["bd"], ["bd"]),
+            asel(T.idb[:], T.one[:, 0:128], [[-1, 128]], OP.is_equal, 0, 1, ["one"], ["idb"]),
+            iota(T.i3[:], [[16, 16]], 0, 0, ["i3"]), iota(T.i4[:, 0:2], [[0, 2]], 0, 1, ["i4"]),
+            iota(T.i1[:], [[0, 8], [-1, 8], [0, 2]], 8, 1, ["i1"]), iota(T.i2[:], [[0, 16], [2, 8]], 1, 0, ["i2"]),
+            iota(T.i5[:], [[-8, 16]], 128, 1, ["i5"]),
+            ms(T.cst[0:64, :], 6144.0, ["cst"]), ms(T.cst[64:128, :], 33.0 / 64, ["cst"]),
+            ms(T.mp[:], 1.0, ["mp"]), ms(T.pat[:, 0:256], 0.0, ["pat"]), ms(T.pat[:, 256:512], 1.0, ["pat"]),
+            ms(T.X[:, 0:256], 0.0, ["X0"]), ms(T.X[:, 4352:4608], 0.0, ["X1"]), ms(T.mp[:, 0::16], 0.0, ["mp"]),
+            ms(T.qw[:], 0.0, ["qw"]), ms(T.rx[:, 0:8], 0.0, ["rx"]), ms(T.m192[:], -192.0, ["m192"]), ms(T.o32[:], 32.0, ["o32"]),
+            ts(T.idm[:], T.idb[:], -2048.0, OP.mult, ["idb"], ["idm"]),
+            ts(T.bdw[:], T.bd[:], T.w[:], OP.mult, ["bd", "w"], ["bdw"]),
+            ts(T.bdw2[:], T.bd[:], T.w[:], OP.mult, ["bd", "w"], ["bdw2"], 2.0, OP.mult)]
+    late = [ts(T.idn[:], T.idb[:], -1.0, OP.mult, ["idb"], ["idn"]), ts(T.id16[:], T.idb[:], 16.0, OP.mult, ["idb"], ["id16"]),
+            cp(T.idf[:], T.idb[:], ["idb"], ["idf"]), cp(T.qw[:, 15:143:16], T.bdw[:, 0::16], ["bdw", "qw"], ["qw"]),
+            cp(T.rx[:, 8:16], T.bd[:, 0::16], ["bd"], ["rxa"]), cp(T.rx[:, 16:24], T.bd[:, 0::16], ["bd"], ["rxb"]),
+            ts(T.rx[:, 24:32], T.bd[:, 0::16], -1.0, OP.mult, ["bd"], ["rxc"]),
+            ts(T.i4[:, 0:1], T.i4[:, 0:1], 15, OP.bitwise_and, ["i4"], ["i4a"]),
+            ts(T.i4[:, 1:2], T.i4[:, 1:2], 1, OP.bitwise_and, ["i4"], ["i4b"]),
+            ts(T.i1[:], T.i1[:], 7, OP.bitwise_and, ["i1"], ["i1"]), ts(T.i5[:], T.i5[:], 3, OP.arith_shift_right, ["i5"], ["i5"]),
+            cp(T.TV[:, 384:512], T.i2[:], ["i2", "TV"], ["kc"]), cp(T.pc[:], T.i4[:, 0:2], ["i4a", "i4b"], ["pc"]),
+            ts(T.zm[:], T.i1[:], 0.0, OP.is_equal, ["i1"], ["zm"]),
+            ts(T.ro[:, 96:112], T.i5[:], 16.0, OP.is_equal, ["i5"], ["ro6"]),
+            ts(T.il[:], T.i3[:], T.pc[:, 0:1], OP.add, ["i3", "pc"], ["il"]),
+            ts(T.zo[:], T.i3[:, 0:8], 0.125, OP.mult, ["i3", "pc"], ["zo"], T.pc[:, 1:2], OP.add)]
+    for j, (rs, ca, cb, ma, mb) in enumerate(((256.0, 1.0, 0.0, 0.0, 60000.0), (BIG, 1.0, 0.0, 1.0, 256.0), (BIG, 1.0, 0.0, None, None),
+                                              (-BIG, 1.0, 2048.0, None, None), (-BIG, 1.0, 256.0, 1.0, 0.0), (256.0, 1.0, 0.0, 0.0, 0.0),
+                                              (None, 16.0, -1.0, None, None))):
+        sl = slice(16 * j, 16 * j + 16)
+        if rs is not None:
+            late.append(ts(T.ro[:, sl], T.ro[:, 96:112], rs, OP.mult, ["ro6"], ["ro%d" % j]))
+        late.append(ts(T.co[:, sl], T.il[:], ca, OP.mult, ["il"], ["co%d" % j], cb, OP.add))
+        if ma is not None:
+            late.append(ts(T.cm[:, sl], T.il[:], ma, OP.mult, ["il"], ["cm%d" % j], mb, OP.add))
+    late += [ts(T.c8[:, 0:16], T.il[:], 8.0, OP.mult, ["il"], ["c80"], 256.0, OP.add), ts(T.c8[:, 16:32], T.il[:], 8.0, OP.mult, ["il"], ["c81"])]
+
+    def tables(t, c):
+        w, d, k = W(t, c), T["D%d%d" % (t, c)], "%d%d" % (t, c)
+        out = send(t, c, "j", w[:, 4096:4352], w[:, 0:256], ["J" + k], "Jr" + k)
+        out += [dma("y", d[:, 0:16, :], w[:, 0:256], ["J" + k], ["Do" + k], "do" + k),
+                dma("y", d[:, 16:32, :], w[:, 4096:4352], ["Jr" + k], ["Dr" + k], "dr" + k)]
+        out += [dma("y", w[:, 256 * s:256 * s + 256], d[:, s:s + 16, :], ["Do" + k, "Dr" + k], ["Wt" + k], "dt" + k, 15) for s in range(1, 16)]
+        return out
+
+    def prep1(c):
+        zu = T["ZU%d" % c]
+        return [mm(T.SR[:, 256:512], T.bdw[:], T.z[:, ln(c)], True, True, ["bdw", "z%d" % c], ["SR", "raw"]),
+                mm(zu[:, 0:256], T.idb[:], T.z[:, ln(c)], True, True, ["idb", "z%d" % c], ["ZU%d" % c, "zp%d" % c])]
+
+    def prep2(c):
+        zu, k = T["ZU%d" % c], ["ZU%d" % c, "u%d" % c]
+        return [act(T.nb[:, ln(c)], T.SR[:, 256:512], AF.Identity, ["SR", "raw"], ["nb%d" % c], 191.5 + 1.0 / 2048, 1.0 / 1024),
+                mm(zu[:, 256:512], T.cst[:], T.one[:], True, False, ["cst", "one"], k),
+                mm(zu[:, 256:512], T.bdw2[:], T.z[:, ln(c)], False, False, ["bdw2", "z%d" % c], k),
+                mm(zu[:, 256:512], T.idm[:], T.nb[:, ln(c)], False, True, ["idm", "nb%d" % c], k)]
+
+    def prod(t, c):
+        return [tt(T.pi[:, ln(c)], W(t, c)[:, 0:256], T["ZU%d" % c][:, 256:512], OP.mult, ["J%d%d" % (t, c), "ZU%d" % c, "u%d" % c],
+                   ["pi%d" % (2 * c), "pi%d" % (2 * c + 1)])]
+
+    def hops(t, c):
+        st = [[], [], []]
+        for q in (2 * c, 2 * c + 1):
+            sl, k = slice(128 * q, 128 * q + 128), "pi%d" % q
+            if t > 0:
+                st[0].append(ts(T.pi[:, sl], T.pi[:, sl], T.LL[:, 128:129], OP.add, [k, "LL", "acol"], [k]))
+            st[1].append(ts(T.pi[:, sl], T.pi[:, sl], 5, OP.arith_shift_right, [k], [k], 4095, OP.bitwise_and))
+            st[2].append(cp(T.hu[:, sl], T.pi[:, sl], [k], ["hu%d" % q]))
+        return st[0] + st[1] + st[2]
+
+    def pick(eng, l0, n):
+        src = T.X[:, 256:4352].indirect(T.hu[:, l0:l0 + n])
+        out, rd = T.xg[:, 16 * l0:16 * (l0 + n)], XK + ["Xl", "hu%d" % (l0 // 128)]
+        wr = ["x%d" % j for j in range(l0 // 64, (l0 + n + 63) // 64)]
+        return [act(out, src, AF.Copy, rd, wr) if eng == "s" else cp(out, src, rd, wr)]
+
+    def mins(q):
+        c, h = q // 2, q % 2
+        return [tt(T.mg[:, 4096 * c + 256 * k + 128 * h:4096 * c + 256 * k + 128 * h + 128], T.xg[:, 2048 * q + k:2048 * (q + 1):16],
+                   T["ZU%d" % c][:, 128 * h:128 * h + 128], OP.min, ["x%d" % (2 * q), "x%d" % (2 * q + 1), "ZU%d" % c, "zp%d" % c], ["m%d_%d" % (q, k)])
+                for k in range(16)]
+
+    def pscan(q, n=1):
+        def piece(j):
+            w = 2048 // n
+            sl = slice(2048 * q + w * j, 2048 * q + w * j + w)
+            return o("v", lambda e: e.tensor_tensor_scan(T.pg[:, sl], T.mp[:, 0:w], T.xg[:, sl], 0.0, OP.mult, OP.max),
+                     ["mp", "x%d" % (2 * q), "x%d" % (2 * q + 1)], ["pg%d_%d" % (q, i) for i in range(8 * j // n, 8 * (j + 1) // n)])
+        return [piece(j) for j in range(n)]
+
+    def sums_x(c):
+        gs, k = T["GS%d" % c], ["GS%d" % c]
+        out = [mm(gs[:], T.one[0:1, 0:128], T.pat[0:1, :], True, False, ["one", "pat"], k)]
+        for kk in range(16):
+            for b in range(2):
+                out.append(mm(gs[:, 256 + 16 * b + kk:512:32], T.xg[:, 4096 * c + 16 * b + kk:4096 * (c + 1):32], T.rx[:, 8:16], False, False,
+                              ["x%d" % j for j in range(4 * c, 4 * c + 4)] + ["rxa"], k))
+        return out
+
+    def sums_m(c, kk):
+        gs, base = T["GS%d" % c], 4096 * c + 256 * kk
+        return [mm(gs[:, 16 * b + kk:512:32], T.mg[:, base + b:base + 256:2], T.rx[:, 16:32], False, kk == 15 and b == 1,
+                   ["m%d_%d" % (2 * c, kk), "m%d_%d" % (2 * c + 1, kk), "rxb", "rxc"], ["GS%d" % c]) for b in range(2)]
+
+    def mins_sums(c):
+        out = []
+        for kk, m in enumerate(mins(2 * c + 1)):
+            out += [m] + sums_m(c, kk)
+        return out
+
+    def search(c):
+        gs, bk, f = T["GS%d" % c], "GS%d" % c, 48 * c
+        out = [o("v", lambda e: e.tensor_tensor_scan(T.s0[:], T.mp[:, 0:256], gs[:, 256:512], 0.0, OP.mult, OP.add), ["mp", bk], ["S0"]),
+               o("v", lambda e: e.tensor_tensor_scan(T.TV[:, 0:256], T.mp[:, 0:256], gs[:, 0:256], 0.0, OP.mult, OP.add), ["mp", bk, "TV", "G2", "G3"], ["G0"])]
+        gk = [(T.TV, 0, "TV"), (gs, 0, bk), (T.TV, 0, "TV"), (T.TV, 128, "TV"), (T.fin, f + 16, "fin%d" % c)]
+        ss = [T.s0[:], T.s1[:], T.s2[:], T.s3[:], T.fin[:, f:f + 16]]
+        sb = [T.s0, T.s1, T.s2, T.s3]
+        for lv in range(4):
+            n = 128 >> lv
+            (bi, a, ki), (bo, a2, ko) = gk[lv], gk[lv + 1]
+            G, S, G2, S2 = "G%d" % lv, "S%d" % lv, "G%d" % (lv + 1), "S%d" % (lv + 1) if lv < 3 else "fs%d" % c
+            ga, gb, sa, sbb = bi[:, a:a + 2 * n:2], bi[:, a + 1:a + 2 * n:2], sb[lv][:, 0::2], sb[lv][:, 1::2]
+            tmp = T.TV[:, 256:256 + n]
+            out += [tt(T.p1[:, 0:n], gb, sa, OP.mult, [ki, G, S], ["p1"]), tt(tmp, ga, sbb, OP.mult, [ki, "TV", G, S], ["tmp"]),
+                    tt(T.cc[:, 0:n], T.p1[:, 0:n], tmp, OP.is_gt, ["p1", "TV", "tmp"], ["cc"]),
+                    tt(T.cgk[:, 0:n], T.cc[:, 0:n], gb, OP.mult, ["cc", ki, G], ["cg1"]),
+                    tt(tmp, T.cc[:, 0:n], sbb if lv else gs[:, 257:512:2], OP.mult, ["cc", S, "TV", bk], ["tmp"])]
+            if lv == 0:
+                out += [tt(bo[:, a2 + n:a2 + 2 * n], T.cc[:], T.TV[:, 384:512], OP.add, ["cc", "kc", "TV", ko], [G2 + "k"]),
+                        tt(bo[:, a2:a2 + n], ga, T.cgk[:, 0:n], OP.max, [ki, ko, G, "cg1"], [G2])]
+            else:
+                out += [tt(T.cgk[:, n:2 * n], T.cc[:, 0:n], bi[:, a + 2 * n + 1:a + 4 * n:2], OP.mult, ["cc", ki, G, G + "k"], ["cg2"]),
+                        tt(bo[:, a2:a2 + 2 * n], bi[:, a:a + 4 * n:2], T.cgk[:, 0:2 * n], OP.max, [G, G + "k", "TV", ki, "cg1", "cg2"],
+                           [G2] if lv < 3 else [ko])]
+            out.append(tt(ss[lv + 1], sa, tmp, OP.max if lv else OP.add, [S, "TV", "tmp"], [S2]))
+        return out
+
+    def send_gs(t, c):
+        return send(t, c, "g", T["RG%d%d" % (t, c)][:], T.fin[:, 48 * c:48 * c + 32], ["fin%d" % c, "fs%d" % c], "RG%d%d" % (t, c))
+
+    def place(c):
+        return [mm(T.LL[:, 0:16], T.idf[:], T.co[:, 96:112], True, False, ["idf", "co6"], ["LL", "ly"]),
+                tt(T.zz[:], T.fin[:, 48 * c + 32:48 * c + 48].indirect(T.zo[:]), T.zm[:], OP.mult, ["fin%d" % c, "zo", "zm"], ["zz"]),
+                mm(T.LL[:, 0:16], T.zz[:], T.ro[:, 96:112], False, True, ["zz", "ro6"], ["LL", "ly"])], \
+               [cp(T.oy[:, 16 * c:16 * c + 16], T.LL[:, 0:16], ["LL", "ly"], ["oy%d" % c])]
+
+    def profile(t, c):
+        k = "y%d" % c
+        return [act(T.yy[:, ln(c)], T.pg[:, 4096 * c:4096 * (c + 1)].indirect(T.oy[:, 16 * c:16 * c + 16]), AF.Copy,
+                    ["pg%d_%d" % (2 * c + i // 8, i % 8) for i in range(16)] + ["oy%d" % c], [k])] \
+            + send(t, c, "y", T["RY%d%d" % (t, c)][:], T.yy[:, ln(c)], [k], "RY%d%d" % (t, c)) \
+            + [mm(T.DZ[:, 256:512], T.idb[:], T.vv[:, ln(c)], True, False, ["idb", "v%d" % c], ["DZ"]),
+               mm(T.DZ[:, 256:512], T.idb[:], T.yy[:, ln(c)], False, True, [k], ["DZ"]),
+               mm(T.DZ[:, 0:256], T.idb[:], T.z[:, ln(c)], True, False, ["z%d" % c], ["DZ"]),
+               mm(T.DZ[:, 0:256], T.idn[:], T.yy[:, ln(c)], False, True, ["idn", k], ["DZ"])]
+
+    def winner(c):
+        return [act(T.nv[:, ln(c)], T.DZ[:, 256:512], AF.Identity, ["DZ"], ["nv%d" % c], 191.75, 0.5),
+                act(T.t1[:, ln(c)], T.DZ[:, 0:256], AF.Abs, ["DZ"], ["t1%d" % c]),
+                act(T.cz[:, CW[c]:CW[c] + 256], T.t1[:, ln(c)], AF.Relu, ["t1%d" % c], ["cw%d" % c], -1.0)]
+
+    def loser(t, c):
+        return [mm(T.SR[:, 0:256], T.idb[:], T.z[:, ln(c)], True, False, ["z%d" % c], ["SR"]),
+                mm(T.SR[:, 0:256], T.idb[:], T["RY%d%d" % (t, c)][:], False, True, ["RY%d%d" % (t, c)], ["SR"]),
+                act(T.t2[:, ln(c)], T.SR[:, 0:256], AF.Identity, ["SR"], ["t2%d" % c], 191.75, 0.5),
+                act(T.cz[:, CL[c]:CL[c] + 256], T.t2[:, ln(c)], AF.Relu, ["t2%d" % c], ["cl%d" % c], -193.0)]
+
+    def cols():
+        out = [mm(T.LL[:, 64:96], T.qw[:, 15 - a:143 - a], T.z[:, a::16], a == 0, a == 15, ["qw", "z0", "z1"], ["LL", "rl"]) for a in range(16)]
+        return out, [cp(T.ri[:], T.LL[:, 64:96], ["LL", "rl"], ["ri"]), ts(T.ri[:], T.ri[:], 7, OP.bitwise_and, ["ri"], ["ri"]),
+                     tt(T.cm[:, 32:64], T.ri[:], T.c8[:], OP.add, ["ri", "c80", "c81"], ["cm2", "cm3"]),
+                     cp(T.cu[:], T.cm[:, 32:64], ["cm2", "cm3"], ["cu"])]
+
+    def old(c):
+        return [act(T.vv[:, ln(c)], XW[c].indirect(T.cu[:, 16 * c:16 * c + 16]), AF.Copy, [XK[c], "Xl", "cu"], ["v%d" % c])]
+
+    def meet(t, c):
+        f, r, k = 48 * c, T["RG%d%d" % (t, c)], "RG%d%d" % (t, c)
+        j3 = range(3 * c, 3 * c + 3)
+        return [mm(T.LL[:, 16:64], T.idf[:], T.co[:, f:f + 48], True, False, ["idf"] + ["co%d" % j for j in j3], ["LL", "lo"]),
+                tt(T.wa[:, 0:16], T.fin[:, f + 16:f + 32], r[:, 0:16], OP.mult, ["fin%d" % c, k], ["wa0"]),
+                tt(T.wa[:, 16:32], T.fin[:, f:f + 16], r[:, 16:32], OP.mult, ["fs%d" % c, k], ["wa1"]),
+                tt(T.wa[:, 32:48], T.wa[:, 0:16], T.wa[:, 16:32], OP.is_ge if rank < (rank ^ STEPS[t]) else OP.is_gt, ["wa0", "wa1"], ["wa2"]),
+                tt(T.sig[:, 16 * c:16 * c + 16], T.wa[:, 32:48], T.fin[:, f + 32:f + 48], OP.mult, ["wa2", "fin%d" % c], ["sg%d" % c]),
+                tt(T.zz[:], T.sig[:, 16 * c:16 * c + 16].indirect(T.zo[:]), T.zm[:], OP.mult, ["sg%d" % c, "zo", "zm"], ["zz"]),
+                mm(T.LL[:, 16:64], T.zz[:], T.ro[:, f:f + 48], False, True, ["zz"] + ["ro%d" % j for j in j3], ["LL", "lo"])], \
+               [tt(T.of[:], T.LL[:, 16:64], T.cm[:, f:f + 48], OP.max if c else OP.min, ["LL", "lo"] + ["cm%d" % j for j in j3], ["of"]),
+                cp(T.ou[:, f:f + 48], T.of[:], ["of"], ["ou%d" % c])]
+
+    def scatter(c):
+        return [tt(XW[c].indirect(T.ou[:, OS[c]:OS[c] + 16]), T.nv[:, ln(c)], T.m192[:], OP.add, ["nv%d" % c, "m192", "ou%d" % c], [XK[c]])]
+
+    def demand(t, c):
+        out = [act(T.z[:, ln(c)], T.cz[:, 512 * c:512 * c + 512].indirect(T.ou[:, OZ[c]:OZ[c] + 16]), AF.Identity,
+                   ["cw%d" % c, "cl%d" % c, "ou%d" % c], ["z%d" % c], 1.0)]
+        return out + (prep1(c) if t < 2 else [dma("y", T.yz[:, ln(c)], T.z[:, ln(c)], ["z%d" % c], [], "sz%d" % c)])
+
+    def names(t, c):
+        k = "%d%d" % (t, c)
+        src, rd = W(t, c)[:].indirect(T.ou[:, OJ[c]:OJ[c] + 16]), ["J" + k, "Jr" + k, "Wt" + k, "ou%d" % c]
+        if t < 2:
+            return [act(W(t + 1, c)[:, 0:256], src, AF.Copy, rd, ["J%d%d" % (t + 1, c)])] + tables(t + 1, c)
+        return [act(T.jo[:, ln(c)], src, AF.Copy, rd, ["jo%d" % c]), dma("y", T.yj[:, ln(c)], T.jo[:, ln(c)], ["jo%d" % c], [], "sj%d" % c)]
+
+    def count():
+        return [o("v", lambda e: e.tensor_reduce(T.a1[:], T.sig[:], AX.X, OP.add), ["sg0", "sg1"], ["a1"]),
+                mm(T.LL[:, 128:129], T.o32[:], T.a1[:], True, True, ["o32", "a1"], ["LL", "acol"])]
+
+    YB = ("ZU0", "ZU1", "GS0", "GS1")
+
+    ops += prep1(0) + prep2(0)
+    ops += [cp(W(0, c)[:, 0:256], T.ji[:, ln(c)], ["ji"], ["J0%d" % c]) for c in range(2)]
+    ops += tables(0, 0) + prep1(1) + prep2(1) + late[:12] + prod(0, 0) + weave(hops(0, 0), late[12:24]) + tables(0, 1)
+    late = late[24:]
+
+    for t in range(3):
+        ops += pick("s", 0, 64) + pick("v", 64, 64)
+        if t > 0:
+            ops += loser(t - 1, 1) + demand(t - 1, 1) + pick("s", 128, 32) + prep2(1) + pick("s", 160, 96)
+        else:
+            ops += late + pick("s", 128, 128)
+        c1, c2 = cols()
+        ops += mins(0) + weave(prod(t, 1) + hops(t, 1), pscan(0, 4)) + c1
+        ops += pick("s", 256, 128) + pick("s", 384, 128)
+        ops += sums_x(0) + mins_sums(0) + sums_x(1) + weave(c2, mins(2)[:8]) + old(0) + old(1)
+        a1, a2 = place(0)
+        ops += mins(2)[8:12] + weave(search(0), mins(2)[12:] + pscan(1, 8)) + send_gs(t, 0) + a1
+        b = mins_sums(1)
+        ops += b[:6] + a2 + profile(t, 0)[:3] + b[6:] + profile(t, 0)[3:] + winner(0) + loser(t, 0)
+        a1, a2 = place(1)
+        m1, m2 = meet(t, 0)
+        p2 = pscan(2, 8)
+        ops += p2[:2] + weave(search(1), m1 + p2[2:4] + m2 + demand(t, 0) + (prep2(0) if t < 2 else []) + p2[4:] + names(t, 0))
+        ops += send_gs(t, 1) + a1
+        m1, m2 = meet(t, 1)
+        if t < 2:
+            h = hops(t + 1, 0)
+            ops += pscan(3) + a2 + profile(t, 1) + winner(1) + scatter(0)
+            ops += prod(t + 1, 0) + m1 + count() + m2 + names(t, 1) + h[:1] + scatter(1) + h[1:]
+        else:
+            ops += scatter(0) + [mm(T[YB[j]][:], T.idb[:], T.X[:, 256 + 512 * j:768 + 512 * j], True, False, ["X0", "Xl"], [YB[j]]) for j in range(4)]
+            ops += pscan(3) + a2 + profile(t, 1) + winner(1) + m1 + m2 + names(t, 1) + scatter(1)
+    for j in range(4):
+        if j == 3:
+            ops += loser(2, 1) + demand(2, 1)
+        sl = slice(512 * j, 512 * j + 512)
+        ops.append(mm(T[YB[j]][:], T.id16[:], T.X[:, 2304 + 512 * j:2816 + 512 * j], False, True, ["X1", "Xl", "id16"], [YB[j]]))
+        ops.append(cp(T.yo[:, sl], T[YB[j]][:], [YB[j]], ["yo%d" % j]) if j % 2 == 0 else act(T.yo[:, sl], T[YB[j]][:], AF.Copy, [YB[j]], ["yo%d" % j]))
+        if j % 2:
+            h = slice(512 * (j - 1), 512 * (j + 1))
+            ops.append(dma("y", T.yx[:, h], T.yo[:, h], ["yo%d" % (j - 1), "yo%d" % j], [], "sy%d" % (j // 2)))
+    emit(g, T, ops)

@@ -11,12 +11,12 @@ SCRATCH = {
     "jo": ("sbuf", [128, 512], F), "pi": ("sbuf", [128, 512], I), "hu": ("sbuf", [128, 512], U),
     "yy": ("sbuf", [128, 512], B), "vv": ("sbuf", [128, 512], B), "nv": ("sbuf", [128, 512], B),
     "t1": ("sbuf", [128, 512], B), "t2": ("sbuf", [128, 512], B), "nb": ("sbuf", [128, 512], B),
-    "cz": ("sbuf", [128, 1024], B), "yo": ("sbuf", [128, 2048], B),
+    "cz": ("sbuf", [128, 1024], B), "yo": ("sbuf", [128, 2560], B),
     "s0": ("sbuf", [128, 256], F), "s1": ("sbuf", [128, 128], F), "s2": ("sbuf", [128, 64], F), "s3": ("sbuf", [128, 32], F),
     "p1": ("sbuf", [128, 128], F), "cc": ("sbuf", [128, 128], F), "cgk": ("sbuf", [128, 128], F),
     "fin": ("sbuf", [128, 96], F), "wa": ("sbuf", [128, 48], F), "sig": ("sbuf", [128, 32], F), "a1": ("sbuf", [128, 1], F),
     "zz": ("sbuf", [128, 128], B), "oy": ("sbuf", [128, 32], U), "of": ("sbuf", [128, 48], F), "ou": ("sbuf", [128, 96], U),
-    "ri": ("sbuf", [128, 32], I), "cu": ("sbuf", [128, 32], U),
+    "yv": ("sbuf", [128, 512], B), "ri": ("sbuf", [128, 32], I), "cu": ("sbuf", [128, 32], U),
     "one": ("sbuf", [128, 256], B), "idb": ("sbuf", [128, 128], B), "idn": ("sbuf", [128, 128], B), "id16": ("sbuf", [128, 128], B),
     "idm": ("sbuf", [128, 128], B), "idf": ("sbuf", [128, 128], F), "o32": ("sbuf", [128, 128], F), "bd": ("sbuf", [128, 128], B),
     "bdw": ("sbuf", [128, 128], B), "bdw2": ("sbuf", [128, 128], B), "qw": ("sbuf", [128, 144], B), "cst": ("sbuf", [128, 128], B),
@@ -166,8 +166,8 @@ def rank_program(g, core, T, topo):
     OJ, OZ, OS = (0, 80), (16, 64), (32, 48)
     CL, CW = (0, 768), (256, 512)
 
-    ops += [dma("s", T.z[:], T.zd[:], [], ["z0", "z1"], "ldz"), dma("s", T.w[:], T.wt[:], [], ["w"], "ldw"),
-            dma("y", T.ji[:], T.jn[:], [], ["ji"], "ldj"), dma("y", T.X[:, 256:4352], T.xt[:], [], ["Xl"], "ldx")]
+    ops += [dma("s", T.w[:], T.wt[:], [], ["w"], "ldw"), dma("y", T.z[:], T.zd[:], [], ["z0", "z1"], "ldz"),
+            dma("s", T.ji[:], T.jn[:], [], ["ji"], "ldj"), dma("y", T.X[:, 256:4352], T.xt[:], [], ["Xl"], "ldx")]
     ops += [ms(T.one[:], 1.0, ["one"]),
             asel(T.bd[:], T.one[:, 0:128], [[-16, 8], [0, 16]], OP.is_ge, 0, 1, ["one"], ["bd"]),
             asel(T.bd[:], T.bd[:], [[16, 8], [0, 16]], OP.is_ge, 15, -1, ["bd"], ["bd"]),
@@ -195,15 +195,15 @@ def rank_program(g, core, T, topo):
             ts(T.il[:], T.i3[:], T.pc[:, 0:1], OP.add, ["i3", "pc"], ["il"]),
             ts(T.zo[:], T.i3[:, 0:8], 0.125, OP.mult, ["i3", "pc"], ["zo"], T.pc[:, 1:2], OP.add)]
     for j, (rs, ca, cb, ma, mb) in enumerate(((256.0, 1.0, 0.0, 0.0, 60000.0), (BIG, 1.0, 0.0, 1.0, 256.0), (BIG, 1.0, 0.0, None, None),
-                                              (-BIG, 1.0, 2048.0, None, None), (-BIG, 1.0, 256.0, 1.0, 0.0), (256.0, 1.0, 0.0, 0.0, 0.0),
-                                              (None, 16.0, -1.0, None, None))):
+                                              (-BIG, 1.0, 2048.0, None, None), (-BIG, 1.0, 256.0, 1.0, 0.0), (256.0, 1.0, 0.0, 0.0, 0.0))):
         sl = slice(16 * j, 16 * j + 16)
         if rs is not None:
             late.append(ts(T.ro[:, sl], T.ro[:, 96:112], rs, OP.mult, ["ro6"], ["ro%d" % j]))
         late.append(ts(T.co[:, sl], T.il[:], ca, OP.mult, ["il"], ["co%d" % j], cb, OP.add))
         if ma is not None:
             late.append(ts(T.cm[:, sl], T.il[:], ma, OP.mult, ["il"], ["cm%d" % j], mb, OP.add))
-    late += [ts(T.c8[:, 0:16], T.il[:], 8.0, OP.mult, ["il"], ["c80"], 256.0, OP.add), ts(T.c8[:, 16:32], T.il[:], 8.0, OP.mult, ["il"], ["c81"])]
+    late += [ts(T.a1[:], T.pc[:, 1:2], 2040.0, OP.mult, ["pc"], ["a1"], -1.0, OP.add),
+             ts(T.co[:, 96:112], T.il[:], 8.0, OP.mult, ["il", "a1"], ["co6"], T.a1[:], OP.add), ms(T.yo[:, 0:256], 0.0, ["Yd"]), ms(T.yo[:, 2304:2560], 0.0, ["Yd"]), ts(T.c8[:, 0:16], T.il[:], 8.0, OP.mult, ["il"], ["c80"], 256.0, OP.add), ts(T.c8[:, 16:32], T.il[:], 8.0, OP.mult, ["il"], ["c81"])]
 
     def tables(t, c):
         w, d, k = W(t, c), T["D%d%d" % (t, c)], "%d%d" % (t, c)
@@ -226,17 +226,18 @@ def rank_program(g, core, T, topo):
                 mm(zu[:, 256:512], T.idm[:], T.nb[:, ln(c)], False, True, ["idm", "nb%d" % c], k)]
 
     def prod(t, c):
-        return [tt(T.pi[:, ln(c)], W(t, c)[:, 0:256], T["ZU%d" % c][:, 256:512], OP.mult, ["J%d%d" % (t, c), "ZU%d" % c, "u%d" % c],
-                   ["pi%d" % (2 * c), "pi%d" % (2 * c + 1)])]
+        return [tt(T.pi[:, 256 * c + 128 * b:256 * c + 128 * b + 128], W(t, c)[:, b:256:2], T["ZU%d" % c][:, 256 + b:512:2], OP.mult,
+                   ["J%d%d" % (t, c), "ZU%d" % c, "u%d" % c], ["pi%d" % (2 * c + b)]) for b in range(2)]
 
-    def hops(t, c):
+    def hops(t, c, w):
         st = [[], [], []]
-        for q in (2 * c, 2 * c + 1):
-            sl, k = slice(128 * q, 128 * q + 128), "pi%d" % q
+        for a in range(256 * c, 256 * c + 256, w):
+            sl, qs = slice(a, a + w), range(a // 128, (a + w) // 128)
+            k = ["pi%d" % q for q in qs]
             if t > 0:
-                st[0].append(ts(T.pi[:, sl], T.pi[:, sl], T.LL[:, 128:129], OP.add, [k, "LL", "acol"], [k]))
-            st[1].append(ts(T.pi[:, sl], T.pi[:, sl], 5, OP.arith_shift_right, [k], [k], 4095, OP.bitwise_and))
-            st[2].append(cp(T.hu[:, sl], T.pi[:, sl], [k], ["hu%d" % q]))
+                st[0].append(ts(T.pi[:, sl], T.pi[:, sl], T.LL[:, 128:129], OP.add, k + ["LL", "acol"], k))
+            st[1].append(ts(T.pi[:, sl], T.pi[:, sl], 5, OP.arith_shift_right, k, k, 4095, OP.bitwise_and))
+            st[2].append(cp(T.hu[:, sl], T.pi[:, sl], k, ["hu%d" % q for q in qs]))
         return st[0] + st[1] + st[2]
 
     def pick(eng, l0, n):
@@ -248,7 +249,7 @@ def rank_program(g, core, T, topo):
     def mins(q):
         c, h = q // 2, q % 2
         return [tt(T.mg[:, 4096 * c + 256 * k + 128 * h:4096 * c + 256 * k + 128 * h + 128], T.xg[:, 2048 * q + k:2048 * (q + 1):16],
-                   T["ZU%d" % c][:, 128 * h:128 * h + 128], OP.min, ["x%d" % (2 * q), "x%d" % (2 * q + 1), "ZU%d" % c, "zp%d" % c], ["m%d_%d" % (q, k)])
+                   T["ZU%d" % c][:, h:256:2], OP.min, ["x%d" % (2 * q), "x%d" % (2 * q + 1), "ZU%d" % c, "zp%d" % c], ["m%d_%d" % (q, k)])
                 for k in range(16)]
 
     def pscan(q, n=1):
@@ -259,24 +260,20 @@ def rank_program(g, core, T, topo):
                      ["mp", "x%d" % (2 * q), "x%d" % (2 * q + 1)], ["pg%d_%d" % (q, i) for i in range(8 * j // n, 8 * (j + 1) // n)])
         return [piece(j) for j in range(n)]
 
-    def sums_x(c):
+    def sums_x(q):
+        c, b = q // 2, q % 2
         gs, k = T["GS%d" % c], ["GS%d" % c]
-        out = [mm(gs[:], T.one[0:1, 0:128], T.pat[0:1, :], True, False, ["one", "pat"], k)]
-        for kk in range(16):
-            for b in range(2):
-                out.append(mm(gs[:, 256 + 16 * b + kk:512:32], T.xg[:, 4096 * c + 16 * b + kk:4096 * (c + 1):32], T.rx[:, 8:16], False, False,
-                              ["x%d" % j for j in range(4 * c, 4 * c + 4)] + ["rxa"], k))
-        return out
+        out = [] if b else [mm(gs[:], T.one[0:1, 0:128], T.pat[0:1, :], True, False, ["one", "pat"], k)]
+        return out + [mm(gs[:, 256 + 16 * b + kk:512:32], T.xg[:, 2048 * q + kk:2048 * (q + 1):16], T.rx[:, 8:16], False, False,
+                         ["x%d" % (2 * q), "x%d" % (2 * q + 1), "rxa"], k) for kk in range(16)]
 
-    def sums_m(c, kk):
-        gs, base = T["GS%d" % c], 4096 * c + 256 * kk
-        return [mm(gs[:, 16 * b + kk:512:32], T.mg[:, base + b:base + 256:2], T.rx[:, 16:32], False, kk == 15 and b == 1,
-                   ["m%d_%d" % (2 * c, kk), "m%d_%d" % (2 * c + 1, kk), "rxb", "rxc"], ["GS%d" % c]) for b in range(2)]
-
-    def mins_sums(c):
+    def mins_sums(q):
+        c, b = q // 2, q % 2
         out = []
-        for kk, m in enumerate(mins(2 * c + 1)):
-            out += [m] + sums_m(c, kk)
+        for kk, m in enumerate(mins(q)):
+            base = 4096 * c + 256 * kk + 128 * b
+            out += [m, mm(T["GS%d" % c][:, 16 * b + kk:512:32], T.mg[:, base:base + 128], T.rx[:, 16:32], False, kk == 15 and b == 1,
+                          ["m%d_%d" % (q, kk), "rxb", "rxc"], ["GS%d" % c])]
         return out
 
     def search(c):
@@ -358,7 +355,10 @@ def rank_program(g, core, T, topo):
                [tt(T.of[:], T.LL[:, 16:64], T.cm[:, f:f + 48], OP.max if c else OP.min, ["LL", "lo"] + ["cm%d" % j for j in j3], ["of"]),
                 cp(T.ou[:, f:f + 48], T.of[:], ["of"], ["ou%d" % c])]
 
-    def scatter(c):
+    def scatter(t, c):
+        if t == 2:
+            return [tt(T.yo[:, 256 * c:256 * c + 2304].indirect(T.ou[:, OS[c]:OS[c] + 16]), T.t2[:, 256:512] if c else T.nv[:, 0:256], T.yv[:, ln(c)], OP.add,
+                       ["n16" if c else "nv0", "t21", "e%d" % c, "ou%d" % c, "Y0", "Y1", "Y2", "Y3", "Yd"], ["Y"])]
         return [tt(XW[c].indirect(T.ou[:, OS[c]:OS[c] + 16]), T.nv[:, ln(c)], T.m192[:], OP.add, ["nv%d" % c, "m192", "ou%d" % c], [XK[c]])]
 
     def demand(t, c):
@@ -377,12 +377,24 @@ def rank_program(g, core, T, topo):
         return [o("v", lambda e: e.tensor_reduce(T.a1[:], T.sig[:], AX.X, OP.add), ["sg0", "sg1"], ["a1"]),
                 mm(T.LL[:, 128:129], T.o32[:], T.a1[:], True, True, ["o32", "a1"], ["LL", "acol"])]
 
-    YB = ("ZU0", "ZU1", "GS0", "GS1")
+    def packed(j, bk):
+        return [mm(T[bk][:], T.idb[:], T.X[:, 256 + 512 * j:768 + 512 * j], True, False, ["X0", "Xl"], [bk]),
+                mm(T[bk][:], T.id16[:], T.X[:, 2304 + 512 * j:2816 + 512 * j], False, True, ["X1", "Xl", "id16"], [bk]),
+                act(T.yo[:, 256 + 512 * j:768 + 512 * j], T[bk][:], AF.Copy, [bk], ["Y%d" % j])]
+
+    def rest0():
+        return [act(T.yv[:, 0:256], T.X[:, 2048:4352].indirect(T.cu[:, 0:16]), AF.Identity, XK + ["Xl", "cu"], ["e0"], -192.0, 16.0)]
+
+    def rest1():
+        return [act(T.nb[:, 0:256], T.yo[:, 256:2560].indirect(T.cu[:, 16:32]), AF.Copy, ["Y", "cu"], ["nb0"]),
+                mm(T.SR[:, 256:512], T.id16[:], T.vv[:, 256:512], True, False, ["v1"], ["SR"]),
+                mm(T.SR[:, 256:512], T.idn[:], T.nb[:, 0:256], False, True, ["nb0"], ["SR"]),
+                act(T.yv[:, 256:512], T.SR[:, 256:512], AF.Identity, ["SR"], ["e1"], 0.0, -1.0)]
 
     ops += prep1(0) + prep2(0)
     ops += [cp(W(0, c)[:, 0:256], T.ji[:, ln(c)], ["ji"], ["J0%d" % c]) for c in range(2)]
-    ops += tables(0, 0) + prep1(1) + prep2(1) + late[:12] + prod(0, 0) + weave(hops(0, 0), late[12:24]) + tables(0, 1)
-    late = late[24:]
+    ops += tables(0, 0) + prep1(1) + prep2(1) + late[:12] + prod(0, 0) + weave(hops(0, 0, 128), late[12:20]) + tables(0, 1) + late[20:34]
+    late = late[34:]
 
     for t in range(3):
         ops += pick("s", 0, 64) + pick("v", 64, 64)
@@ -391,33 +403,30 @@ def rank_program(g, core, T, topo):
         else:
             ops += late + pick("s", 128, 128)
         c1, c2 = cols()
-        ops += mins(0) + weave(prod(t, 1) + hops(t, 1), pscan(0, 4)) + c1
+        ops += sums_x(0) + mins_sums(0) + weave(prod(t, 1) + hops(t, 1, 256), pscan(0, 4)) + c1
         ops += pick("s", 256, 128) + pick("s", 384, 128)
-        ops += sums_x(0) + mins_sums(0) + sums_x(1) + weave(c2, mins(2)[:8]) + old(0) + old(1)
+        ops += sums_x(1) + mins_sums(1) + weave(c2, pscan(1, 4)) + old(0) + old(1) + sums_x(2)
         a1, a2 = place(0)
-        ops += mins(2)[8:12] + weave(search(0), mins(2)[12:] + pscan(1, 8)) + send_gs(t, 0) + a1
-        b = mins_sums(1)
-        ops += b[:6] + a2 + profile(t, 0)[:3] + b[6:] + profile(t, 0)[3:] + winner(0) + loser(t, 0)
+        if t == 2:
+            ops += packed(0, "ZU0") + packed(1, "DZ") + packed(2, "SR") + rest0()
+        b = weave(search(0), mins_sums(2))
+        ops += b[:44] + sums_x(3) + b[44:] + send_gs(t, 0) + a1
+        b = mins_sums(3)
+        ops += b[:4] + a2 + profile(t, 0)[:3] + b[4:] + profile(t, 0)[3:] + winner(0) + (packed(3, "ZU0") if t == 2 else [])
         a1, a2 = place(1)
         m1, m2 = meet(t, 0)
         p2 = pscan(2, 8)
-        ops += p2[:2] + weave(search(1), m1 + p2[2:4] + m2 + demand(t, 0) + (prep2(0) if t < 2 else []) + p2[4:] + names(t, 0))
+        ops += p2[:2] + weave(search(1), m1 + p2[2:4] + m2 + loser(t, 0) + demand(t, 0) + (prep2(0) if t < 2 else []) + p2[4:] + names(t, 0))
         ops += send_gs(t, 1) + a1
         m1, m2 = meet(t, 1)
         if t < 2:
-            h = hops(t + 1, 0)
-            ops += pscan(3) + a2 + profile(t, 1) + winner(1) + scatter(0)
-            ops += prod(t + 1, 0) + m1 + count() + m2 + names(t, 1) + h[:1] + scatter(1) + h[1:]
+            h = hops(t + 1, 0, 128)
+            ops += pscan(3) + a2 + profile(t, 1) + winner(1) + scatter(t, 0)
+            ops += m1 + count() + prod(t + 1, 0) + m2 + names(t, 1) + h[:1] + scatter(t, 1) + [h[2], h[1], h[4], h[3], h[5]]
         else:
-            ops += scatter(0) + [mm(T[YB[j]][:], T.idb[:], T.X[:, 256 + 512 * j:768 + 512 * j], True, False, ["X0", "Xl"], [YB[j]]) for j in range(4)]
-            ops += pscan(3) + a2 + profile(t, 1) + winner(1) + m1 + m2 + names(t, 1) + scatter(1)
-    for j in range(4):
-        if j == 3:
-            ops += loser(2, 1) + demand(2, 1)
-        sl = slice(512 * j, 512 * j + 512)
-        ops.append(mm(T[YB[j]][:], T.id16[:], T.X[:, 2304 + 512 * j:2816 + 512 * j], False, True, ["X1", "Xl", "id16"], [YB[j]]))
-        ops.append(cp(T.yo[:, sl], T[YB[j]][:], [YB[j]], ["yo%d" % j]) if j % 2 == 0 else act(T.yo[:, sl], T[YB[j]][:], AF.Copy, [YB[j]], ["yo%d" % j]))
-        if j % 2:
-            h = slice(512 * (j - 1), 512 * (j + 1))
-            ops.append(dma("y", T.yx[:, h], T.yo[:, h], ["yo%d" % (j - 1), "yo%d" % j], [], "sy%d" % (j // 2)))
+            ops += pscan(3) + a2 + scatter(t, 0) + profile(t, 1) + rest1()[:3] + winner(1)[:1]
+            ops += [act(T.t2[:, 256:512], T.nv[:, 256:512], AF.Identity, ["nv1"], ["n16", "t21"], -3072.0, 16.0)] + rest1()[3:]
+            ops += m1 + winner(1)[1:] + m2 + names(t, 1) + scatter(t, 1)
+            ops += [dma("y", T.yx[:], T.yo[:, 256:2304], ["Y"], [], "sy0")]
+            ops += loser(t, 1) + demand(t, 1)
     emit(g, T, ops)

@@ -16,6 +16,7 @@ SCRATCH = {
     "p1": ("sbuf", [128, 128], F), "cc": ("sbuf", [128, 128], F), "cgk": ("sbuf", [128, 128], F),
     "fin": ("sbuf", [128, 96], F), "wa": ("sbuf", [128, 48], F), "sig": ("sbuf", [128, 32], F), "a1": ("sbuf", [128, 1], F),
     "zz": ("sbuf", [128, 128], B), "oy": ("sbuf", [128, 32], U), "of": ("sbuf", [128, 48], F), "ou": ("sbuf", [128, 96], U),
+    "qa": ("sbuf", [128, 144], B), "qb": ("sbuf", [128, 144], B), "r8": ("sbuf", [128, 128], B), "ro8": ("sbuf", [128, 384], B),
     "yv": ("sbuf", [128, 512], B), "ri": ("sbuf", [128, 32], I), "cu": ("sbuf", [128, 32], U),
     "one": ("sbuf", [128, 256], B), "idb": ("sbuf", [128, 128], B), "idn": ("sbuf", [128, 128], B), "id16": ("sbuf", [128, 128], B),
     "idm": ("sbuf", [128, 128], B), "idf": ("sbuf", [128, 128], F), "o32": ("sbuf", [128, 128], F), "bd": ("sbuf", [128, 128], B),
@@ -50,6 +51,15 @@ def weave(a, b):
         out.extend(b[done:upto])
         done = upto
     return out + b[done:]
+
+
+def stages(chain, fill):
+    cuts = [2] + [2 + 8 * lv + d for lv in range(4) for d in (2, 3, 6, 8)]
+    out, a = [], 0
+    for j, b in enumerate(cuts):
+        out += chain[a:b] + (fill[j] if j < len(fill) else [])
+        a = b
+    return out
 
 
 def emit(g, T, ops):
@@ -197,7 +207,7 @@ def rank_program(g, core, T, topo):
     for j, (rs, ca, cb, ma, mb) in enumerate(((256.0, 1.0, 0.0, 0.0, 60000.0), (BIG, 1.0, 0.0, 1.0, 256.0), (BIG, 1.0, 0.0, None, None),
                                               (-BIG, 1.0, 2048.0, None, None), (-BIG, 1.0, 256.0, 1.0, 0.0), (256.0, 1.0, 0.0, 0.0, 0.0))):
         sl = slice(16 * j, 16 * j + 16)
-        if rs is not None:
+        if j > 2:
             late.append(ts(T.ro[:, sl], T.ro[:, 96:112], rs, OP.mult, ["ro6"], ["ro%d" % j]))
         late.append(ts(T.co[:, sl], T.il[:], ca, OP.mult, ["il"], ["co%d" % j], cb, OP.add))
         if ma is not None:
@@ -306,10 +316,15 @@ def rank_program(g, core, T, topo):
     def send_gs(t, c):
         return send(t, c, "g", T["RG%d%d" % (t, c)][:], T.fin[:, 48 * c:48 * c + 32], ["fin%d" % c, "fs%d" % c], "RG%d%d" % (t, c))
 
+    def turn(qb, qk, src, a, sk, out, r, rk, n, ok):
+        return [act(qb[:, 14 + b:142:16], src[:, a + b:a + 16:2], AF.Copy, [sk, qk], [qk + str(b)]) for b in range(2)] \
+            + [mm(out, qb[:, 14 - 2 * j:142 - 2 * j], r[:, n * j:n * j + n], False, j == 7, [qk + "0", qk + "1", rk], ["LL", ok]) for j in range(8)]
+
     def place(c):
-        return [mm(T.LL[:, 0:16], T.idf[:], T.co[:, 96:112], True, False, ["idf", "co6"], ["LL", "ly"]),
-                tt(T.zz[:], T.fin[:, 48 * c + 32:48 * c + 48].indirect(T.zo[:]), T.zm[:], OP.mult, ["fin%d" % c, "zo", "zm"], ["zz"]),
-                mm(T.LL[:, 0:16], T.zz[:], T.ro[:, 96:112], False, True, ["zz", "ro6"], ["LL", "ly"])], \
+        return [mm(T.LL[:, 0:16], T.idf[:], T.co[:, 96:112], True, False, ["idf", "co6"], ["LL", "ly"])] \
+            + ([tt(T.zz[:], T.fin[:, 80:96].indirect(T.zo[:]), T.zm[:], OP.mult, ["fin1", "zo", "zm"], ["zz"]),
+                mm(T.LL[:, 0:16], T.zz[:], T.ro[:, 96:112], False, True, ["zz", "ro6"], ["LL", "ly"])] if c else
+               turn(T.qa, "qa", T.fin, 32, "fin0", T.LL[:, 0:16], T.r8, "r8", 16, "ly")), \
                [cp(T.oy[:, 16 * c:16 * c + 16], T.LL[:, 0:16], ["LL", "ly"], ["oy%d" % c])]
 
     def profile(t, c):
@@ -349,9 +364,10 @@ def rank_program(g, core, T, topo):
                 tt(T.wa[:, 0:16], T.fin[:, f + 16:f + 32], r[:, 0:16], OP.mult, ["fin%d" % c, k], ["wa0"]),
                 tt(T.wa[:, 16:32], T.fin[:, f:f + 16], r[:, 16:32], OP.mult, ["fs%d" % c, k], ["wa1"]),
                 tt(T.wa[:, 32:48], T.wa[:, 0:16], T.wa[:, 16:32], OP.is_ge if rank < (rank ^ STEPS[t]) else OP.is_gt, ["wa0", "wa1"], ["wa2"]),
-                tt(T.sig[:, 16 * c:16 * c + 16], T.wa[:, 32:48], T.fin[:, f + 32:f + 48], OP.mult, ["wa2", "fin%d" % c], ["sg%d" % c]),
-                tt(T.zz[:], T.sig[:, 16 * c:16 * c + 16].indirect(T.zo[:]), T.zm[:], OP.mult, ["sg%d" % c, "zo", "zm"], ["zz"]),
-                mm(T.LL[:, 16:64], T.zz[:], T.ro[:, f:f + 48], False, True, ["zz"] + ["ro%d" % j for j in j3], ["LL", "lo"])], \
+                tt(T.sig[:, 16 * c:16 * c + 16], T.wa[:, 32:48], T.fin[:, f + 32:f + 48], OP.mult, ["wa2", "fin%d" % c], ["sg%d" % c])] \
+            + ([tt(T.zz[:], T.sig[:, 16 * c:16 * c + 16].indirect(T.zo[:]), T.zm[:], OP.mult, ["sg%d" % c, "zo", "zm"], ["zz"]),
+                mm(T.LL[:, 16:64], T.zz[:], T.ro[:, f:f + 48], False, True, ["zz"] + ["ro%d" % j for j in j3], ["LL", "lo"])] if c else
+               turn(T.qb, "qb", T.sig, 0, "sg0", T.LL[:, 16:64], T.ro8, "ro8", 48, "lo")), \
                [tt(T.of[:], T.LL[:, 16:64], T.cm[:, f:f + 48], OP.max if c else OP.min, ["LL", "lo"] + ["cm%d" % j for j in j3], ["of"]),
                 cp(T.ou[:, f:f + 48], T.of[:], ["of"], ["ou%d" % c])]
 
@@ -386,7 +402,7 @@ def rank_program(g, core, T, topo):
         return [act(T.yv[:, 0:256], T.X[:, 2048:4352].indirect(T.cu[:, 0:16]), AF.Identity, XK + ["Xl", "cu"], ["e0"], -192.0, 16.0)]
 
     def rest1():
-        return [act(T.nb[:, 0:256], T.yo[:, 256:2560].indirect(T.cu[:, 16:32]), AF.Copy, ["Y", "cu"], ["nb0"]),
+        return [act(T.nb[:, 0:256], T.yo[:, 256:2560].indirect(T.cu[:, 16:32]), AF.Copy, ["Y", "Yb", "cu"], ["nb0"]),
                 mm(T.SR[:, 256:512], T.id16[:], T.vv[:, 256:512], True, False, ["v1"], ["SR"]),
                 mm(T.SR[:, 256:512], T.idn[:], T.nb[:, 0:256], False, True, ["nb0"], ["SR"]),
                 act(T.yv[:, 256:512], T.SR[:, 256:512], AF.Identity, ["SR"], ["e1"], 0.0, -1.0)]
@@ -394,12 +410,15 @@ def rank_program(g, core, T, topo):
     ops += prep1(0) + prep2(0)
     ops += [cp(W(0, c)[:, 0:256], T.ji[:, ln(c)], ["ji"], ["J0%d" % c]) for c in range(2)]
     ops += tables(0, 0) + prep1(1) + prep2(1) + late[:12] + prod(0, 0) + weave(hops(0, 0, 128), late[12:20]) + tables(0, 1) + late[20:34]
-    late = late[34:]
+    late = late[34:] + [ms(T.qa[:], 0.0, ["qa"]), ms(T.qb[:], 0.0, ["qb"])]
+    ops += [asel(T.r8[:], T.one[:, 0:128], [[-1, 8], [-8, 16]], OP.is_equal, 0, 1, ["one"], ["r8"]),
+            o("g", lambda q: q.iota(T.ro8[:], [[0, 8], [8192, 3], [0, 16]], 256, 0, allow_small_or_imprecise_dtypes=True), [], ["ro8"]),
+            asel(T.ro8[:], T.ro8[:], [[-1, 8], [0, 3], [-8, 16]], OP.is_equal, 0, 1, ["ro8"], ["ro8"])]
 
     for t in range(3):
         ops += pick("s", 0, 64) + pick("v", 64, 64)
         if t > 0:
-            ops += loser(t - 1, 1) + demand(t - 1, 1) + pick("s", 128, 32) + prep2(1) + pick("s", 160, 96)
+            ops += prep2(1) + pick("s", 128, 128)
         else:
             ops += late + pick("s", 128, 128)
         c1, c2 = cols()
@@ -409,24 +428,33 @@ def rank_program(g, core, T, topo):
         a1, a2 = place(0)
         if t == 2:
             ops += packed(0, "ZU0") + packed(1, "DZ") + packed(2, "SR") + rest0()
-        b = weave(search(0), mins_sums(2))
-        ops += b[:44] + sums_x(3) + b[44:] + send_gs(t, 0) + a1
+        b = mins_sums(2)
+        ops += stages(search(0), [b[2 * j:2 * j + 2] + (sums_x(3) if j == 10 else []) for j in range(16)]) + send_gs(t, 0) + a1
         b = mins_sums(3)
-        ops += b[:4] + a2 + profile(t, 0)[:3] + b[4:] + profile(t, 0)[3:] + winner(0) + (packed(3, "ZU0") if t == 2 else [])
+        ops += b[:16] + a2 + profile(t, 0)[:3] + b[16:] + profile(t, 0)[3:] + winner(0) + (packed(3, "ZU0") if t == 2 else [])
         a1, a2 = place(1)
         m1, m2 = meet(t, 0)
-        p2 = pscan(2, 8)
-        ops += p2[:2] + weave(search(1), m1 + p2[2:4] + m2 + loser(t, 0) + demand(t, 0) + (prep2(0) if t < 2 else []) + p2[4:] + names(t, 0))
+        p2 = [[x] for x in pscan(2, 8) + pscan(3, 8)]
+        after = loser(t, 0) + demand(t, 0) + (prep2(0) if t < 2 else []) + names(t, 0)[:1 if t < 2 else 2]
+        ops += p2[0] + stages(search(1), [p2[1], m1[:3], m1[3:4], m1[4:]] + p2[2:8] + [m2[:1], m2[1:] + after] + p2[8:12])
         ops += send_gs(t, 1) + a1
+        p3 = pscan(3, 2)[1:]
         m1, m2 = meet(t, 1)
         if t < 2:
             h = hops(t + 1, 0, 128)
-            ops += pscan(3) + a2 + profile(t, 1) + winner(1) + scatter(t, 0)
-            ops += m1 + count() + prod(t + 1, 0) + m2 + names(t, 1) + h[:1] + scatter(t, 1) + [h[2], h[1], h[4], h[3], h[5]]
+            pr = prod(t + 1, 0)
+            ops += p3 + a2 + profile(t, 1) + tables(t + 1, 0) + winner(1) + scatter(t, 0)
+            ops += m1[:3] + pr[:1] + m1[3:4] + pr[1:] + m1[4:] + count() + m2[:1] + h[:1] + m2[1:] + names(t, 1) + loser(t, 1) + demand(t, 1)
+            ops += [h[2]] + scatter(t, 1) + [h[4], h[1], h[3], h[5]]
         else:
-            ops += pscan(3) + a2 + scatter(t, 0) + profile(t, 1) + rest1()[:3] + winner(1)[:1]
+            ops += p3 + a2 + scatter(t, 0) + profile(t, 1) + rest1()[:3] + winner(1)[:1]
             ops += [act(T.t2[:, 256:512], T.nv[:, 256:512], AF.Identity, ["nv1"], ["n16", "t21"], -3072.0, 16.0)] + rest1()[3:]
-            ops += m1 + winner(1)[1:] + m2 + names(t, 1) + scatter(t, 1)
-            ops += [dma("y", T.yx[:], T.yo[:, 256:2304], ["Y"], [], "sy0")]
+            ops += m1 + winner(1)[1:] + m2 + [ts(T.oy[:, 0:8], T.of[:, 8:16], -1024.0, OP.add, ["of"], ["oy0"])]
+            for h in range(2):
+                off = T.oy[:, 0:8] if h else T.ou[:, 48:56]
+                ops += [tt(T.yo[:, 256 + 1024 * h:2560].indirect(off), T.t2[:, 256 + 128 * h:384 + 128 * h], T.yv[:, 256 + 128 * h:384 + 128 * h], OP.add,
+                           ["n16", "t21", "e1", "ou1", "oy0", "Y"], ["Yb"] + ["Yh%d" % j for j in range(h, 2)]),
+                        dma("y" if h else "s", T.yx[:, 1024 * h:1024 * h + 1024], T.yo[:, 256 + 1024 * h:1280 + 1024 * h], ["Yh%d" % h], [], "sy%d" % h)]
+            ops += names(t, 1)
             ops += loser(t, 1) + demand(t, 1)
     emit(g, T, ops)

@@ -1,64 +1,144 @@
 from concourse.mybir import AluOpType as OP, AxisListType as AX, ActivationFunctionType as AF
 
 STEPS = (5, 2, 7)
-BIG = 8192.0
 F, B, I, U = "float32", "bfloat16", "int32", "uint16"
+SP = 2560
+BIG = 4096.0
+SHARED = (3,)
+VPICK = (1,)
+GATHER, SCATTER = 2.0, 3.8
 
 SCRATCH = {
-    "X": ("sbuf", [128, 4608], B),
+    "X": ("sbuf", [128, SP + 6144], B), "yo": ("sbuf", [128, SP + 4096], B),
     "xg": ("sbuf", [128, 8192], B), "mg": ("sbuf", [128, 8192], B), "pg": ("sbuf", [128, 8192], B),
-    "ji": ("sbuf", [128, 512], I), "z": ("sbuf", [128, 512], B), "w": ("sbuf", [128, 1], F),
+    "ji": ("sbuf", [128, 512], I), "z": ("sbuf", [128, 512], B), "za": ("sbuf", [128, 512], B), "w": ("sbuf", [128, 1], F),
     "jo": ("sbuf", [128, 512], F), "pi": ("sbuf", [128, 512], I), "hu": ("sbuf", [128, 512], U),
-    "yy": ("sbuf", [128, 512], B), "vv": ("sbuf", [128, 512], B), "nv": ("sbuf", [128, 512], B),
-    "t1": ("sbuf", [128, 512], B), "t2": ("sbuf", [128, 512], B), "nb": ("sbuf", [128, 512], B),
-    "cz": ("sbuf", [128, 1024], B), "yo": ("sbuf", [128, 2560], B),
-    "s0": ("sbuf", [128, 256], F), "s1": ("sbuf", [128, 128], F), "s2": ("sbuf", [128, 64], F), "s3": ("sbuf", [128, 32], F),
-    "p1": ("sbuf", [128, 128], F), "cc": ("sbuf", [128, 128], F), "cgk": ("sbuf", [128, 128], F),
-    "fin": ("sbuf", [128, 96], F), "wa": ("sbuf", [128, 48], F), "sig": ("sbuf", [128, 32], F), "a1": ("sbuf", [128, 1], F),
-    "zz": ("sbuf", [128, 128], B), "oy": ("sbuf", [128, 32], U), "of": ("sbuf", [128, 48], F), "ou": ("sbuf", [128, 96], U),
-    "qa": ("sbuf", [128, 144], B), "qb": ("sbuf", [128, 144], B), "r8": ("sbuf", [128, 128], B), "ro8": ("sbuf", [128, 384], B),
-    "yv": ("sbuf", [128, 512], B), "ri": ("sbuf", [128, 32], I), "cu": ("sbuf", [128, 32], U),
-    "one": ("sbuf", [128, 256], B), "idb": ("sbuf", [128, 128], B), "idn": ("sbuf", [128, 128], B), "id16": ("sbuf", [128, 128], B),
-    "idm": ("sbuf", [128, 128], B), "idf": ("sbuf", [128, 128], F), "o32": ("sbuf", [128, 128], F), "bd": ("sbuf", [128, 128], B),
-    "bdw": ("sbuf", [128, 128], B), "bdw2": ("sbuf", [128, 128], B), "qw": ("sbuf", [128, 144], B), "cst": ("sbuf", [128, 128], B),
-    "rx": ("sbuf", [128, 32], B), "pat": ("sbuf", [128, 512], B), "mp": ("sbuf", [128, 2048], B),
-    "m192": ("sbuf", [128, 256], B), "zo": ("sbuf", [128, 8], U), "zm": ("sbuf", [128, 128], B), "ro": ("sbuf", [128, 112], B),
-    "co": ("sbuf", [128, 112], F), "cm": ("sbuf", [128, 96], F), "c8": ("sbuf", [128, 32], F),
-    "i1": ("sbuf", [128, 128], I), "i2": ("sbuf", [128, 128], I), "i3": ("sbuf", [128, 16], I), "i4": ("sbuf", [128, 16], I),
-    "i5": ("sbuf", [128, 16], I), "pc": ("sbuf", [128, 2], F), "il": ("sbuf", [128, 16], F),
-    "ZU0": ("psum", [128, 512], F), "ZU1": ("psum", [128, 512], F), "GS0": ("psum", [128, 512], F), "GS1": ("psum", [128, 512], F),
-    "TV": ("psum", [128, 512], F), "DZ": ("psum", [128, 512], F), "SR": ("psum", [128, 512], F), "LL": ("psum", [128, 512], F),
+    "yy": ("sbuf", [128, 512], B), "vv": ("sbuf", [128, 512], B), "nb": ("sbuf", [128, 512], B),
+    "cz": ("sbuf", [128, 2, 768], B), "yv": ("sbuf", [128, 512], B),
+    "h0": ("sbuf", [128, 256], F), "h1": ("sbuf", [128, 256], F), "h2": ("sbuf", [128, 128], F), "h3": ("sbuf", [128, 64], F),
+    "k1": ("sbuf", [128, 256], B), "k2": ("sbuf", [128, 128], B), "k3": ("sbuf", [128, 64], B),
+    "pp": ("sbuf", [128, 128], F), "dd": ("sbuf", [128, 256], B), "fin": ("sbuf", [128, 2, 2, 32], F), "wa": ("sbuf", [128, 32], F),
+    "k4": ("sbuf", [128, 2, 32], B), "sb": ("sbuf", [128, 4, 144], B),
+    "oy": ("sbuf", [128, 32], U), "ou": ("sbuf", [128, 96], U), "ri": ("sbuf", [128, 32], I), "cu": ("sbuf", [128, 48], U),
+    "one": ("sbuf", [128, 256], B), "idb": ("sbuf", [128, 128], B), "ids": ("sbuf", [128, 6, 128], B),
+    "idf": ("sbuf", [128, 128], F), "o32": ("sbuf", [128, 128], B),
+    "bd": ("sbuf", [128, 128], B), "bd4": ("sbuf", [128, 8, 16], B), "f4": ("sbuf", [128, 128], B), "kc": ("sbuf", [128, 256], B),
+    "zq": ("sbuf", [128, 128], B), "bdw": ("sbuf", [128, 128], B), "bdw2": ("sbuf", [128, 128], B), "qw": ("sbuf", [128, 144], B),
+    "cst": ("sbuf", [128, 128], B), "mp": ("sbuf", [128, 1024], B), "m192": ("sbuf", [128, 256], B),
+    "r8": ("sbuf", [128, 128], B), "ro": ("sbuf", [128, 384], B), "cm": ("sbuf", [128, 6, 16], F), "cy": ("sbuf", [128, 16], F),
+    "c8": ("sbuf", [128, 32], F), "adj": ("sbuf", [128, 16], F), "i3": ("sbuf", [128, 16], I), "i4": ("sbuf", [128, 2], I),
+    "pc": ("sbuf", [128, 2], F), "a1": ("sbuf", [128, 1], F), "a32": ("sbuf", [128, 1], F),
+    "Z0": ("psum", [128, 512], F), "Z1": ("psum", [128, 512], F), "S0": ("psum", [128, 2, 256], F), "S1": ("psum", [128, 2, 256], F),
+    "HH": ("psum", [128, 2, 2, 8, 16], F), "UU": ("psum", [128, 512], F), "DZ": ("psum", [128, 512], F), "LL": ("psum", [128, 512], F),
 }
-SEMAPHORES = ["cv", "cs", "cp", "cg", "ldx", "ldj", "ldz", "ldw", "sy0", "sy1", "sj0", "sj1", "sz0", "sz1"]
+SEMAPHORES = ["cv", "cs", "cp", "cg", "ldx", "pk", "ldj", "ldk", "ldz", "ldw", "sy0", "sy1", "sj0", "sj1", "sz0", "sz1"]
 for _t in range(3):
     for _c in range(2):
         SCRATCH["W%d%d" % (_t, _c)] = ("sbuf", [128, 17 * 256], F)
         SCRATCH["D%d%d" % (_t, _c)] = ("dram", [8, 32, 256], F)
-        SCRATCH["RG%d%d" % (_t, _c)] = ("sbuf", [128, 32], F)
+        SCRATCH["RG%d%d" % (_t, _c)] = ("sbuf", [128, 2, 32], F)
         SCRATCH["RY%d%d" % (_t, _c)] = ("sbuf", [128, 256], B)
         for _k in ("aj", "ag", "ay", "lj", "lg", "ly", "do", "dr", "dt"):
             SEMAPHORES.append("%s%d%d" % (_k, _t, _c))
-BANKS = ("ZU0", "ZU1", "GS0", "GS1", "TV", "DZ", "SR", "LL")
+BANKS = ("Z0", "Z1", "S0", "S1", "HH", "UU", "DZ", "LL")
 ESEM = {"v": "cv", "s": "cs", "p": "cp", "g": "cg"}
+IDS = (-1.0, 16.0, -16.0, -2048.0, 2.0, -2.0)
+WAKE, FILL, AHEAD = 100.0, 200.0, {"v": 150.0, "s": 400.0, "p": 100.0, "g": 300.0, "y": 0.0}
 
 
-def weave(a, b):
-    out, n = [], max(len(a), 1)
-    done = 0
-    for i, o in enumerate(a):
-        out.append(o)
-        upto = (i + 1) * len(b) // n
-        out.extend(b[done:upto])
-        done = upto
-    return out + b[done:]
+def knockout(c, fill):
+    out = []
+    for lv in range(4):
+        out += ["pp", "tmp"] + fill[2 * lv].split() + ["dd"] + fill[2 * lv + 1].split()
+        out += ["%s%d" % (k, lv + 1) for k in "sHK"] if lv < 3 else ["%s%d" % (k, c) for k in ("fs", "fh", "kb")]
+    return out + ["sb30", "sb31"]
 
 
-def stages(chain, fill):
-    cuts = [2] + [2 + 8 * lv + d for lv in range(4) for d in (2, 3, 6, 8)]
-    out, a = [], 0
-    for j, b in enumerate(cuts):
-        out += chain[a:b] + (fill[j] if j < len(fill) else [])
-        a = b
+def vector_line(t):
+    out = ("x1 pi1 pi1 hu1 m0_0 m0_1 z1 m0_2 m0_3 pg0 pg1 pg2 pi2 pi3 pi2" if t else "x1 m0_0 m0_1 m0_2 m0_3 pg0 pg1 pg2 pi2 pi3").split()
+    out += "ri pi2 pg3 hu2 m1_0 m1_1 m1_2 m1_3".split() + ["Yp"] * (t == 2) + "pg4 pg5 s0".split()
+    out += knockout(0, ["pg6", "pg7", "ri m2_0", "m2_1", "cm1 m2_2", "m2_3", "cu", "pg8"]) + "M6 oy0 M7 pg9 pg10 wa pg11 sb20 sb21 s0 sb00 sb01".split()
+    out += knockout(1, ["pg12", "ou0", "oj0", "pg13", "pg14", "pg15", "z0", ""])
+    out += ("X0 oy1 pi0 pi1 wa sb20 sb21 sb10 sb11 ou1 a32 X1 pi0 oj1 pi0 hu0" if t < 2 else "cu2 oy1 Y wa sb20 sb21 sb10 sb11 ou1 oj1").split()
+    return out
+
+
+def scalar_line(t):
+    out = ("x0 cl1 za1 x2 nb1" if t else "nb0 nb1 x0 x2") + " x3 x4 H0 x5 x6 x7 m6 m7 y0"
+    if t < 2:
+        return (out + " H0 vv nv0 cl0 za0 J%d0 nb0 y1 nv1 J%d1" % (t + 1, t + 1)).split()
+    return (out + " H0 vv nv0 e0 cl0 za0 jo0 y1 nv1 nb0 e1 jo1 cl1 za1").split()
+
+
+def order(ops, setup, lines):
+    n = len(ops)
+    pred, lastw, readers = [set() for _ in ops], {}, {}
+    for i, (eng, fn, rd, wr, tok, busy, lat) in enumerate(ops):
+        wr = wr + [k for k in rd if k in BANKS]
+        for k in rd + wr:
+            pred[i].update(lastw.get(k, []))
+        for k in wr:
+            pred[i].update(readers.get(k, []))
+        for k in rd:
+            readers.setdefault(k, []).append(i)
+        for k in wr:
+            lastw[k], readers[k] = [i], []
+        if fn is None:
+            pred[i].add(i - 1)
+        pred[i].discard(i)
+    soft, writers = set(), {}
+    for i, a in enumerate(ops):
+        if (i >= setup or a[0] == "y") and a[3]:
+            writers.setdefault((a[0], a[3][0]), []).append(i)
+    for eng, keys in lines.items():
+        line = [writers[eng, k].pop(0) for k in keys]
+        for j, i in zip(line, line[1:]):
+            if j not in pred[i]:
+                pred[i].add(j)
+                soft.add((j, i))
+
+    def gap(j, i):
+        a, b = ops[j], ops[i]
+        if (j, i) in soft or a[0] == b[0] and (a[0] == "p" or (a[4] is not None and a[4] == b[4])):
+            return a[5]
+        return a[5] + a[6] + WAKE
+    succ = [[] for _ in ops]
+    for i in range(n):
+        for j in pred[i]:
+            succ[j].append(i)
+    rank, todo = [0.0] * n, [len(s) for s in succ]
+    back = [i for i in range(n) if not todo[i]]
+    for i in back:
+        rank[i] = max([ops[i][5] + ops[i][6]] + [gap(i, j) + rank[j] for j in succ[i]])
+        for j in pred[i]:
+            todo[j] -= 1
+            if not todo[j]:
+                back.append(j)
+    assert len(back) == n
+    left, est, free, out = [len(p) for p in pred], [0.0] * n, {}, []
+    ready, last = [i for i in range(n) if not left[i]], 0
+    while ready:
+        at = {i: max(est[i], free.get(ops[i][0], 0.0)) if ops[i][1] else est[i] for i in ready}
+        first = min(ready, key=lambda i: (at[i], -rank[i]))
+        i = first
+        if ops[i][1]:
+            near = [j for j in ready if ops[j][0] == ops[i][0] and ops[j][1] and at[j] <= at[i] + AHEAD[ops[i][0]]]
+            best = max(near, key=lambda j: (rank[j], -j))
+            short = [j for j in near if at[j] < at[best] and at[j] + ops[j][5] <= at[best] + FILL]
+            i = max(short, key=lambda j: (rank[j], -j)) if short else best
+            if ops[i][0] == "p":
+                if last + 1 in near and ops[last + 1][3] == ops[last][3]:
+                    i = last + 1
+                last = i
+        ready.remove(i)
+        out.append(ops[i])
+        if ops[i][1]:
+            free[ops[i][0]] = at[i] + ops[i][5]
+        for j in succ[i]:
+            est[j] = max(est[j], at[i] + gap(i, j))
+            left[j] -= 1
+            if not left[j]:
+                ready.append(j)
     return out
 
 
@@ -68,7 +148,7 @@ def emit(g, T, ops):
     know = {e: {} for e in Q}
     clock = {}
     lastw, readers, bank, total = {}, {}, {}, {}
-    for eng, fn, rd, wr, tok in ops:
+    for eng, fn, rd, wr, tok, _, _ in ops:
         deps = []
         for k in rd:
             if k not in BANKS:
@@ -115,39 +195,52 @@ def emit(g, T, ops):
             g.wait_ge(T.sem[s], v)
 
 
+def size(ap):
+    n = 1
+    for d in ap.shape[1:]:
+        n *= d
+    return n
+
+
 def rank_program(g, core, T, topo):
     rank = T.rank_of(core)
     if rank is None:
         return
     ops = []
 
-    def o(eng, fn, rd, wr, tok=None):
-        return (eng, fn, list(rd), list(wr), tok)
+    def o(eng, fn, rd, wr, busy, lat=0.0, tok=None):
+        return (eng, fn, list(rd), list(wr), tok, busy, lat)
 
-    def tt(out, a, b, op, rd, wr):
-        return o("v", lambda q: q.tensor_tensor(out, a, b, op), rd, wr)
+    def vec(fn, n, rd, wr):
+        return o("v", fn, rd, wr, 32.0 + 0.83 * n)
 
-    def ts(out, a, s1, op0, rd, wr, s2=None, op1=None):
+    def tt(out, a, b, op, rd, wr, r=1.0):
+        return vec(lambda q: q.tensor_tensor(out, a, b, op), r * size(b), rd, wr)
+
+    def ts(out, a, s1, op0, rd, wr, s2=None, op1=None, r=1.0):
         if op1 is None:
-            return o("v", lambda q: q.tensor_scalar(out, a, s1, None, op0), rd, wr)
-        return o("v", lambda q: q.tensor_scalar(out, a, s1, s2, op0, op1), rd, wr)
+            return vec(lambda q: q.tensor_scalar(out, a, s1, None, op0), r * size(a), rd, wr)
+        return vec(lambda q: q.tensor_scalar(out, a, s1, s2, op0, op1), r * size(a), rd, wr)
 
-    def cp(out, a, rd, wr):
-        return o("v", lambda q: q.tensor_copy(out, a), rd, wr)
+    def cp(out, a, rd, wr, n=None):
+        return vec(lambda q: q.tensor_copy(out, a), n or size(out), rd, wr)
 
     def ms(ap, c, wr):
-        return o("v", lambda q: q.memset(ap, c), [], wr)
+        return vec(lambda q: q.memset(ap, c), 0.5 * size(ap), [], wr)
 
-    def act(out, a, fn, rd, wr, bias=0.0, scale=1.0):
-        return o("s", lambda q: q.activation(out, a, fn, bias=bias, scale=scale), rd, wr)
+    def scan(out, a, b, op0, op1, rd, wr, r=1.0):
+        return vec(lambda q: q.tensor_tensor_scan(out, a, b, 0.0, op0, op1), r * size(out), rd, wr)
 
-    def mm(out, l, r, st, sp, rd, wr):
-        return o("p", lambda q: q.matmul(out, l, r, st, sp), rd, wr)
+    def act(out, a, fn, rd, wr, bias=0.0, scale=1.0, r=1.0):
+        return o("s", lambda q: q.activation(out, a, fn, bias=bias, scale=scale), rd, wr, 120.0 + 0.83 * r * size(out))
 
-    def dma(eng, out, a, rd, wr, sem, n=1):
-        return o(eng, lambda q: q.dma_start(out, a), rd, wr, (sem, 16 * n))
+    def mm(out, l, r, st, sp, rd, wr, slow=1):
+        return o("p", lambda q: q.matmul(out, l, r, st, sp), rd, wr, 5.0 + 0.7 * slow * max(64, size(r)))
 
-    def send(t, c, kind, dst, src, rd, land):
+    def dma(eng, out, a, rd, wr, sem, kb, n=1):
+        return o(eng, lambda q: q.dma_start(out, a), rd, wr, 60.0 if eng == "s" else 2.5 * kb, 1000.0 + (2.5 * kb if eng == "s" else 0), (sem, 16 * n))
+
+    def send(t, c, kind, dst, src, rd, land, kb):
         peer = T.cores[rank ^ STEPS[t]]
         assert topo.may_write(core, peer)
         rid, pid, _ = topo.addr(peer)
@@ -157,13 +250,13 @@ def rank_program(g, core, T, topo):
 
         def f(q):
             q.remote_dma(dst, src, T.sem[a], T.sem[l], pid, rid, topo.mask(core, peer))
-        return [o("g", f, rd, [], (l, n)), o("g", None, [], [land], (a, back))]
+        return [o("g", f, rd, [], 300.0, 700.0 + 10.0 * kb, (l, n)), o("g", None, [], [land], 0.0, 500.0, (a, back))]
 
-    def iota(out, pat, base, cm, wr):
-        return o("g", lambda q: q.iota(out, pat, base, cm), [], wr)
+    def iota(out, pat, base, cm, wr, **kw):
+        return o("g", lambda q: q.iota(out, pat, base, cm, **kw), [], wr, 130.0 + 1.66 * size(out))
 
     def asel(out, a, pat, cmp, base, cm, rd, wr):
-        return o("g", lambda q: q.affine_select(out, a, pat, cmp, 0.0, base, cm), rd, wr)
+        return o("g", lambda q: q.affine_select(out, a, pat, cmp, 0.0, base, cm), rd, wr, 170.0 + 1.66 * size(out))
 
     def W(t, c):
         return T["W%d%d" % (t, c)]
@@ -171,290 +264,249 @@ def rank_program(g, core, T, topo):
     def ln(c):
         return slice(256 * c, 256 * c + 256)
 
-    XW = (T.X[:, 0:2304], T.X[:, 2304:4608])
-    XK = ["X0", "X1"]
-    OJ, OZ, OS = (0, 80), (16, 64), (32, 48)
-    CL, CW = (0, 768), (256, 512)
+    def zs(j):
+        return T.z[:, 256 * (j // 2) + j % 2:256 * (j // 2) + 256:2]
 
-    ops += [dma("s", T.w[:], T.wt[:], [], ["w"], "ldw"), dma("y", T.z[:], T.zd[:], [], ["z0", "z1"], "ldz"),
-            dma("s", T.ji[:], T.jn[:], [], ["ji"], "ldj"), dma("y", T.X[:, 256:4352], T.xt[:], [], ["Xl"], "ldx")]
+    def idx(v):
+        return T.ids[:, IDS.index(v), :]
+
+    REC = T.X[:, SP:SP + 4096]
+    XK = ["X0", "X1", "Xl"]
+    OJ, OS, OZ = (0, 48), (16, 80), (32, 64)
+
+    ops += [dma("s", T.w[:], T.wt[:], [], ["w"], "ldw", 1), dma("y", T.z[:], T.zd[:], [], ["z0", "z1"], "ldz", 128),
+            dma("s", T.ji[:, ln(0)], T.jn[:, ln(0)], [], ["ji0"], "ldj", 128), dma("y", REC, T.xt[:], [], ["Xl"], "ldx", 1024),
+            dma("y", T.ji[:, ln(1)], T.jn[:, ln(1)], [], ["ji1"], "ldk", 128)]
+    small = dict(allow_small_or_imprecise_dtypes=True)
     ops += [ms(T.one[:], 1.0, ["one"]),
             asel(T.bd[:], T.one[:, 0:128], [[-16, 8], [0, 16]], OP.is_ge, 0, 1, ["one"], ["bd"]),
             asel(T.bd[:], T.bd[:], [[16, 8], [0, 16]], OP.is_ge, 15, -1, ["bd"], ["bd"]),
             asel(T.idb[:], T.one[:, 0:128], [[-1, 128]], OP.is_equal, 0, 1, ["one"], ["idb"]),
-            iota(T.i3[:], [[16, 16]], 0, 0, ["i3"]), iota(T.i4[:, 0:2], [[0, 2]], 0, 1, ["i4"]),
-            iota(T.i1[:], [[0, 8], [-1, 8], [0, 2]], 8, 1, ["i1"]), iota(T.i2[:], [[0, 16], [2, 8]], 1, 0, ["i2"]),
-            iota(T.i5[:], [[-8, 16]], 128, 1, ["i5"]),
-            ms(T.cst[0:64, :], 6144.0, ["cst"]), ms(T.cst[64:128, :], 33.0 / 64, ["cst"]),
-            ms(T.mp[:], 1.0, ["mp"]), ms(T.pat[:, 0:256], 0.0, ["pat"]), ms(T.pat[:, 256:512], 1.0, ["pat"]),
-            ms(T.X[:, 0:256], 0.0, ["X0"]), ms(T.X[:, 4352:4608], 0.0, ["X1"]), ms(T.mp[:, 0::16], 0.0, ["mp"]),
-            ms(T.qw[:], 0.0, ["qw"]), ms(T.rx[:, 0:8], 0.0, ["rx"]), ms(T.m192[:], -192.0, ["m192"]), ms(T.o32[:], 32.0, ["o32"]),
-            ts(T.idm[:], T.idb[:], -2048.0, OP.mult, ["idb"], ["idm"]),
+            iota(T.i3[:], [[16, 16]], 0, 0, ["i3"]), iota(T.i4[:], [[0, 2]], 0, 1, ["i4"]),
+            iota(T.kc[:], [[0, 16], [1, 16]], 1, 0, ["kc"], **small),
+            asel(T.r8[:], T.one[:, 0:128], [[-1, 8], [-8, 16]], OP.is_equal, 0, 1, ["one"], ["r8"]),
+            iota(T.ro[:], [[0, 8], [256 - SP, 3], [0, 16]], SP, 0, ["ro"], **small),
+            asel(T.ro[:], T.ro[:], [[-1, 8], [0, 3], [-8, 16]], OP.is_equal, 0, 1, ["ro"], ["ro"]),
+            ms(T.cst[0:64, :], 6144.0, ["cst0"]), ms(T.cst[64:128, :], 33.0 / 64, ["cst1"]),
+            ms(T.mp[:], 1.0, ["mp"]), ms(T.dd[:], BIG * BIG, ["dd"]),
+            ms(T.sb[:], 0.0, ["sb%d%d" % (i, b) for i in range(4) for b in range(2)]), ms(T.mp[:, 0::16], 0.0, ["mp"]),
+            ms(T.qw[:], 0.0, ["qw"]), ms(T.m192[:], -192.0, ["m192"]), ms(T.o32[:], 32.0, ["o32"]), ms(T.f4[0:1, :], BIG, ["f4"]),
             ts(T.bdw[:], T.bd[:], T.w[:], OP.mult, ["bd", "w"], ["bdw"]),
-            ts(T.bdw2[:], T.bd[:], T.w[:], OP.mult, ["bd", "w"], ["bdw2"], 2.0, OP.mult)]
-    late = [ts(T.idn[:], T.idb[:], -1.0, OP.mult, ["idb"], ["idn"]), ts(T.id16[:], T.idb[:], 16.0, OP.mult, ["idb"], ["id16"]),
+            ts(T.bdw2[:], T.bd[:], T.w[:], OP.mult, ["bd", "w"], ["bdw2"], 2.0, OP.mult),
+            ts(T.bd4[:], T.bd[:], BIG, OP.mult, ["bd"], ["bd4"], r=0.5),
             cp(T.idf[:], T.idb[:], ["idb"], ["idf"]), cp(T.qw[:, 15:143:16], T.bdw[:, 0::16], ["bdw", "qw"], ["qw"]),
-            cp(T.rx[:, 8:16], T.bd[:, 0::16], ["bd"], ["rxa"]), cp(T.rx[:, 16:24], T.bd[:, 0::16], ["bd"], ["rxb"]),
-            ts(T.rx[:, 24:32], T.bd[:, 0::16], -1.0, OP.mult, ["bd"], ["rxc"]),
+            ts(T.zq[:], T.bd[:], -BIG, OP.mult, ["bd"], ["zq"], r=0.5),
             ts(T.i4[:, 0:1], T.i4[:, 0:1], 15, OP.bitwise_and, ["i4"], ["i4a"]),
             ts(T.i4[:, 1:2], T.i4[:, 1:2], 1, OP.bitwise_and, ["i4"], ["i4b"]),
-            ts(T.i1[:], T.i1[:], 7, OP.bitwise_and, ["i1"], ["i1"]), ts(T.i5[:], T.i5[:], 3, OP.arith_shift_right, ["i5"], ["i5"]),
-            cp(T.TV[:, 384:512], T.i2[:], ["i2", "TV"], ["kc"]), cp(T.pc[:], T.i4[:, 0:2], ["i4a", "i4b"], ["pc"]),
-            ts(T.zm[:], T.i1[:], 0.0, OP.is_equal, ["i1"], ["zm"]),
-            ts(T.ro[:, 96:112], T.i5[:], 16.0, OP.is_equal, ["i5"], ["ro6"]),
-            ts(T.il[:], T.i3[:], T.pc[:, 0:1], OP.add, ["i3", "pc"], ["il"]),
-            ts(T.zo[:], T.i3[:, 0:8], 0.125, OP.mult, ["i3", "pc"], ["zo"], T.pc[:, 1:2], OP.add)]
-    for j, (rs, ca, cb, ma, mb) in enumerate(((256.0, 1.0, 0.0, 0.0, 60000.0), (BIG, 1.0, 0.0, 1.0, 256.0), (BIG, 1.0, 0.0, None, None),
-                                              (-BIG, 1.0, 2048.0, None, None), (-BIG, 1.0, 256.0, 1.0, 0.0), (256.0, 1.0, 0.0, 0.0, 0.0))):
-        sl = slice(16 * j, 16 * j + 16)
-        if j > 2:
-            late.append(ts(T.ro[:, sl], T.ro[:, 96:112], rs, OP.mult, ["ro6"], ["ro%d" % j]))
-        late.append(ts(T.co[:, sl], T.il[:], ca, OP.mult, ["il"], ["co%d" % j], cb, OP.add))
-        if ma is not None:
-            late.append(ts(T.cm[:, sl], T.il[:], ma, OP.mult, ["il"], ["cm%d" % j], mb, OP.add))
-    late += [ts(T.a1[:], T.pc[:, 1:2], 2040.0, OP.mult, ["pc"], ["a1"], -1.0, OP.add),
-             ts(T.co[:, 96:112], T.il[:], 8.0, OP.mult, ["il", "a1"], ["co6"], T.a1[:], OP.add), ms(T.yo[:, 0:256], 0.0, ["Yd"]), ms(T.yo[:, 2304:2560], 0.0, ["Yd"]), ts(T.c8[:, 0:16], T.il[:], 8.0, OP.mult, ["il"], ["c80"], 256.0, OP.add), ts(T.c8[:, 16:32], T.il[:], 8.0, OP.mult, ["il"], ["c81"])]
+            cp(T.pc[:], T.i4[:], ["i4a", "i4b"], ["pc"]),
+            ts(T.a1[:], T.pc[:, 1:2], 2040.0, OP.mult, ["pc"], ["a1"], -1.0, OP.add)]
+    ops += [ts(idx(v), T.idb[:], v, OP.mult, ["idb"], ["id%d" % v], r=0.5) for v in IDS]
+    ops += [ts(T.cm[:, j, :], T.i3[:], T.pc[:, 0:1], OP.add, ["i3", "pc"], ["cm%d" % j]) for j in (0, 2, 4)]
+    ops += [ts(T.cy[:], T.cm[:, 0, :], 8.0, OP.mult, ["cm0", "a1"], ["cy"], T.a1[:], OP.add),
+            ts(T.c8[:, 0:16], T.cm[:, 0, :], 8.0, OP.mult, ["cm0"], ["c80"]),
+            ts(T.c8[:, 16:32], T.cm[:, 0, :], 8.0, OP.mult, ["cm0"], ["c81"], 2048.0, OP.add),
+            ts(T.adj[:], T.i3[:], 128.0, OP.is_ge, ["i3"], ["adj"], -1024.0, OP.mult)]
 
     def tables(t, c):
         w, d, k = W(t, c), T["D%d%d" % (t, c)], "%d%d" % (t, c)
-        out = send(t, c, "j", w[:, 4096:4352], w[:, 0:256], ["J" + k], "Jr" + k)
-        out += [dma("y", d[:, 0:16, :], w[:, 0:256], ["J" + k], ["Do" + k], "do" + k),
-                dma("y", d[:, 16:32, :], w[:, 4096:4352], ["Jr" + k], ["Dr" + k], "dr" + k)]
-        out += [dma("y", w[:, 256 * s:256 * s + 256], d[:, s:s + 16, :], ["Do" + k, "Dr" + k], ["Wt" + k], "dt" + k, 15) for s in range(1, 16)]
+        out = send(t, c, "j", w[:, 4096:4352], w[:, 0:256], ["J" + k, "RY%d1" % (t - 1)], "Jr" + k, 128)
+        out += [dma("y", d[:, 0:16, :], w[:, 0:256], ["J" + k], ["Do" + k], "do" + k, 128),
+                dma("y", d[:, 16:32, :], w[:, 4096:4352], ["Jr" + k], ["Dr" + k], "dr" + k, 128)]
+        out += [dma("y", w[:, 256 * s:256 * s + 256], d[:, s:s + 16, :], ["Do" + k, "Dr" + k], ["Wt" + k], "dt" + k, 128, 15) for s in range(1, 16)]
         return out
 
-    def prep1(c):
-        zu = T["ZU%d" % c]
-        return [mm(T.SR[:, 256:512], T.bdw[:], T.z[:, ln(c)], True, True, ["bdw", "z%d" % c], ["SR", "raw"]),
-                mm(zu[:, 0:256], T.idb[:], T.z[:, ln(c)], True, True, ["idb", "z%d" % c], ["ZU%d" % c, "zp%d" % c])]
-
-    def prep2(c):
-        zu, k = T["ZU%d" % c], ["ZU%d" % c, "u%d" % c]
-        return [act(T.nb[:, ln(c)], T.SR[:, 256:512], AF.Identity, ["SR", "raw"], ["nb%d" % c], 191.5 + 1.0 / 2048, 1.0 / 1024),
-                mm(zu[:, 256:512], T.cst[:], T.one[:], True, False, ["cst", "one"], k),
-                mm(zu[:, 256:512], T.bdw2[:], T.z[:, ln(c)], False, False, ["bdw2", "z%d" % c], k),
-                mm(zu[:, 256:512], T.idm[:], T.nb[:, ln(c)], False, True, ["idm", "nb%d" % c], k)]
+    def factor(c):
+        k = ["UU"]
+        return [mm(T.S0[:, 1], T.bdw[:], T.z[:, ln(c)], True, True, ["bdw", "z%d" % c], ["S0"]),
+                act(T.nb[:, ln(c)], T.S0[:, 1], AF.Identity, ["S0"], ["nb%d" % c], 191.5 + 1.0 / 2048, 1.0 / 1024),
+                mm(T.UU[:, ln(c)], T.cst[:], T.one[:], True, False, ["cst0", "cst1", "one"], k),
+                mm(T.UU[:, ln(c)], T.bdw2[:], T.z[:, ln(c)], False, False, ["bdw2", "z%d" % c], k),
+                mm(T.UU[:, ln(c)], idx(-2048), T.nb[:, ln(c)], False, True, ["id-2048", "nb%d" % c], k)]
 
     def prod(t, c):
-        return [tt(T.pi[:, 256 * c + 128 * b:256 * c + 128 * b + 128], W(t, c)[:, b:256:2], T["ZU%d" % c][:, 256 + b:512:2], OP.mult,
-                   ["J%d%d" % (t, c), "ZU%d" % c, "u%d" % c], ["pi%d" % (2 * c + b)]) for b in range(2)]
+        src, k = (T.ji[:, ln(c)], "ji%d" % c) if t == 0 else (W(t, c)[:, 0:256], "J%d%d" % (t, c))
+        return [tt(T.pi[:, 256 * c + 128 * b:256 * c + 128 * b + 128], src[:, b:256:2], T.UU[:, 256 * c + b:256 * c + 256:2], OP.mult,
+                   [k, "UU"], ["pi%d" % (2 * c + b)]) for b in range(2)]
 
     def hops(t, c, w):
-        st = [[], [], []]
+        out = []
         for a in range(256 * c, 256 * c + 256, w):
             sl, qs = slice(a, a + w), range(a // 128, (a + w) // 128)
             k = ["pi%d" % q for q in qs]
             if t > 0:
-                st[0].append(ts(T.pi[:, sl], T.pi[:, sl], T.LL[:, 128:129], OP.add, k + ["LL", "acol"], k))
-            st[1].append(ts(T.pi[:, sl], T.pi[:, sl], 5, OP.arith_shift_right, k, k, 4095, OP.bitwise_and))
-            st[2].append(cp(T.hu[:, sl], T.pi[:, sl], k, ["hu%d" % q for q in qs]))
-        return st[0] + st[1] + st[2]
+                out.append(ts(T.pi[:, sl], T.pi[:, sl], T.a32[:], OP.add, k + ["a32"], k))
+            out.append(ts(T.pi[:, sl], T.pi[:, sl], 5, OP.arith_shift_right, k, k, 4095, OP.bitwise_and))
+            out.append(cp(T.hu[:, sl], T.pi[:, sl], k, ["hu%d" % q for q in qs]))
+        return out
 
-    def pick(eng, l0, n):
-        src = T.X[:, 256:4352].indirect(T.hu[:, l0:l0 + n])
-        out, rd = T.xg[:, 16 * l0:16 * (l0 + n)], XK + ["Xl", "hu%d" % (l0 // 128)]
-        wr = ["x%d" % j for j in range(l0 // 64, (l0 + n + 63) // 64)]
-        return [act(out, src, AF.Copy, rd, wr) if eng == "s" else cp(out, src, rd, wr)]
+    def pick(j):
+        out, src, rd, wr = T.xg[:, 1024 * j:1024 * j + 1024], REC.indirect(T.hu[:, 64 * j:64 * j + 64]), XK + ["hu%d" % (j // 2)], ["x%d" % j]
+        return [cp(out, src, rd, wr, GATHER * 1024) if j in VPICK else act(out, src, AF.Copy, rd, wr, r=GATHER)]
 
-    def mins(q):
-        c, h = q // 2, q % 2
-        return [tt(T.mg[:, 4096 * c + 256 * k + 128 * h:4096 * c + 256 * k + 128 * h + 128], T.xg[:, 2048 * q + k:2048 * (q + 1):16],
-                   T["ZU%d" % c][:, h:256:2], OP.min, ["x%d" % (2 * q), "x%d" % (2 * q + 1), "ZU%d" % c, "zp%d" % c], ["m%d_%d" % (q, k)])
-                for k in range(16)]
+    def spread(j):
+        bk = "Z%d" % (j % 2)
+        return [mm(T[bk][:, r::4], T.idb[:], zs(j), True, True, ["idb", "z%d" % (j // 2)], [bk]) for r in range(4)]
 
-    def pscan(q, n=1):
-        def piece(j):
-            w = 2048 // n
-            sl = slice(2048 * q + w * j, 2048 * q + w * j + w)
-            return o("v", lambda e: e.tensor_tensor_scan(T.pg[:, sl], T.mp[:, 0:w], T.xg[:, sl], 0.0, OP.mult, OP.max),
-                     ["mp", "x%d" % (2 * q), "x%d" % (2 * q + 1)], ["pg%d_%d" % (q, i) for i in range(8 * j // n, 8 * (j + 1) // n)])
-        return [piece(j) for j in range(n)]
+    def over(j, h):
+        x, m, k = T.xg[:, 2048 * j + h:2048 * j + 2048:4], T.mg[:, 2048 * j + h:2048 * j + 2048:4], ["m%d_%d" % (j, h)]
+        return [tt(m, x, T["Z%d" % (j % 2)][:], OP.max, ["x%d" % (2 * j), "x%d" % (2 * j + 1), "Z%d" % (j % 2)], k)]
 
     def sums_x(q):
-        c, b = q // 2, q % 2
-        gs, k = T["GS%d" % c], ["GS%d" % c]
-        out = [] if b else [mm(gs[:], T.one[0:1, 0:128], T.pat[0:1, :], True, False, ["one", "pat"], k)]
-        return out + [mm(gs[:, 256 + 16 * b + kk:512:32], T.xg[:, 2048 * q + kk:2048 * (q + 1):16], T.rx[:, 8:16], False, False,
-                         ["x%d" % (2 * q), "x%d" % (2 * q + 1), "rxa"], k) for kk in range(16)]
+        b = q % 2
+        out = [] if b else [mm(T.HH[:, 0], T.f4[0:1, :], T.kc[0:1, :], True, False, ["f4", "kc"], ["HH"])]
+        return out + [mm(T.HH[:, 0, b, :, k:16], T.xg[:, 2048 * q + k:2048 * q + 2048:16], T.bd4[:, :, k:16], False, b == 1 and k == 15,
+                         ["x%d" % (2 * q), "x%d" % (2 * q + 1), "bd4"], ["HH"]) for k in range(16)]
 
-    def mins_sums(q):
+    def sums_m(q, h):
         c, b = q // 2, q % 2
+        s, bk = T["S%d" % c], ["S%d" % c]
         out = []
-        for kk, m in enumerate(mins(q)):
-            base = 4096 * c + 256 * kk + 128 * b
-            out += [m, mm(T["GS%d" % c][:, 16 * b + kk:512:32], T.mg[:, base:base + 128], T.rx[:, 16:32], False, kk == 15 and b == 1,
-                          ["m%d_%d" % (q, kk), "rxb", "rxc"], ["GS%d" % c])]
-        return out
+        st = 2 if q in SHARED else 1
+        if h == st - 1 and b == 0:
+            out.append(mm(s[:, 1], T.f4[0:1, :], T.one[0:1, :], True, False, ["f4", "one"], bk))
+        if h == st - 1:
+            out.append(mm(s[:, 1, 128 * b:128 * b + 128:st], zs(q), T.zq[:, ::st], False, False, ["z%d" % c, "zq"], bk))
+        keys = ["%s%d" % ("Mm"[h], j) for j in (2 * q, 2 * q + 1)] if q in SHARED else ["m%d_%d" % (q, h)]
+        return out + [mm(s[:, 1, 128 * b + k:128 * b + 128:16], T.mg[:, 2048 * q + k:2048 * q + 2048:16], T.bd4[:, :, 0], False, b == 1 and k == 16 - st,
+                         keys + ["bd4"], bk) for k in range(h, 16, 4 // st)]
 
-    def search(c):
-        gs, bk, f = T["GS%d" % c], "GS%d" % c, 48 * c
-        out = [o("v", lambda e: e.tensor_tensor_scan(T.s0[:], T.mp[:, 0:256], gs[:, 256:512], 0.0, OP.mult, OP.add), ["mp", bk], ["S0"]),
-               o("v", lambda e: e.tensor_tensor_scan(T.TV[:, 0:256], T.mp[:, 0:256], gs[:, 0:256], 0.0, OP.mult, OP.add), ["mp", bk, "TV", "G2", "G3"], ["G0"])]
-        gk = [(T.TV, 0, "TV"), (gs, 0, bk), (T.TV, 0, "TV"), (T.TV, 128, "TV"), (T.fin, f + 16, "fin%d" % c)]
-        ss = [T.s0[:], T.s1[:], T.s2[:], T.s3[:], T.fin[:, f:f + 16]]
-        sb = [T.s0, T.s1, T.s2, T.s3]
+    def shared(j):
+        a, zb, bk, k = 1024 * j, ("Z1", "S0")[j % 2], ("UU", "DZ")[j % 2], "z%d" % (j // 4)
+        b = 256 * (j // 4) + 128 * (j % 2) + (j // 2) % 2
+        z = T.z[:, b:b + 127:2]
+        return [mm(T[zb][..., r::8], T.idb[:], z, True, True, ["idb", k], [zb]) for r in range(8)] \
+            + [mm(T[bk][:], T.idb[:], T.xg[:, a + 1:a + 1024:2], True, False, ["x%d" % j], [bk])] \
+            + [mm(T[bk][:, r::8], idx(-1), z, False, r == 7, ["id-1", k], [bk]) for r in range(8)] \
+            + [act(T.mg[:, a + 1:a + 1024:2], T[bk][:], AF.Relu, [bk], ["m%d" % j]),
+               tt(T.mg[:, a:a + 1024:2], T.xg[:, a:a + 1024:2], T[zb][:], OP.max, ["x%d" % j, zb], ["M%d" % j])]
+
+    def quarter(q):
+        out = pick(2 * q) + pick(2 * q + 1)
+        if q in SHARED:
+            out += shared(2 * q) + shared(2 * q + 1) + sums_x(q) + sums_m(q, 1) + sums_m(q, 0)
+        else:
+            out += spread(q) + sums_x(q)
+            for h in range(4):
+                out += over(q, h) + sums_m(q, h)
+        if q % 2:
+            s, bk = T["S%d" % (q // 2)], "S%d" % (q // 2)
+            out += [act(T.h0[:], T.HH[:, 0], AF.Copy, ["HH"], ["H0"]),
+                    scan(s[:, 0, :], T.mp[:, 0:256], s[:, 1, :], OP.mult, OP.add, ["mp", bk], ["s0"])]
+        return out + [scan(T.pg[:, 512 * i:512 * i + 512], T.mp[:, 0:512], T.xg[:, 512 * i:512 * i + 512], OP.mult, OP.max, ["mp", "x%d" % (i // 2)],
+                           ["pg%d" % i], 0.5) for i in range(4 * q, 4 * q + 4)]
+
+    def search(t, c):
+        s, bk = T["S%d" % c], "S%d" % c
+        So = [s[:, 1, :], s[:, 0, 0:128], s[:, 1, 0:64], T.fin[:, c, 0, :]]
+        Ho = [T.h1[:], T.h2[:], T.h3[:], T.fin[:, c, 1, :]]
+        Ko = [T.k1[:], T.k2[:], T.k3[:], T.k4[:, c, :]]
+        out = []
         for lv in range(4):
-            n = 128 >> lv
-            (bi, a, ki), (bo, a2, ko) = gk[lv], gk[lv + 1]
-            G, S, G2, S2 = "G%d" % lv, "S%d" % lv, "G%d" % (lv + 1), "S%d" % (lv + 1) if lv < 3 else "fs%d" % c
-            ga, gb, sa, sbb = bi[:, a:a + 2 * n:2], bi[:, a + 1:a + 2 * n:2], sb[lv][:, 0::2], sb[lv][:, 1::2]
-            tmp = T.TV[:, 256:256 + n]
-            out += [tt(T.p1[:, 0:n], gb, sa, OP.mult, [ki, G, S], ["p1"]), tt(tmp, ga, sbb, OP.mult, [ki, "TV", G, S], ["tmp"]),
-                    tt(T.cc[:, 0:n], T.p1[:, 0:n], tmp, OP.is_gt, ["p1", "TV", "tmp"], ["cc"]),
-                    tt(T.cgk[:, 0:n], T.cc[:, 0:n], gb, OP.mult, ["cc", ki, G], ["cg1"]),
-                    tt(tmp, T.cc[:, 0:n], sbb if lv else gs[:, 257:512:2], OP.mult, ["cc", S, "TV", bk], ["tmp"])]
-            if lv == 0:
-                out += [tt(bo[:, a2 + n:a2 + 2 * n], T.cc[:], T.TV[:, 384:512], OP.add, ["cc", "kc", "TV", ko], [G2 + "k"]),
-                        tt(bo[:, a2:a2 + n], ga, T.cgk[:, 0:n], OP.max, [ki, ko, G, "cg1"], [G2])]
-            else:
-                out += [tt(T.cgk[:, n:2 * n], T.cc[:, 0:n], bi[:, a + 2 * n + 1:a + 4 * n:2], OP.mult, ["cc", ki, G, G + "k"], ["cg2"]),
-                        tt(bo[:, a2:a2 + 2 * n], bi[:, a:a + 4 * n:2], T.cgk[:, 0:2 * n], OP.max, [G, G + "k", "TV", ki, "cg1", "cg2"],
-                           [G2] if lv < 3 else [ko])]
-            out.append(tt(ss[lv + 1], sa, tmp, OP.max if lv else OP.add, [S, "TV", "tmp"], [S2]))
-        return out
-
-    def send_gs(t, c):
-        return send(t, c, "g", T["RG%d%d" % (t, c)][:], T.fin[:, 48 * c:48 * c + 32], ["fin%d" % c, "fs%d" % c], "RG%d%d" % (t, c))
-
-    def turn(qb, qk, src, a, sk, out, r, rk, n, ok):
-        return [act(qb[:, 14 + b:142:16], src[:, a + b:a + 16:2], AF.Copy, [sk, qk], [qk + str(b)]) for b in range(2)] \
-            + [mm(out, qb[:, 14 - 2 * j:142 - 2 * j], r[:, n * j:n * j + n], False, j == 7, [qk + "0", qk + "1", rk], ["LL", ok]) for j in range(8)]
-
-    def place(c):
-        return [mm(T.LL[:, 0:16], T.idf[:], T.co[:, 96:112], True, False, ["idf", "co6"], ["LL", "ly"])] \
-            + ([tt(T.zz[:], T.fin[:, 80:96].indirect(T.zo[:]), T.zm[:], OP.mult, ["fin1", "zo", "zm"], ["zz"]),
-                mm(T.LL[:, 0:16], T.zz[:], T.ro[:, 96:112], False, True, ["zz", "ro6"], ["LL", "ly"])] if c else
-               turn(T.qa, "qa", T.fin, 32, "fin0", T.LL[:, 0:16], T.r8, "r8", 16, "ly")), \
-               [cp(T.oy[:, 16 * c:16 * c + 16], T.LL[:, 0:16], ["LL", "ly"], ["oy%d" % c])]
+            n, w = 128 >> lv, min(lv, 1) + 1
+            every, a, b = slice(w - 1, 2 * n * w, w), slice(w - 1, 2 * n * w, 2 * w), slice(2 * w - 1, 2 * n * w, 2 * w)
+            h, k, r = (T.h0, T.h1, T.h2, T.h3)[lv], (T.kc, T.k1, T.k2, T.k3)[lv], lv % 2
+            d, last, tmp, hk, sk = T.dd[:, 0:2 * n], lv == 3, s[:, 1 - r, 128:128 + n], "H%d" % lv, "s%d" % lv
+            out += [tt(T.pp[:, 0:n], h[:, b], s[:, r, a], OP.mult, [hk, bk, sk], ["pp"]),
+                    tt(tmp, h[:, a], s[:, r, b], OP.mult, [hk, bk, sk], ["tmp"]),
+                    tt(T.dd[:, 1:2 * n:2], T.pp[:, 0:n], tmp, OP.subtract, ["pp", "tmp", bk], ["dd"]),
+                    scan(So[lv], d, s[:, r, every], OP.max, OP.min, ["dd", bk, sk], ["fs%d" % c if last else "s%d" % (lv + 1)]),
+                    scan(Ho[lv], d, h[:, every], OP.max, OP.min, ["dd", hk], ["fh%d" % c if last else "H%d" % (lv + 1)]),
+                    scan(Ko[lv], d, k[:, every], OP.max, OP.min, ["dd", "kc", "K%d" % lv], ["kb%d" % c if last else "K%d" % (lv + 1)], 0.5)]
+        return out + send(t, c, "g", T["RG%d%d" % (t, c)][:], T.fin[:, c], ["fs%d" % c, "fh%d" % c], "RG%d%d" % (t, c), 32)
 
     def profile(t, c):
         k = "y%d" % c
-        return [act(T.yy[:, ln(c)], T.pg[:, 4096 * c:4096 * (c + 1)].indirect(T.oy[:, 16 * c:16 * c + 16]), AF.Copy,
-                    ["pg%d_%d" % (2 * c + i // 8, i % 8) for i in range(16)] + ["oy%d" % c], [k])] \
-            + send(t, c, "y", T["RY%d%d" % (t, c)][:], T.yy[:, ln(c)], [k], "RY%d%d" % (t, c)) \
-            + [mm(T.DZ[:, 256:512], T.idb[:], T.vv[:, ln(c)], True, False, ["idb", "v%d" % c], ["DZ"]),
+        return [mm(T.LL[:, 0:16], T.idf[:], T.cy[:], True, False, ["idf", "cy"], ["LL"], 4)] \
+            + [cp(T.sb[:, 3, 14 + b:142:16], T.k4[:, c, 16 * b + 1:16 * b + 16:2], ["kb%d" % c], ["sb3%d" % b]) for b in range(2)] \
+            + [mm(T.LL[:, 0:16], T.sb[:, 3, 14 - 2 * j:142 - 2 * j], T.r8[:, 16 * j:16 * j + 16], False, j == 7, ["sb30", "sb31", "r8"], ["LL"]) for j in range(8)] \
+            + [cp(T.oy[:, 16 * c:16 * c + 16], T.LL[:, 0:16], ["LL"], ["oy%d" % c]),
+               act(T.yy[:, ln(c)], T.pg[:, 4096 * c:4096 * (c + 1)].indirect(T.oy[:, 16 * c:16 * c + 16]), AF.Copy,
+                   ["pg%d" % i for i in range(8 * c, 8 * c + 8)] + ["oy%d" % c], [k], r=GATHER)] \
+            + send(t, c, "y", T["RY%d%d" % (t, c)][:], T.yy[:, ln(c)], [k], "RY%d%d" % (t, c), 64) \
+            + [mm(T.DZ[:, 256:512], T.idb[:], T.vv[:, ln(c)], True, False, ["idb", "vv"], ["DZ"]),
                mm(T.DZ[:, 256:512], T.idb[:], T.yy[:, ln(c)], False, True, [k], ["DZ"]),
-               mm(T.DZ[:, 0:256], T.idb[:], T.z[:, ln(c)], True, False, ["z%d" % c], ["DZ"]),
-               mm(T.DZ[:, 0:256], T.idn[:], T.yy[:, ln(c)], False, True, ["idn", k], ["DZ"])]
+               mm(T.DZ[:, 0:256], idx(2), T.z[:, ln(c)], True, False, ["id2", "z%d" % c], ["DZ"]),
+               mm(T.DZ[:, 0:256], idx(-2), T.yy[:, ln(c)], False, True, ["id-2", k], ["DZ"]),
+               act(T.cz[:, c, 256:768], T.DZ[:], AF.Identity, ["DZ"], ["nv%d" % c], 191.75, 0.5)]
 
-    def winner(c):
-        return [act(T.nv[:, ln(c)], T.DZ[:, 256:512], AF.Identity, ["DZ"], ["nv%d" % c], 191.75, 0.5),
-                act(T.t1[:, ln(c)], T.DZ[:, 0:256], AF.Abs, ["DZ"], ["t1%d" % c]),
-                act(T.cz[:, CW[c]:CW[c] + 256], T.t1[:, ln(c)], AF.Relu, ["t1%d" % c], ["cw%d" % c], -1.0)]
-
-    def loser(t, c):
-        return [mm(T.SR[:, 0:256], T.idb[:], T.z[:, ln(c)], True, False, ["z%d" % c], ["SR"]),
-                mm(T.SR[:, 0:256], T.idb[:], T["RY%d%d" % (t, c)][:], False, True, ["RY%d%d" % (t, c)], ["SR"]),
-                act(T.t2[:, ln(c)], T.SR[:, 0:256], AF.Identity, ["SR"], ["t2%d" % c], 191.75, 0.5),
-                act(T.cz[:, CL[c]:CL[c] + 256], T.t2[:, ln(c)], AF.Relu, ["t2%d" % c], ["cl%d" % c], -193.0)]
-
-    def cols():
-        out = [mm(T.LL[:, 64:96], T.qw[:, 15 - a:143 - a], T.z[:, a::16], a == 0, a == 15, ["qw", "z0", "z1"], ["LL", "rl"]) for a in range(16)]
-        return out, [cp(T.ri[:], T.LL[:, 64:96], ["LL", "rl"], ["ri"]), ts(T.ri[:], T.ri[:], 7, OP.bitwise_and, ["ri"], ["ri"]),
-                     tt(T.cm[:, 32:64], T.ri[:], T.c8[:], OP.add, ["ri", "c80", "c81"], ["cm2", "cm3"]),
-                     cp(T.cu[:], T.cm[:, 32:64], ["cm2", "cm3"], ["cu"])]
-
-    def old(c):
-        return [act(T.vv[:, ln(c)], XW[c].indirect(T.cu[:, 16 * c:16 * c + 16]), AF.Copy, [XK[c], "Xl", "cu"], ["v%d" % c])]
+    def columns():
+        return [mm(T.LL[:, 64:96], T.qw[:, 15 - a:143 - a], T.z[:, a::16], a == 0, a == 15, ["qw", "z0", "z1"], ["LL"]) for a in range(16)] \
+            + [cp(T.ri[:], T.LL[:, 64:96], ["LL"], ["ri"]), ts(T.ri[:], T.ri[:], 7, OP.bitwise_and, ["ri"], ["ri"]),
+               tt(T.cm[:, 1::4, :], T.ri[:], T.c8[:], OP.add, ["ri", "c80", "c81"], ["cm1", "cm5"], 2),
+               cp(T.cu[:, 0:32], T.cm[:, 1::4, :], ["cm1", "cm5"], ["cu"]),
+               act(T.vv[:], REC.indirect(T.cu[:, 0:32]), AF.Copy, XK + ["cu"], ["vv"], r=GATHER)]
 
     def meet(t, c):
-        f, r, k = 48 * c, T["RG%d%d" % (t, c)], "RG%d%d" % (t, c)
-        j3 = range(3 * c, 3 * c + 3)
-        return [mm(T.LL[:, 16:64], T.idf[:], T.co[:, f:f + 48], True, False, ["idf"] + ["co%d" % j for j in j3], ["LL", "lo"]),
-                tt(T.wa[:, 0:16], T.fin[:, f + 16:f + 32], r[:, 0:16], OP.mult, ["fin%d" % c, k], ["wa0"]),
-                tt(T.wa[:, 16:32], T.fin[:, f:f + 16], r[:, 16:32], OP.mult, ["fs%d" % c, k], ["wa1"]),
-                tt(T.wa[:, 32:48], T.wa[:, 0:16], T.wa[:, 16:32], OP.is_ge if rank < (rank ^ STEPS[t]) else OP.is_gt, ["wa0", "wa1"], ["wa2"]),
-                tt(T.sig[:, 16 * c:16 * c + 16], T.wa[:, 32:48], T.fin[:, f + 32:f + 48], OP.mult, ["wa2", "fin%d" % c], ["sg%d" % c])] \
-            + ([tt(T.zz[:], T.sig[:, 16 * c:16 * c + 16].indirect(T.zo[:]), T.zm[:], OP.mult, ["sg%d" % c, "zo", "zm"], ["zz"]),
-                mm(T.LL[:, 16:64], T.zz[:], T.ro[:, f:f + 48], False, True, ["zz"] + ["ro%d" % j for j in j3], ["LL", "lo"])] if c else
-               turn(T.qb, "qb", T.sig, 0, "sg0", T.LL[:, 16:64], T.ro8, "ro8", 48, "lo")), \
-               [tt(T.of[:], T.LL[:, 16:64], T.cm[:, f:f + 48], OP.max if c else OP.min, ["LL", "lo"] + ["cm%d" % j for j in j3], ["of"]),
-                cp(T.ou[:, f:f + 48], T.of[:], ["of"], ["ou%d" % c])]
+        r, k, f = T["RG%d%d" % (t, c)], "RG%d%d" % (t, c), 48 * c
+        out = [mm(T.LL[:, 32:64], T.idf[:], T.cm[:, 3 * c + 1:3 * c + 3, :], True, False, ["idf"] + ["cm%d" % j for j in (1, 2, 4, 5)], ["LL"], 4),
+               mm(T.Z1[:, 0:16], T.idf[:], T.cm[:, 0, :], True, False, ["idf", "cm0"], ["Z1"], 4)]
+        if t == 2 and c:
+            out.append(mm(T.LL[:, 48:64], T.idf[:], T.adj[:], False, False, ["adj"], ["LL"], 4))
+        out += [tt(T.wa[:], T.fin[:, c, :, 1::2], r[:, ::-1, 1::2], OP.mult, ["fs%d" % c, "fh%d" % c, k], ["wa"], 2)]
+        out += [tt(T.sb[:, 2, 14 + b:142:16], T.wa[:, 16 + 8 * b:24 + 8 * b], T.wa[:, 8 * b:8 * b + 8], OP.is_ge if rank < (rank ^ STEPS[t]) else OP.is_gt,
+                   ["wa"], ["sb2%d" % b], 2) for b in range(2)]
+        out += [tt(T.sb[:, c, 14 + b:142:16], T.sb[:, 2, 14 + b:142:16], T.k4[:, c, 16 * b + 1:16 * b + 16:2], OP.mult, ["sb2%d" % b, "kb%d" % c],
+                   ["sb%d%d" % (c, b)], 2) for b in range(2)]
+        sig = ["sb%d0" % c, "sb%d1" % c]
+        out += [mm(T.LL[:, 32:64], T.sb[:, 2, 14 - 2 * j:142 - 2 * j], T.ro[:, 48 * j + 16 * c:48 * j + 16 * c + 32], False, j == 7,
+                   ["sb20", "sb21", "ro"], ["LL"]) for j in range(8)] + [cp(T.ou[:, f + 16:f + 48], T.LL[:, 32:64], ["LL"], ["ou%d" % c])]
+        out += [mm(T.Z1[:, 0:16], T.sb[:, c, 14 - 2 * j:142 - 2 * j], T.ro[:, 48 * j + 16:48 * j + 32], False, j == 7,
+                   sig + ["ro"], ["Z1"]) for j in range(8)] + [cp(T.ou[:, f:f + 16], T.Z1[:, 0:16], ["Z1"], ["oj%d" % c])]
+        if t < 2:
+            out += [mm(T.HH[:, 1, 0, 0, 8 * c:8 * c + 8], T.o32[:], T.sb[:, c, 14 + b:142:16], b == 0, b == 1, ["o32"] + sig, ["HH"]) for b in range(2)]
+            if c:
+                out.append(vec(lambda q: q.tensor_reduce(T.a32[:], T.HH[:, 1, 0, 0, :], AX.X, OP.add), 16, ["HH"], ["a32"]))
+        return out
 
-    def scatter(t, c):
-        if t == 2:
-            return [tt(T.yo[:, 256 * c:256 * c + 2304].indirect(T.ou[:, OS[c]:OS[c] + 16]), T.t2[:, 256:512] if c else T.nv[:, 0:256], T.yv[:, ln(c)], OP.add,
-                       ["n16" if c else "nv0", "t21", "e%d" % c, "ou%d" % c, "Y0", "Y1", "Y2", "Y3", "Yd"], ["Y"])]
-        return [tt(XW[c].indirect(T.ou[:, OS[c]:OS[c] + 16]), T.nv[:, ln(c)], T.m192[:], OP.add, ["nv%d" % c, "m192", "ou%d" % c], [XK[c]])]
+    def scatter(c):
+        win = T.X[:, SP + 2048:SP + 6144] if c else T.X[:, 0:SP + 2048]
+        return [tt(win.indirect(T.ou[:, OS[c]:OS[c] + 16]), T.cz[:, c, 512:768], T.m192[:], OP.add, ["nv%d" % c, "m192", "ou%d" % c], [XK[c]], SCATTER)]
 
     def demand(t, c):
-        out = [act(T.z[:, ln(c)], T.cz[:, 512 * c:512 * c + 512].indirect(T.ou[:, OZ[c]:OZ[c] + 16]), AF.Identity,
-                   ["cw%d" % c, "cl%d" % c, "ou%d" % c], ["z%d" % c], 1.0)]
-        return out + (prep1(c) if t < 2 else [dma("y", T.yz[:, ln(c)], T.z[:, ln(c)], ["z%d" % c], [], "sz%d" % c)])
+        out = [mm(T.S0[:, 0], T.idb[:], T.z[:, ln(c)], True, False, ["z%d" % c], ["S0"]),
+               mm(T.S0[:, 0], T.idb[:], T["RY%d%d" % (t, c)][:], False, True, ["RY%d%d" % (t, c)], ["S0"]),
+               act(T.cz[:, c, 0:256], T.S0[:, 0], AF.Identity, ["S0"], ["cl%d" % c], 191.75, 0.5),
+               act(T.za[:, ln(c)], T.cz[:, c, 0:512].indirect(T.ou[:, OZ[c]:OZ[c] + 16]), AF.Abs,
+                   ["nv%d" % c, "cl%d" % c, "ou%d" % c], ["za%d" % c], -192.0, r=GATHER),
+               ts(T.z[:, ln(c)], T.za[:, ln(c)], 1.0, OP.max, ["za%d" % c], ["z%d" % c], r=0.5)]
+        return out + (factor(c) if t < 2 else [dma("y", T.yz[:, ln(c)], T.z[:, ln(c)], ["z%d" % c], [], "sz%d" % c, 64)])
 
     def names(t, c):
         k = "%d%d" % (t, c)
-        src, rd = W(t, c)[:].indirect(T.ou[:, OJ[c]:OJ[c] + 16]), ["J" + k, "Jr" + k, "Wt" + k, "ou%d" % c]
+        src, rd = W(t, c)[:].indirect(T.ou[:, OJ[c]:OJ[c] + 16]), ["J" + k, "Jr" + k, "Wt" + k, "oj%d" % c]
         if t < 2:
-            return [act(W(t + 1, c)[:, 0:256], src, AF.Copy, rd, ["J%d%d" % (t + 1, c)])] + tables(t + 1, c)
-        return [act(T.jo[:, ln(c)], src, AF.Copy, rd, ["jo%d" % c]), dma("y", T.yj[:, ln(c)], T.jo[:, ln(c)], ["jo%d" % c], [], "sj%d" % c)]
+            return [act(W(t + 1, c)[:, 0:256], src, AF.Copy, rd, ["J%d%d" % (t + 1, c)], r=GATHER)]
+        return [act(T.jo[:, ln(c)], src, AF.Copy, rd, ["jo%d" % c], r=GATHER), dma("y", T.yj[:, ln(c)], T.jo[:, ln(c)], ["jo%d" % c], [], "sj%d" % c, 128)]
 
-    def count():
-        return [o("v", lambda e: e.tensor_reduce(T.a1[:], T.sig[:], AX.X, OP.add), ["sg0", "sg1"], ["a1"]),
-                mm(T.LL[:, 128:129], T.o32[:], T.a1[:], True, True, ["o32", "a1"], ["LL", "acol"])]
+    def output(c):
+        if c == 0:
+            return [ts(T.yo[:, SP:SP + 2048], T.X[:, SP + 2048:SP + 4096], 16.0, OP.mult, XK, ["Yp"], r=0.5),
+                    o("g", lambda q: q.dma_start(T.yo[:, SP:SP + 2048], T.X[:, SP:SP + 2048], accum_op=OP.add), XK + ["Yp"], ["Yp"],
+                      1000.0, 3000.0, ("pk", 16)),
+                    act(T.yv[:, 0:256], T.X[:, SP + 2048:SP + 4096].indirect(T.cu[:, 0:16]), AF.Identity, XK + ["cu"], ["e0"], -192.0, 16.0, GATHER),
+                   tt(T.yo[:, 0:SP + 2048].indirect(T.ou[:, OS[0]:OS[0] + 16]), T.cz[:, 0, 512:768], T.yv[:, 0:256], OP.add,
+                      ["nv0", "e0", "ou0", "Yp"], ["Y"], SCATTER)]
+        out = [ts(T.cu[:, 32:48], T.cm[:, 5, :], -2048.0, OP.add, ["cm5"], ["cu2"]),
+               act(T.nb[:, 0:256], T.yo[:, SP:SP + 2048].indirect(T.cu[:, 32:48]), AF.Copy, ["Y", "Yb", "cu2"], ["nb0"], r=GATHER),
+               mm(T.UU[:, 0:256], T.idb[:], T.nb[:, 0:256], True, False, ["nb0"], ["UU"]),
+               mm(T.UU[:, 0:256], idx(-16), T.vv[:, 256:512], False, False, ["vv", "id-16"], ["UU"]),
+               mm(T.UU[:, 0:256], idx(16), T.cz[:, 1, 512:768], False, True, ["nv1"], ["UU"]),
+               act(T.yv[:, 256:512], T.UU[:, 0:256], AF.Identity, ["UU"], ["e1"], -3072.0)]
+        for h in range(2):
+            out += [cp(T.yo[:, SP + 1024 * h:SP + 4096].indirect(T.ou[:, OS[1] + 8 * h:OS[1] + 8 * h + 8]), T.yv[:, 256 + 128 * h:384 + 128 * h],
+                       ["e1", "ou1", "Y"], ["Yb"] + ["Yh%d" % j for j in range(h, 2)], SCATTER * 128),
+                    dma("y" if h else "s", T.yx[:, 1024 * h:1024 * h + 1024], T.yo[:, SP + 1024 * h:SP + 1024 * h + 1024], ["Yh%d" % h], [], "sy%d" % h, 256)]
+        return out
 
-    def packed(j, bk):
-        return [mm(T[bk][:], T.idb[:], T.X[:, 256 + 512 * j:768 + 512 * j], True, False, ["X0", "Xl"], [bk]),
-                mm(T[bk][:], T.id16[:], T.X[:, 2304 + 512 * j:2816 + 512 * j], False, True, ["X1", "Xl", "id16"], [bk]),
-                act(T.yo[:, 256 + 512 * j:768 + 512 * j], T[bk][:], AF.Copy, [bk], ["Y%d" % j])]
-
-    def rest0():
-        return [act(T.yv[:, 0:256], T.X[:, 2048:4352].indirect(T.cu[:, 0:16]), AF.Identity, XK + ["Xl", "cu"], ["e0"], -192.0, 16.0)]
-
-    def rest1():
-        return [act(T.nb[:, 0:256], T.yo[:, 256:2560].indirect(T.cu[:, 16:32]), AF.Copy, ["Y", "Yb", "cu"], ["nb0"]),
-                mm(T.SR[:, 256:512], T.id16[:], T.vv[:, 256:512], True, False, ["v1"], ["SR"]),
-                mm(T.SR[:, 256:512], T.idn[:], T.nb[:, 0:256], False, True, ["nb0"], ["SR"]),
-                act(T.yv[:, 256:512], T.SR[:, 256:512], AF.Identity, ["SR"], ["e1"], 0.0, -1.0)]
-
-    ops += prep1(0) + prep2(0)
-    ops += [cp(W(0, c)[:, 0:256], T.ji[:, ln(c)], ["ji"], ["J0%d" % c]) for c in range(2)]
-    ops += tables(0, 0) + prep1(1) + prep2(1) + late[:12] + prod(0, 0) + weave(hops(0, 0, 128), late[12:20]) + tables(0, 1) + late[20:34]
-    late = late[34:] + [ms(T.qa[:], 0.0, ["qa"]), ms(T.qb[:], 0.0, ["qb"])]
-    ops += [asel(T.r8[:], T.one[:, 0:128], [[-1, 8], [-8, 16]], OP.is_equal, 0, 1, ["one"], ["r8"]),
-            o("g", lambda q: q.iota(T.ro8[:], [[0, 8], [8192, 3], [0, 16]], 256, 0, allow_small_or_imprecise_dtypes=True), [], ["ro8"]),
-            asel(T.ro8[:], T.ro8[:], [[-1, 8], [0, 3], [-8, 16]], OP.is_equal, 0, 1, ["ro8"], ["ro8"])]
-
+    setup = len(ops)
+    ops += [cp(W(0, c)[:, 0:256], T.ji[:, ln(c)], ["ji%d" % c], ["J0%d" % c]) for c in range(2)] + tables(0, 0) + tables(0, 1)
+    ops += factor(0) + prod(0, 0) + factor(1)
     for t in range(3):
-        ops += pick("s", 0, 64) + pick("v", 64, 64)
-        if t > 0:
-            ops += prep2(1) + pick("s", 128, 128)
-        else:
-            ops += late + pick("s", 128, 128)
-        c1, c2 = cols()
-        ops += sums_x(0) + mins_sums(0) + weave(prod(t, 1) + hops(t, 1, 256), pscan(0, 4)) + c1
-        ops += pick("s", 256, 128) + pick("s", 384, 128)
-        ops += sums_x(1) + mins_sums(1) + weave(c2, pscan(1, 4)) + old(0) + old(1) + sums_x(2)
-        a1, a2 = place(0)
-        if t == 2:
-            ops += packed(0, "ZU0") + packed(1, "DZ") + packed(2, "SR") + rest0()
-        b = mins_sums(2)
-        ops += stages(search(0), [b[2 * j:2 * j + 2] + (sums_x(3) if j == 10 else []) for j in range(16)]) + send_gs(t, 0) + a1
-        b = mins_sums(3)
-        ops += b[:16] + a2 + profile(t, 0)[:3] + b[16:] + profile(t, 0)[3:] + winner(0) + (packed(3, "ZU0") if t == 2 else [])
-        a1, a2 = place(1)
-        m1, m2 = meet(t, 0)
-        p2 = [[x] for x in pscan(2, 8) + pscan(3, 8)]
-        after = loser(t, 0) + demand(t, 0) + (prep2(0) if t < 2 else []) + names(t, 0)[:1 if t < 2 else 2]
-        ops += p2[0] + stages(search(1), [p2[1], m1[:3], m1[3:4], m1[4:]] + p2[2:8] + [m2[:1], m2[1:] + after] + p2[8:12])
-        ops += send_gs(t, 1) + a1
-        p3 = pscan(3, 2)[1:]
-        m1, m2 = meet(t, 1)
-        if t < 2:
-            h = hops(t + 1, 0, 128)
-            pr = prod(t + 1, 0)
-            ops += p3 + a2 + profile(t, 1) + tables(t + 1, 0) + winner(1) + scatter(t, 0)
-            ops += m1[:3] + pr[:1] + m1[3:4] + pr[1:] + m1[4:] + count() + m2[:1] + h[:1] + m2[1:] + names(t, 1) + loser(t, 1) + demand(t, 1)
-            ops += [h[2]] + scatter(t, 1) + [h[4], h[1], h[3], h[5]]
-        else:
-            ops += p3 + a2 + scatter(t, 0) + profile(t, 1) + rest1()[:3] + winner(1)[:1]
-            ops += [act(T.t2[:, 256:512], T.nv[:, 256:512], AF.Identity, ["nv1"], ["n16", "t21"], -3072.0, 16.0)] + rest1()[3:]
-            ops += m1 + winner(1)[1:] + m2 + [ts(T.oy[:, 0:8], T.of[:, 8:16], -1024.0, OP.add, ["of"], ["oy0"])]
-            for h in range(2):
-                off = T.oy[:, 0:8] if h else T.ou[:, 48:56]
-                ops += [tt(T.yo[:, 256 + 1024 * h:2560].indirect(off), T.t2[:, 256 + 128 * h:384 + 128 * h], T.yv[:, 256 + 128 * h:384 + 128 * h], OP.add,
-                           ["n16", "t21", "e1", "ou1", "oy0", "Y"], ["Yb"] + ["Yh%d" % j for j in range(h, 2)]),
-                        dma("y" if h else "s", T.yx[:, 1024 * h:1024 * h + 1024], T.yo[:, 256 + 1024 * h:1280 + 1024 * h], ["Yh%d" % h], [], "sy%d" % h)]
-            ops += names(t, 1)
-            ops += loser(t, 1) + demand(t, 1)
-    emit(g, T, ops)
+        ops += hops(t, 0, 128) + (demand(t - 1, 1) if t else []) + quarter(0) + prod(t, 1) + hops(t, 1, 256) + columns() + quarter(1)
+        ops += search(t, 0) + quarter(2) + quarter(3) + profile(t, 0) + meet(t, 0) + names(t, 0) + demand(t, 0)
+        ops += (scatter(0) + prod(t + 1, 0) if t < 2 else output(0))
+        ops += search(t, 1) + profile(t, 1) + meet(t, 1) + names(t, 1)
+        ops += scatter(1) + tables(t + 1, 0) + tables(t + 1, 1) if t < 2 else output(1) + demand(t, 1)
+    scalar = scalar_line(0) + scalar_line(1) + scalar_line(2)
+    vector = "pi0 pi1 pi0 pi1 hu0 hu1".split() + vector_line(0) + vector_line(1) + vector_line(2)
+    emit(g, T, order(ops, setup, {"s": scalar, "y": ["z0", "Xl", "ji1"], "v": vector}))

@@ -1,16 +1,22 @@
+from concourse.bass import DstId, RemoteDMATransfer
 from concourse.mybir import AluOpType as OP, AxisListType as AX, ActivationFunctionType as AF
 
 STEPS = (5, 2, 7)
 F, B, I, U = "float32", "bfloat16", "int32", "uint16"
 SP = 2560
 BIG = 4096.0
-SHARED = (3,)
-VPICK = (1,)
-GATHER, SCATTER = 2.0, 3.8
+LIFT = 1.0 / 16
+SCAN = (1, 3)
+HELP = False
+ZS = 3
+PARTS = 4
+PW = 512
+VPICK = (64, 64, 64)
 
 SCRATCH = {
     "X": ("sbuf", [128, SP + 6144], B), "yo": ("sbuf", [128, SP + 4096], B),
     "xg": ("sbuf", [128, 8192], B), "mg": ("sbuf", [128, 8192], B), "pg": ("sbuf", [128, 8192], B),
+    "m0": ("sbuf", [128, 384], B), "zl": ("sbuf", [128, 3, 128], B), "zr": ("sbuf", [128, 6144], B), "rw": ("sbuf", [128, 3, 8, 32], B),
     "ji": ("sbuf", [128, 512], I), "z": ("sbuf", [128, 512], B), "za": ("sbuf", [128, 512], B), "w": ("sbuf", [128, 1], F),
     "jo": ("sbuf", [128, 512], F), "pi": ("sbuf", [128, 512], I), "hu": ("sbuf", [128, 512], U),
     "yy": ("sbuf", [128, 512], B), "vv": ("sbuf", [128, 512], B), "nb": ("sbuf", [128, 512], B),
@@ -18,62 +24,72 @@ SCRATCH = {
     "h0": ("sbuf", [128, 256], F), "h1": ("sbuf", [128, 256], F), "h2": ("sbuf", [128, 128], F), "h3": ("sbuf", [128, 64], F),
     "k1": ("sbuf", [128, 256], B), "k2": ("sbuf", [128, 128], B), "k3": ("sbuf", [128, 64], B),
     "pp": ("sbuf", [128, 128], F), "dd": ("sbuf", [128, 256], B), "fin": ("sbuf", [128, 2, 2, 32], F), "wa": ("sbuf", [128, 32], F),
-    "k4": ("sbuf", [128, 2, 32], B), "sb": ("sbuf", [128, 4, 144], B),
+    "four": ("sbuf", [128, 2, 64], F), "wb": ("sbuf", [128, 2, 80], F), "fl": ("sbuf", [128, 80], B), "ks": ("sbuf", [128, 80], B), "wk": ("sbuf", [128, 80], B),
+    "k4": ("sbuf", [128, 2, 32], B), "sb": ("sbuf", [128, 4, 71, 2], B),
     "oy": ("sbuf", [128, 32], U), "ou": ("sbuf", [128, 96], U), "ri": ("sbuf", [128, 32], I), "cu": ("sbuf", [128, 48], U),
     "one": ("sbuf", [128, 256], B), "idb": ("sbuf", [128, 128], B), "ids": ("sbuf", [128, 6, 128], B),
     "idf": ("sbuf", [128, 128], F), "o32": ("sbuf", [128, 128], B),
-    "bd": ("sbuf", [128, 128], B), "bd4": ("sbuf", [128, 8, 16], B), "f4": ("sbuf", [128, 128], B), "kc": ("sbuf", [128, 256], B),
-    "zq": ("sbuf", [128, 128], B), "bdw": ("sbuf", [128, 128], B), "bdw2": ("sbuf", [128, 128], B), "qw": ("sbuf", [128, 144], B),
-    "cst": ("sbuf", [128, 128], B), "mp": ("sbuf", [128, 1024], B), "m192": ("sbuf", [128, 256], B),
-    "r8": ("sbuf", [128, 128], B), "ro": ("sbuf", [128, 384], B), "cm": ("sbuf", [128, 6, 16], F), "cy": ("sbuf", [128, 16], F),
+    "bd": ("sbuf", [128, 128], B), "bd4": ("sbuf", [128, 2, 8, 16], B), "f4": ("sbuf", [128, 128], B), "kc": ("sbuf", [128, 256], B),
+    "bdw": ("sbuf", [128, 128], B), "bdw2": ("sbuf", [128, 128], B), "qw": ("sbuf", [128, 144], B),
+    "cst": ("sbuf", [128, 128], B), "mp": ("sbuf", [128, PW], B), "mr": ("sbuf", [128, PW], B), "m192": ("sbuf", [128, 128], B),
+    "r8": ("sbuf", [128, 128], B), "ro": ("sbuf", [128, 8, 3, 16], B), "cm": ("sbuf", [128, 6, 16], F), "cy": ("sbuf", [128, 16], F),
     "c8": ("sbuf", [128, 32], F), "adj": ("sbuf", [128, 16], F), "i3": ("sbuf", [128, 16], I), "i4": ("sbuf", [128, 2], I),
     "pc": ("sbuf", [128, 2], F), "a1": ("sbuf", [128, 1], F), "a32": ("sbuf", [128, 1], F),
     "Z0": ("psum", [128, 512], F), "Z1": ("psum", [128, 512], F), "S0": ("psum", [128, 2, 256], F), "S1": ("psum", [128, 2, 256], F),
-    "HH": ("psum", [128, 2, 2, 8, 16], F), "UU": ("psum", [128, 512], F), "DZ": ("psum", [128, 512], F), "LL": ("psum", [128, 512], F),
+    "HH": ("psum", [128, 2, 8, 32], F), "UU": ("psum", [128, 512], F), "DZ": ("psum", [128, 512], F), "LL": ("psum", [128, 512], F),
 }
-SEMAPHORES = ["cv", "cs", "cp", "cg", "ldx", "pk", "ldj", "ldk", "ldz", "ldw", "sy0", "sy1", "sj0", "sj1", "sz0", "sz1"]
+SEMAPHORES = ["cv", "cs", "cp", "cg", "ldx", "ldj", "ldz", "ldw", "sy0", "sy1", "sj0", "sj1", "sz0", "sz1", "lt"]
 for _t in range(3):
     for _c in range(2):
         SCRATCH["W%d%d" % (_t, _c)] = ("sbuf", [128, 17 * 256], F)
         SCRATCH["D%d%d" % (_t, _c)] = ("dram", [8, 32, 256], F)
-        SCRATCH["RG%d%d" % (_t, _c)] = ("sbuf", [128, 2, 32], F)
+        SCRATCH["RG%d%d" % (_t, _c)] = ("sbuf", [128, 2, 32 + 32 * _c], F)
         SCRATCH["RY%d%d" % (_t, _c)] = ("sbuf", [128, 256], B)
-        for _k in ("aj", "ag", "ay", "lj", "lg", "ly", "do", "dr", "dt"):
+        for _k in ("aj", "ao", "ag", "ay", "lj", "lg", "ly", "do", "dt"):
             SEMAPHORES.append("%s%d%d" % (_k, _t, _c))
+    SEMAPHORES += ["dp%d%d" % (_t, _p) for _p in range(PARTS)]
 BANKS = ("Z0", "Z1", "S0", "S1", "HH", "UU", "DZ", "LL")
 ESEM = {"v": "cv", "s": "cs", "p": "cp", "g": "cg"}
-IDS = (-1.0, 16.0, -16.0, -2048.0, 2.0, -2.0)
-WAKE, FILL, AHEAD = 100.0, 200.0, {"v": 150.0, "s": 400.0, "p": 100.0, "g": 300.0, "y": 0.0}
+IDS = (16.0, -16.0, -2048.0, 2.0, -2.0, -1.0)
+
+HEAD = {
+    "v": "one cst0 zz qw i4a mr mp mr i4b bdw cst1 bd5 zl1 bd4 bdw2 id-2048 rw mr qw J0 pc mp zl3 pi0 pi1 pi0 cm0 rw1 hu0 pi1 J1 c80 rw0 id-1 "
+         "pi2 pi3 hu1 c81 pi2 f4 rw2 ri hu2 ri",
+    "s": "w ji nb0 zs nb1 zs zs",
+    "p": "us0 uc0 us1 uz0 uq0 rq1 uc1 uz1 uq1 col ig0 ih0 rq0",
+    "g": "i4 bd bd idb kc i3 sj0 zr0 zr0 zr0 sj1 " + "zr0 " * 9,
+    "y": "z0 Xl",
+}
+ROUND = {
+    "v": "pi1:12 idf:0 pi1:12 z1:12 hu1:12 x1 u00 sb0:0 ri:12 zl3:12 pi2:12 id2:0 u10 a1:0 pi3:12 u01 pi2:12 id-2:0 pg3 pi2:12 u11 hu2:12 "
+         "n2 pg2 m3 m2 f2 pg0 pg5 pg4 pg6 ro2:0 cy:0 G0 pg8:01 ri:12 dd:0 "
+         "pp tmp pg1 ro0:0 dd cm1 ro1:0 adj:0 H1 G1 K1 m20 m192:0 pp tmp m21 dd m22 H2 G2 m23 n6 pp tmp K2 pg10:2 m6 dd f6 n7 G3 H3 f7 m7 K3 "
+         "pp tmp pg7 dd cu cm4:0 kb0 pg9:2 pg12:01 sb3 G0 fh0 fg0 "
+         "pp tmp oy0 id-16:0 cu2:2 dd wz:0 pg8:2 kz:0 G1 H1 K1 pp tmp pg11:01 pg12:2 dd pg15 G2 H2 K2 cg pp tmp wa ch dd cm2:0 pg11:2 sb2 H3 G3 sb0 K3 "
+         "pp tmp pg14 dd pg13:2 pg9:01 kb1 ou0 fg1 sb3 fh1 "
+         "Y:2 ks:2 oy1:2 wb3:2 oj0:2 wb1:2 Y:2 wb0:2 wb2:2 z0:2 fl:2 wk:2 sb2:2 ou1:2 sb1:2 Yb:2 oj1:2 Yb:2 z1:2 "
+         "pg13:01 wz:0 oj0:01 pg10:01 oy1:01 z0:01 wb3:01 wb2:01 wb0:01 wb1:01 o32:0 ks:01 fl:01 zl1:01 wk:01 X0:01 sb2:01 sb1:01 X0:01 "
+         "pi0:01 a32:01 ou1:01 pi1:01 pi0:01 oj1:01 X1:01 pi0:01 X1:01 hu0:01 id16:0",
+    "s": "cl1:12 za1:12 x0 nb1:12 x2 x3 x4 H0 x5 x6 x7 H0 vv Yp0:2 y0 e0:2 Yp1:2 nv0 Yp2:2 Yp3:2 cl0 za0 y1 j0 nb0:01 zs:01 nb0:2 nv1 e1:2 cl1:2 "
+         "zs:01 za1:2 zs:01 j1",
+    "p": "us1:12 uc1:12 uz1:12 col:12 uq1:12 hx0 gm00 rz1 hx1 hz1 gm01 gm1 ih1 rp2 ig1 rz3 pa0:2 gm20 ly0 hx2 gm21 gm22 lj0 gm23 hx3 hz3 gm3 sy0 "
+         "dv0 pa1:2 pa2:2 dy0 uc0:01 zy0 lm0 pa3:2 sm0 zr0 sj0 ly1 sy1 dv1 lm1 us0:01 uz0:01 ac0:01 dy1 lj1 ac1:01 uq0:01 sm1 sj1:01 pk:2 zy1 zr1:01 "
+         "ih0:01 sj1:2 rq0:01 zr1:2 ig0:01 rq1:01",
+    "g": "r8:0 sj1:12 " + "zr0:12 " * 6 + "zr1 " * 15 + "sg0 sy0 sg1 sy1 " + "zr0:01 " * 5 + "sj0:01 zr0:01",
+    "y": "do0 do1 dr0 dr1 wa0 wb0 wc0 wa1 wb1 wc1 oj0:2 oz0:2 oy0:2 oy1:2 oz1:2 oj1:2",
+}
 
 
-def knockout(c, fill):
-    out = []
-    for lv in range(4):
-        out += ["pp", "tmp"] + fill[2 * lv].split() + ["dd"] + fill[2 * lv + 1].split()
-        out += ["%s%d" % (k, lv + 1) for k in "sHK"] if lv < 3 else ["%s%d" % (k, c) for k in ("fs", "fh", "kb")]
-    return out + ["sb30", "sb31"]
-
-
-def vector_line(t):
-    out = ("x1 pi1 pi1 hu1 m0_0 m0_1 z1 m0_2 m0_3 pg0 pg1 pg2 pi2 pi3 pi2" if t else "x1 m0_0 m0_1 m0_2 m0_3 pg0 pg1 pg2 pi2 pi3").split()
-    out += "ri pi2 pg3 hu2 m1_0 m1_1 m1_2 m1_3".split() + ["Yp"] * (t == 2) + "pg4 pg5 s0".split()
-    out += knockout(0, ["pg6", "pg7", "ri m2_0", "m2_1", "cm1 m2_2", "m2_3", "cu", "pg8"]) + "M6 oy0 M7 pg9 pg10 wa pg11 sb20 sb21 s0 sb00 sb01".split()
-    out += knockout(1, ["pg12", "ou0", "oj0", "pg13", "pg14", "pg15", "z0", ""])
-    out += ("X0 oy1 pi0 pi1 wa sb20 sb21 sb10 sb11 ou1 a32 X1 pi0 oj1 pi0 hu0" if t < 2 else "cu2 oy1 Y wa sb20 sb21 sb10 sb11 ou1 oj1").split()
+def line(eng):
+    out = HEAD[eng].split()
+    for t in range(3):
+        out += [k.split(":")[0] for k in ROUND[eng].split() if ":" not in k or str(t) in k.split(":")[1]]
     return out
 
 
-def scalar_line(t):
-    out = ("x0 cl1 za1 x2 nb1" if t else "nb0 nb1 x0 x2") + " x3 x4 H0 x5 x6 x7 m6 m7 y0"
-    if t < 2:
-        return (out + " H0 vv nv0 cl0 za0 J%d0 nb0 y1 nv1 J%d1" % (t + 1, t + 1)).split()
-    return (out + " H0 vv nv0 e0 cl0 za0 jo0 y1 nv1 nb0 e1 jo1 cl1 za1").split()
-
-
-def order(ops, setup, lines):
-    n = len(ops)
-    pred, lastw, readers = [set() for _ in ops], {}, {}
-    for i, (eng, fn, rd, wr, tok, busy, lat) in enumerate(ops):
+def order(ops):
+    pred, lastw, readers, named = [set() for _ in ops], {}, {}, {}
+    for i, (eng, fn, rd, wr, tok, name) in enumerate(ops):
         wr = wr + [k for k in rd if k in BANKS]
         for k in rd + wr:
             pred[i].update(lastw.get(k, []))
@@ -83,62 +99,23 @@ def order(ops, setup, lines):
             readers.setdefault(k, []).append(i)
         for k in wr:
             lastw[k], readers[k] = [i], []
-        if fn is None:
-            pred[i].add(i - 1)
         pred[i].discard(i)
-    soft, writers = set(), {}
-    for i, a in enumerate(ops):
-        if (i >= setup or a[0] == "y") and a[3]:
-            writers.setdefault((a[0], a[3][0]), []).append(i)
-    for eng, keys in lines.items():
-        line = [writers[eng, k].pop(0) for k in keys]
-        for j, i in zip(line, line[1:]):
-            if j not in pred[i]:
-                pred[i].add(j)
-                soft.add((j, i))
-
-    def gap(j, i):
-        a, b = ops[j], ops[i]
-        if (j, i) in soft or a[0] == b[0] and (a[0] == "p" or (a[4] is not None and a[4] == b[4])):
-            return a[5]
-        return a[5] + a[6] + WAKE
-    succ = [[] for _ in ops]
-    for i in range(n):
-        for j in pred[i]:
-            succ[j].append(i)
-    rank, todo = [0.0] * n, [len(s) for s in succ]
-    back = [i for i in range(n) if not todo[i]]
-    for i in back:
-        rank[i] = max([ops[i][5] + ops[i][6]] + [gap(i, j) + rank[j] for j in succ[i]])
-        for j in pred[i]:
-            todo[j] -= 1
-            if not todo[j]:
-                back.append(j)
-    assert len(back) == n
-    left, est, free, out = [len(p) for p in pred], [0.0] * n, {}, []
-    ready, last = [i for i in range(n) if not left[i]], 0
-    while ready:
-        at = {i: max(est[i], free.get(ops[i][0], 0.0)) if ops[i][1] else est[i] for i in ready}
-        first = min(ready, key=lambda i: (at[i], -rank[i]))
-        i = first
-        if ops[i][1]:
-            near = [j for j in ready if ops[j][0] == ops[i][0] and ops[j][1] and at[j] <= at[i] + AHEAD[ops[i][0]]]
-            best = max(near, key=lambda j: (rank[j], -j))
-            short = [j for j in near if at[j] < at[best] and at[j] + ops[j][5] <= at[best] + FILL]
-            i = max(short, key=lambda j: (rank[j], -j)) if short else best
-            if ops[i][0] == "p":
-                if last + 1 in near and ops[last + 1][3] == ops[last][3]:
-                    i = last + 1
-                last = i
-        ready.remove(i)
-        out.append(ops[i])
-        if ops[i][1]:
-            free[ops[i][0]] = at[i] + ops[i][5]
-        for j in succ[i]:
-            est[j] = max(est[j], at[i] + gap(i, j))
-            left[j] -= 1
-            if not left[j]:
-                ready.append(j)
+        if fn is None or eng in "py" and ops[i - 1][0] == eng and ops[i - 1][5] == name:
+            group.append(i)
+        else:
+            group = [i]
+            named.setdefault((eng, name), []).append(group)
+    queue = {e: [i for k in line(e) for i in named[e, k].pop(0)] for e in HEAD}
+    assert not any(named.values())
+    out, done, at = [], set(), {e: 0 for e in queue}
+    while len(out) < len(ops):
+        n = len(out)
+        for e, q in queue.items():
+            while at[e] < len(q) and pred[q[at[e]]] <= done:
+                done.add(q[at[e]])
+                out.append(ops[q[at[e]]])
+                at[e] += 1
+        assert len(out) > n, [(e, at[e], ops[q[at[e]]][5], [ops[j][5] for j in pred[q[at[e]]] - done]) for e, q in queue.items() if at[e] < len(q)]
     return out
 
 
@@ -147,8 +124,8 @@ def emit(g, T, ops):
     cnt = {e: 0 for e in ESEM}
     know = {e: {} for e in Q}
     clock = {}
-    lastw, readers, bank, total = {}, {}, {}, {}
-    for eng, fn, rd, wr, tok, _, _ in ops:
+    lastw, readers, bank, total, seen = {}, {}, {}, {}, {}
+    for eng, fn, rd, wr, tok, _ in ops:
         deps = []
         for k in rd:
             if k not in BANKS:
@@ -167,6 +144,7 @@ def emit(g, T, ops):
                 if kn.get(d[0], 0) < d[1] and d != tok:
                     Q[eng].wait_ge(T.sem[d[0]], d[1])
                     kn[d[0]] = d[1]
+                    seen[d[0]] = max(seen.get(d[0], 0), d[1])
                     for s, v in clock.get(d, {}).items():
                         kn[s] = max(kn.get(s, 0), v)
             ins = fn(Q[eng])
@@ -179,7 +157,7 @@ def emit(g, T, ops):
             ck = clock.setdefault(tok, {})
             for s, v in kn.items():
                 ck[s] = max(ck.get(s, 0), v)
-        total[tok[0]] = max(total.get(tok[0], 0), tok[1])
+        total[tok[0]] = max(total.pop(tok[0], 0), tok[1])
         for k in rd:
             if k not in BANKS:
                 readers.setdefault(k, []).append(tok)
@@ -191,81 +169,95 @@ def emit(g, T, ops):
             if k in BANKS:
                 bank.setdefault(k, {})[eng] = tok
     for s, v in total.items():
-        if know["g"].get(s, 0) < v:
+        if seen.get(s, 0) < v:
             g.wait_ge(T.sem[s], v)
 
 
-def size(ap):
-    n = 1
-    for d in ap.shape[1:]:
-        n *= d
-    return n
+def helpers(T, topo, core):
+    return [h for h in topo.cores_of(core) if topo.die(h) == topo.die(core) and h not in T.cores]
+
+
+def hand_on(g, core, T, topo, rank, c):
+    home = T.cores[rank]
+    rid, pid, _ = topo.addr(home)
+    for t in range(3):
+        k = "%d%d" % (t, c)
+        w, d, far = T["W" + k], T["D" + k], len(topo.engines(T.cores[rank ^ STEPS[t]], core))
+        g.scalar.wait_ge(T.sem["ao" + k], len(topo.engines(home, core)) - far)
+        g.scalar.dma_start(d[:, 0:16, :], w[:, 0:256]).then_inc(T.sem["do" + k], 16)
+        g.sync.wait_ge(T.sem["aj" + k], far)
+        g.sync.dma_start(d[:, 16:32, :], w[:, 4096:4352]).then_inc(T.sem["do" + k], 16)
+        g.sync.wait_ge(T.sem["do" + k], 32)
+        for s in range(1, 16):
+            g.sync.dma_start(w[:, 256 * s:256 * s + 256], d[:, s:s + 16, :]).then_inc(T.sem["dp%d%d" % (t, (s - 1) * PARTS // 16)], 16)
+        for p in range(PARTS):
+            a, b = 1 + 16 * p // PARTS, 1 + 16 * (p + 1) // PARTS
+            g.wait_ge(T.sem["dp%d%d" % (t, p)], 16 * (min(b, 16) - a))
+            g.remote_dma(w[:, 256 * a:256 * b], w[:, 256 * a:256 * b], T.sem["dt" + k], T.sem["lt"], pid, rid, topo.mask(core, home))
+    g.wait_ge(T.sem["lt"], 3 * PARTS * len(topo.engines(core, home)))
 
 
 def rank_program(g, core, T, topo):
     rank = T.rank_of(core)
     if rank is None:
+        for r, home in enumerate(T.cores):
+            if HELP and core in helpers(T, topo, home)[0:2]:
+                hand_on(g, core, T, topo, r, helpers(T, topo, home).index(core))
         return
     ops = []
 
-    def o(eng, fn, rd, wr, busy, lat=0.0, tok=None):
-        return (eng, fn, list(rd), list(wr), tok, busy, lat)
+    def o(eng, fn, rd, wr, name=None, tok=None):
+        return (eng, fn, list(rd), list(wr), tok, name or wr[0])
 
-    def vec(fn, n, rd, wr):
-        return o("v", fn, rd, wr, 32.0 + 0.83 * n)
+    def tt(out, a, b, op, rd, wr):
+        return o("v", lambda q: q.tensor_tensor(out, a, b, op), rd, wr)
 
-    def tt(out, a, b, op, rd, wr, r=1.0):
-        return vec(lambda q: q.tensor_tensor(out, a, b, op), r * size(b), rd, wr)
-
-    def ts(out, a, s1, op0, rd, wr, s2=None, op1=None, r=1.0):
+    def ts(out, a, s1, op0, rd, wr, s2=None, op1=None):
         if op1 is None:
-            return vec(lambda q: q.tensor_scalar(out, a, s1, None, op0), r * size(a), rd, wr)
-        return vec(lambda q: q.tensor_scalar(out, a, s1, s2, op0, op1), r * size(a), rd, wr)
+            return o("v", lambda q: q.tensor_scalar(out, a, s1, None, op0), rd, wr)
+        return o("v", lambda q: q.tensor_scalar(out, a, s1, s2, op0, op1), rd, wr)
 
-    def cp(out, a, rd, wr, n=None):
-        return vec(lambda q: q.tensor_copy(out, a), n or size(out), rd, wr)
+    def cp(out, a, rd, wr, name=None):
+        return o("v", lambda q: q.tensor_copy(out, a), rd, wr, name)
 
     def ms(ap, c, wr):
-        return vec(lambda q: q.memset(ap, c), 0.5 * size(ap), [], wr)
+        return o("v", lambda q: q.memset(ap, c), [], wr)
 
-    def scan(out, a, b, op0, op1, rd, wr, r=1.0):
-        return vec(lambda q: q.tensor_tensor_scan(out, a, b, 0.0, op0, op1), r * size(out), rd, wr)
+    def scan(out, a, b, op0, op1, rd, wr, first=0.0):
+        return o("v", lambda q: q.tensor_tensor_scan(out, a, b, first, op0, op1), rd, wr)
 
-    def act(out, a, fn, rd, wr, bias=0.0, scale=1.0, r=1.0):
-        return o("s", lambda q: q.activation(out, a, fn, bias=bias, scale=scale), rd, wr, 120.0 + 0.83 * r * size(out))
+    def act(out, a, fn, rd, wr, bias=0.0, scale=1.0, name=None):
+        return o("s", lambda q: q.activation(out, a, fn, bias=bias, scale=scale), rd, wr, name)
 
-    def mm(out, l, r, st, sp, rd, wr, slow=1):
-        return o("p", lambda q: q.matmul(out, l, r, st, sp), rd, wr, 5.0 + 0.7 * slow * max(64, size(r)))
+    def mm(name, out, l, r, st, sp, rd, bk):
+        return o("p", lambda q: q.matmul(out, l, r, st, sp), rd, [bk], name)
 
-    def dma(eng, out, a, rd, wr, sem, kb, n=1):
-        return o(eng, lambda q: q.dma_start(out, a), rd, wr, 60.0 if eng == "s" else 2.5 * kb, 1000.0 + (2.5 * kb if eng == "s" else 0), (sem, 16 * n))
+    def dma(eng, name, out, a, rd, wr, sem, n=1):
+        return o(eng, lambda q: q.dma_start(out, a), rd, wr, name, (sem, 16 * n))
 
-    def send(t, c, kind, dst, src, rd, land, kb):
+    def send(t, c, kind, dst, src, rd, land):
         peer = T.cores[rank ^ STEPS[t]]
         assert topo.may_write(core, peer)
         rid, pid, _ = topo.addr(peer)
         n = len(topo.engines(core, peer))
         back = len(topo.engines(peer, core))
-        a, l = "a%s%d%d" % (kind, t, c), "l%s%d%d" % (kind, t, c)
+        a, l, name = "a%s%d%d" % (kind, t, c), "l%s%d%d" % (kind, t, c), "s%s%d" % (kind, c)
 
         def f(q):
             q.remote_dma(dst, src, T.sem[a], T.sem[l], pid, rid, topo.mask(core, peer))
-        return [o("g", f, rd, [], 300.0, 700.0 + 10.0 * kb, (l, n)), o("g", None, [], [land], 0.0, 500.0, (a, back))]
+        return [o("g", f, rd, [], name, (l, n)), o("g", None, [], [land], name, (a, back))]
 
     def iota(out, pat, base, cm, wr, **kw):
-        return o("g", lambda q: q.iota(out, pat, base, cm, **kw), [], wr, 130.0 + 1.66 * size(out))
+        return o("g", lambda q: q.iota(out, pat, base, cm, **kw), [], wr)
 
-    def asel(out, a, pat, cmp, base, cm, rd, wr):
-        return o("g", lambda q: q.affine_select(out, a, pat, cmp, 0.0, base, cm), rd, wr, 170.0 + 1.66 * size(out))
+    def asel(out, a, pat, cmp, base, cm, rd, wr, name=None):
+        return o("g", lambda q: q.affine_select(out, a, pat, cmp, 0.0, base, cm), rd, wr, name)
 
     def W(t, c):
         return T["W%d%d" % (t, c)]
 
     def ln(c):
         return slice(256 * c, 256 * c + 256)
-
-    def zs(j):
-        return T.z[:, 256 * (j // 2) + j % 2:256 * (j // 2) + 256:2]
 
     def idx(v):
         return T.ids[:, IDS.index(v), :]
@@ -274,9 +266,8 @@ def rank_program(g, core, T, topo):
     XK = ["X0", "X1", "Xl"]
     OJ, OS, OZ = (0, 48), (16, 80), (32, 64)
 
-    ops += [dma("s", T.w[:], T.wt[:], [], ["w"], "ldw", 1), dma("y", T.z[:], T.zd[:], [], ["z0", "z1"], "ldz", 128),
-            dma("s", T.ji[:, ln(0)], T.jn[:, ln(0)], [], ["ji0"], "ldj", 128), dma("y", REC, T.xt[:], [], ["Xl"], "ldx", 1024),
-            dma("y", T.ji[:, ln(1)], T.jn[:, ln(1)], [], ["ji1"], "ldk", 128)]
+    ops += [dma("s", "w", T.w[:], T.wt[:], [], ["w"], "ldw"), dma("y", "z0", T.z[:], T.zd[:], [], ["z0", "z1"], "ldz"),
+            dma("s", "ji", T.ji[:], T.jn[:], [], ["ji0", "ji1"], "ldj"), dma("y", "Xl", REC, T.xt[:], [], ["Xl"], "ldx")]
     small = dict(allow_small_or_imprecise_dtypes=True)
     ops += [ms(T.one[:], 1.0, ["one"]),
             asel(T.bd[:], T.one[:, 0:128], [[-16, 8], [0, 16]], OP.is_ge, 0, 1, ["one"], ["bd"]),
@@ -285,22 +276,24 @@ def rank_program(g, core, T, topo):
             iota(T.i3[:], [[16, 16]], 0, 0, ["i3"]), iota(T.i4[:], [[0, 2]], 0, 1, ["i4"]),
             iota(T.kc[:], [[0, 16], [1, 16]], 1, 0, ["kc"], **small),
             asel(T.r8[:], T.one[:, 0:128], [[-1, 8], [-8, 16]], OP.is_equal, 0, 1, ["one"], ["r8"]),
-            iota(T.ro[:], [[0, 8], [256 - SP, 3], [0, 16]], SP, 0, ["ro"], **small),
-            asel(T.ro[:], T.ro[:], [[-1, 8], [0, 3], [-8, 16]], OP.is_equal, 0, 1, ["ro"], ["ro"]),
             ms(T.cst[0:64, :], 6144.0, ["cst0"]), ms(T.cst[64:128, :], 33.0 / 64, ["cst1"]),
             ms(T.mp[:], 1.0, ["mp"]), ms(T.dd[:], BIG * BIG, ["dd"]),
-            ms(T.sb[:], 0.0, ["sb%d%d" % (i, b) for i in range(4) for b in range(2)]), ms(T.mp[:, 0::16], 0.0, ["mp"]),
+            ms(T.sb[:], 0.0, ["sb%d" % i for i in range(4)]), ms(T.mp[:, 0::16], 0.0, ["mp"]),
+            ms(T.mr[:], 1.0, ["mr"]), ms(T.mr[:, 0::16], -1024.0, ["mr"]), ms(T.mr[:, 1::16], -1.0, ["mr"]),
+            ms(T.zr[:, 0::16], 0.0, ["zz"]), ms(T.ks[:], 0.0, ["kz"]), ms(T.wb[:, 0], 0.0, ["wz"]), ms(T.wb[:, 1], 1.0, ["wz"]),
+            ms(T.rw[0:1, 0], -1.0, ["rw0"]), ms(T.rw[0:1, 1:3], 0.0, ["rw"]), ms(T.rw[0:1, 1, :, 16:32], -1.0, ["rw1", "rw"]),
+            cp(T.rw[0:1, 2, :, 0:16], T.kc[0:1, 0:128], ["kc", "rw"], ["rw2"]),
             ms(T.qw[:], 0.0, ["qw"]), ms(T.m192[:], -192.0, ["m192"]), ms(T.o32[:], 32.0, ["o32"]), ms(T.f4[0:1, :], BIG, ["f4"]),
             ts(T.bdw[:], T.bd[:], T.w[:], OP.mult, ["bd", "w"], ["bdw"]),
             ts(T.bdw2[:], T.bd[:], T.w[:], OP.mult, ["bd", "w"], ["bdw2"], 2.0, OP.mult),
-            ts(T.bd4[:], T.bd[:], BIG, OP.mult, ["bd"], ["bd4"], r=0.5),
+            ts(T.bd4[:, 0], T.bd[:], BIG, OP.mult, ["bd"], ["bd4"]), ts(T.bd4[:, 1], T.bd[:], -BIG, OP.mult, ["bd"], ["bd5"]),
             cp(T.idf[:], T.idb[:], ["idb"], ["idf"]), cp(T.qw[:, 15:143:16], T.bdw[:, 0::16], ["bdw", "qw"], ["qw"]),
-            ts(T.zq[:], T.bd[:], -BIG, OP.mult, ["bd"], ["zq"], r=0.5),
             ts(T.i4[:, 0:1], T.i4[:, 0:1], 15, OP.bitwise_and, ["i4"], ["i4a"]),
             ts(T.i4[:, 1:2], T.i4[:, 1:2], 1, OP.bitwise_and, ["i4"], ["i4b"]),
             cp(T.pc[:], T.i4[:], ["i4a", "i4b"], ["pc"]),
             ts(T.a1[:], T.pc[:, 1:2], 2040.0, OP.mult, ["pc"], ["a1"], -1.0, OP.add)]
-    ops += [ts(idx(v), T.idb[:], v, OP.mult, ["idb"], ["id%d" % v], r=0.5) for v in IDS]
+    ops += [ts(idx(v), T.idb[:], v, OP.mult, ["idb"], ["id%d" % v]) for v in IDS]
+    ops += [ts(T.ro[:, :, i, :], T.r8[:], v, OP.mult, ["r8"], ["ro%d" % i]) for i, v in enumerate((1.0 * SP, 256.0, 512.0 - SP))]
     ops += [ts(T.cm[:, j, :], T.i3[:], T.pc[:, 0:1], OP.add, ["i3", "pc"], ["cm%d" % j]) for j in (0, 2, 4)]
     ops += [ts(T.cy[:], T.cm[:, 0, :], 8.0, OP.mult, ["cm0", "a1"], ["cy"], T.a1[:], OP.add),
             ts(T.c8[:, 0:16], T.cm[:, 0, :], 8.0, OP.mult, ["cm0"], ["c80"]),
@@ -308,20 +301,33 @@ def rank_program(g, core, T, topo):
             ts(T.adj[:], T.i3[:], 128.0, OP.is_ge, ["i3"], ["adj"], -1024.0, OP.mult)]
 
     def tables(t, c):
-        w, d, k = W(t, c), T["D%d%d" % (t, c)], "%d%d" % (t, c)
-        out = send(t, c, "j", w[:, 4096:4352], w[:, 0:256], ["J" + k, "RY%d1" % (t - 1)], "Jr" + k, 128)
-        out += [dma("y", d[:, 0:16, :], w[:, 0:256], ["J" + k], ["Do" + k], "do" + k, 128),
-                dma("y", d[:, 16:32, :], w[:, 4096:4352], ["Jr" + k], ["Dr" + k], "dr" + k, 128)]
-        out += [dma("y", w[:, 256 * s:256 * s + 256], d[:, s:s + 16, :], ["Do" + k, "Dr" + k], ["Wt" + k], "dt" + k, 128, 15) for s in range(1, 16)]
-        return out
+        w, k = W(t, c), "%d%d" % (t, c)
+        if not HELP:
+            d, last = T["D" + k], ["RY%d1" % (t - 1)]
+            out = send(t, c, "j", w[:, 4096:4352], w[:, 0:256], ["J" + k] + last, "Jr" + k)
+            out += [dma("y", "do%d" % c, d[:, 0:16, :], w[:, 0:256], ["J" + k] + last, ["Do" + k], "do" + k),
+                    dma("y", "dr%d" % c, d[:, 16:32, :], w[:, 4096:4352], ["Jr" + k], ["Dr" + k], "ao" + k)]
+            return out + [dma("y", "w%s%d" % ("abc"[(s - 1) // 5], c), w[:, 256 * s:256 * s + 256], d[:, s:s + 16, :], ["Do" + k, "Dr" + k], ["Wt" + k],
+                              "dt" + k, 15) for s in range(1, 16)]
+        far, near = helpers(T, topo, T.cores[rank ^ STEPS[t]])[c], helpers(T, topo, core)[c]
+        assert topo.may_write(core, far)
+        mask = topo.mask(core, far)
+        go = [RemoteDMATransfer(dst_ids=[DstId(rid=topo.addr(h)[0], pnc=topo.addr(h)[1])], dma_engine_mask=m, remote_sem=T.sem[s + k], src=w[:, 0:256], dst=dst)
+              for h, m, s, dst in ((far, mask, "aj", w[:, 4096:4352]), (near, topo.mask(core, near) & ~mask, "ao", w[:, 0:256]))]
+
+        def f(q):
+            q.remote_dma_fused(go, local_sem=T.sem["lj" + k])
+        return [o("g", f, ["J" + k] + ["RY%d1" % (t - 1)] * c, [], "sj%d" % c, ("lj" + k, len(topo.engines(core, near)))),
+                o("g", None, [], ["Wt" + k], "sj%d" % c, ("dt" + k, PARTS * len(topo.engines(near, core))))]
 
     def factor(c):
-        k = ["UU"]
-        return [mm(T.S0[:, 1], T.bdw[:], T.z[:, ln(c)], True, True, ["bdw", "z%d" % c], ["S0"]),
-                act(T.nb[:, ln(c)], T.S0[:, 1], AF.Identity, ["S0"], ["nb%d" % c], 191.5 + 1.0 / 2048, 1.0 / 1024),
-                mm(T.UU[:, ln(c)], T.cst[:], T.one[:], True, False, ["cst0", "cst1", "one"], k),
-                mm(T.UU[:, ln(c)], T.bdw2[:], T.z[:, ln(c)], False, False, ["bdw2", "z%d" % c], k),
-                mm(T.UU[:, ln(c)], idx(-2048), T.nb[:, ln(c)], False, True, ["id-2048", "nb%d" % c], k)]
+        z, s, bk = "z%d" % c, T["S%d" % c], "S%d" % c
+        return repeat(c) \
+            + [mm("us%d" % c, s[:, 0], T.bdw[:], T.z[:, ln(c)], True, True, ["bdw", z], bk),
+               act(T.nb[:, ln(c)], s[:, 0], AF.Identity, [bk], ["nb%d" % c], 191.5 + 1.0 / 2048, 1.0 / 1024),
+               mm("uc%d" % c, T.UU[:, ln(c)], T.cst[:], T.one[:], True, False, ["cst0", "cst1", "one"], "UU"),
+               mm("uz%d" % c, T.UU[:, ln(c)], T.bdw2[:], T.z[:, ln(c)], False, False, ["bdw2", z], "UU"),
+               mm("uq%d" % c, T.UU[:, ln(c)], idx(-2048), T.nb[:, ln(c)], False, True, ["id-2048", "nb%d" % c], "UU")]
 
     def prod(t, c):
         src, k = (T.ji[:, ln(c)], "ji%d" % c) if t == 0 else (W(t, c)[:, 0:256], "J%d%d" % (t, c))
@@ -339,65 +345,76 @@ def rank_program(g, core, T, topo):
             out.append(cp(T.hu[:, sl], T.pi[:, sl], k, ["hu%d" % q for q in qs]))
         return out
 
-    def pick(j):
-        out, src, rd, wr = T.xg[:, 1024 * j:1024 * j + 1024], REC.indirect(T.hu[:, 64 * j:64 * j + 64]), XK + ["hu%d" % (j // 2)], ["x%d" % j]
-        return [cp(out, src, rd, wr, GATHER * 1024) if j in VPICK else act(out, src, AF.Copy, rd, wr, r=GATHER)]
+    def xk(j):
+        return ["x%d" % j] + ["w1"] * (j == 1)
 
-    def spread(j):
-        bk = "Z%d" % (j % 2)
-        return [mm(T[bk][:, r::4], T.idb[:], zs(j), True, True, ["idb", "z%d" % (j // 2)], [bk]) for r in range(4)]
+    def pick(t, j):
+        out, cut = [], VPICK[t] if j == 1 else 0
+        for a, b in ((0, cut), (cut, 64)):
+            if a < b:
+                dst, src = T.xg[:, 1024 * j + 16 * a:1024 * j + 16 * b], REC.indirect(T.hu[:, 64 * j + a:64 * j + b])
+                rd = XK + ["hu%d" % (j // 2)]
+                out.append(act(dst, src, AF.Identity, rd, [xk(j)[-1]], LIFT * (j // 2 in SCAN)) if b > cut else ts(dst, src, LIFT * (0 in SCAN), OP.add, rd, ["x%d" % j]))
+        return out
 
-    def over(j, h):
-        x, m, k = T.xg[:, 2048 * j + h:2048 * j + 2048:4], T.mg[:, 2048 * j + h:2048 * j + 2048:4], ["m%d_%d" % (j, h)]
-        return [tt(m, x, T["Z%d" % (j % 2)][:], OP.max, ["x%d" % (2 * j), "x%d" % (2 * j + 1), "Z%d" % (j % 2)], k)]
+    def repeat(c):
+        qs = [q for q in SCAN if q // 2 == c]
+        a, b, k = SCAN.index(qs[0]), SCAN.index(qs[-1]) + 1, ["zl%d" % q for q in qs]
+        return [ts(T.zl[:, SCAN.index(q)], T.z[:, 256 * c + q % 2:256 * c + 256:2], LIFT, OP.add, ["z%d" % c], ["zl%d" % q]) for q in qs] \
+            + [act(T.zr[:, 2048 * a + r:2048 * b:16], T.zl[:, a:b], AF.Copy, k, ["zr%d%d" % (c, r)], name="zs") if c == 0 and r <= ZS else
+               asel(T.zr[:, 2048 * a + r:2048 * b:16], T.zl[:, a:b], [[0, 128 * (b - a)]], OP.is_equal, 0, 0, k, ["zr%d%d" % (c, r)], "zr%d" % c)
+               for r in range(1, 16)]
 
-    def sums_x(q):
-        b = q % 2
-        out = [] if b else [mm(T.HH[:, 0], T.f4[0:1, :], T.kc[0:1, :], True, False, ["f4", "kc"], ["HH"])]
-        return out + [mm(T.HH[:, 0, b, :, k:16], T.xg[:, 2048 * q + k:2048 * q + 2048:16], T.bd4[:, :, k:16], False, b == 1 and k == 15,
-                         ["x%d" % (2 * q), "x%d" % (2 * q + 1), "bd4"], ["HH"]) for k in range(16)]
+    def under(q):
+        c, a, js = q // 2, 2048 * q, (2 * q, 2 * q + 1)
+        if q == 0:
+            out = []
+            for j in js:
+                zb = "Z%d" % j
+                out += [mm("rq%d" % j, T[zb][:, r::8], T.idb[:], T.z[:, 128 * j:128 * j + 128:2], True, True, ["idb", "z0"], zb) for r in range(8)]
+                out += [tt(T.mg[:, 1024 * j + h:1024 * j + 1024:2], T.xg[:, 1024 * j + h:1024 * j + 1024:2], T[zb][:], OP.min, xk(j) + [zb], ["u%d%d" % (j, h)])
+                        for h in range(2)]
+            return out, [["u%d%d" % (j, k % 2) for j in js] for k in range(16)]
+        if q not in SCAN:
+            return [mm("rp%d" % q, T.Z1[:, r::4], T.idb[:], T.z[:, 256 * c + q % 2:256 * c + 256:2], True, True, ["idb", "z%d" % c], "Z1") for r in range(4)] \
+                + [tt(T.mg[:, a + h:a + 2048:4], T.xg[:, a + h:a + 2048:4], T.Z1[:], OP.min, xk(js[0]) + xk(js[1]) + ["Z1"], ["m%d%d" % (q, h)]) for h in range(4)], \
+                [["m%d%d" % (q, k % 4)] for k in range(16)]
+        i, out = SCAN.index(q), []
+        out.append(mm("rz%d" % q, T.Z0[:, 128 * i:128 * i + 128], idx(-1), T.zl[:, i], True, True, ["id-1", "zl%d" % q], "Z0"))
+        parts = [(js, 0, 128)] if c == 0 else [(js[0:1], 0, 64), (js[1:2], 64, 128)]
+        for ps, lo, hi in parts:
+            first, k = T.xg[:, a + 16 * lo:a + 16 * hi:16], [x for j in ps for x in xk(j)]
+            n = ["n%d" % j for j in ps]
+            out += [ts(first, first, -1.0, OP.mult, k, n),
+                    tt(T.m0[:, 128 * i + lo:128 * i + hi], first, T.Z0[:, 128 * i + lo:128 * i + hi], OP.max, k + n + ["Z0"], ["f%d" % j for j in ps])]
+        out += [scan(T.mg[:, 1024 * j:1024 * j + 1024], T.zr[:, 2048 * i + 1024 * (j % 2):2048 * i + 1024 * (j % 2) + 1024], T.xg[:, 1024 * j:1024 * j + 1024],
+                     OP.max, OP.min, xk(j) + ["zz", "n%d" % j] + ["zr%d%d" % (c, r) for r in range(1, 16)], ["m%d" % j]) for j in js]
+        return out, [["%s%d" % ("m" if k else "f", j) for j in js] for k in range(16)]
 
-    def sums_m(q, h):
-        c, b = q // 2, q % 2
-        s, bk = T["S%d" % c], ["S%d" % c]
-        out = []
-        st = 2 if q in SHARED else 1
-        if h == st - 1 and b == 0:
-            out.append(mm(s[:, 1], T.f4[0:1, :], T.one[0:1, :], True, False, ["f4", "one"], bk))
-        if h == st - 1:
-            out.append(mm(s[:, 1, 128 * b:128 * b + 128:st], zs(q), T.zq[:, ::st], False, False, ["z%d" % c, "zq"], bk))
-        keys = ["%s%d" % ("Mm"[h], j) for j in (2 * q, 2 * q + 1)] if q in SHARED else ["m%d_%d" % (q, h)]
-        return out + [mm(s[:, 1, 128 * b + k:128 * b + 128:16], T.mg[:, 2048 * q + k:2048 * q + 2048:16], T.bd4[:, :, 0], False, b == 1 and k == 16 - st,
-                         keys + ["bd4"], bk) for k in range(h, 16, 4 // st)]
-
-    def shared(j):
-        a, zb, bk, k = 1024 * j, ("Z1", "S0")[j % 2], ("UU", "DZ")[j % 2], "z%d" % (j // 4)
-        b = 256 * (j // 4) + 128 * (j % 2) + (j // 2) % 2
-        z = T.z[:, b:b + 127:2]
-        return [mm(T[zb][..., r::8], T.idb[:], z, True, True, ["idb", k], [zb]) for r in range(8)] \
-            + [mm(T[bk][:], T.idb[:], T.xg[:, a + 1:a + 1024:2], True, False, ["x%d" % j], [bk])] \
-            + [mm(T[bk][:, r::8], idx(-1), z, False, r == 7, ["id-1", k], [bk]) for r in range(8)] \
-            + [act(T.mg[:, a + 1:a + 1024:2], T[bk][:], AF.Relu, [bk], ["m%d" % j]),
-               tt(T.mg[:, a:a + 1024:2], T.xg[:, a:a + 1024:2], T[zb][:], OP.max, ["x%d" % j, zb], ["M%d" % j])]
-
-    def quarter(q):
-        out = pick(2 * q) + pick(2 * q + 1)
-        if q in SHARED:
-            out += shared(2 * q) + shared(2 * q + 1) + sums_x(q) + sums_m(q, 1) + sums_m(q, 0)
-        else:
-            out += spread(q) + sums_x(q)
-            for h in range(4):
-                out += over(q, h) + sums_m(q, h)
-        if q % 2:
-            s, bk = T["S%d" % (q // 2)], "S%d" % (q // 2)
-            out += [act(T.h0[:], T.HH[:, 0], AF.Copy, ["HH"], ["H0"]),
-                    scan(s[:, 0, :], T.mp[:, 0:256], s[:, 1, :], OP.mult, OP.add, ["mp", bk], ["s0"])]
-        return out + [scan(T.pg[:, 512 * i:512 * i + 512], T.mp[:, 0:512], T.xg[:, 512 * i:512 * i + 512], OP.mult, OP.max, ["mp", "x%d" % (i // 2)],
-                           ["pg%d" % i], 0.5) for i in range(4 * q, 4 * q + 4)]
+    def quarter(t, q):
+        c, b, up = q // 2, q % 2, q in SCAN
+        s, bk = T["S%d" % c], "S%d" % c
+        mins, keys = under(q)
+        out = pick(t, 2 * q) + pick(t, 2 * q + 1) + mins
+        if b == 0:
+            out.append(mm("ig%d" % c, s[:, 1], T.f4[0:1, :], T.rw[0:1, int(not up)], True, False, ["f4", "rw0", "rw1"], bk))
+        if not up:
+            out.append(mm("ih%d" % c, T.HH[:, 0], T.f4[0:1, :], T.rw[0:1, 2], True, False, ["f4", "rw2"], "HH"))
+        out += [mm("hx%d" % q if k or not up else "hz%d" % q, T.HH[:, 0, :, 16 * b + k:16 * b + 16], T.xg[:, 2048 * q + k:2048 * q + 2048:16],
+                   T.bd4[:, int(up and k == 0), :, k:16], False, b == 1 and k == 0,
+                   xk(2 * q) + xk(2 * q + 1) + ["bd4"] + ["bd5", "n%d" % (2 * q), "n%d" % (2 * q + 1)] * (up and k == 0), "HH") for k in range(15, -1, -1)]
+        ks = sorted(range(16), key=lambda k: keys[k])
+        out += [mm("gm%d%s" % (q, "" if up else keys[k][0][-1]), s[:, 1, 16 * b + k::32],
+                   T.m0[:, 128 * SCAN.index(q):128 * SCAN.index(q) + 128] if up and k == 0 else T.mg[:, 2048 * q + k:2048 * q + 2048:16],
+                   T.bd4[:, int(up and k == 0), :, 0], False, b == 1 and k == ks[-1], keys[k], bk) for k in ks]
+        if b:
+            out += [act(T.h0[:], T.HH[:, 0], AF.Copy, ["HH"], ["H0"]), scan(s[:, 0], T.mp[:, 0:256], s[:, 1], OP.mult, OP.add, ["mp", bk], ["G0"])]
+        return out + [scan(T.pg[:, PW * i:PW * i + PW], (T.mr if up else T.mp)[:], T.xg[:, PW * i:PW * i + PW], OP.mult, OP.max, ["mr" if up else "mp", "n%d" % (i * PW // 1024)] + xk(i * PW // 1024),
+                           ["pg%d" % i], 1.0 * up) for i in range(2048 * q // PW, 2048 * (q + 1) // PW)]
 
     def search(t, c):
         s, bk = T["S%d" % c], "S%d" % c
-        So = [s[:, 1, :], s[:, 0, 0:128], s[:, 1, 0:64], T.fin[:, c, 0, :]]
+        Go = [s[:, 1, :], s[:, 0, 0:128], s[:, 1, 0:64], T.fin[:, c, 0, :]]
         Ho = [T.h1[:], T.h2[:], T.h3[:], T.fin[:, c, 1, :]]
         Ko = [T.k1[:], T.k2[:], T.k3[:], T.k4[:, c, :]]
         out = []
@@ -405,108 +422,125 @@ def rank_program(g, core, T, topo):
             n, w = 128 >> lv, min(lv, 1) + 1
             every, a, b = slice(w - 1, 2 * n * w, w), slice(w - 1, 2 * n * w, 2 * w), slice(2 * w - 1, 2 * n * w, 2 * w)
             h, k, r = (T.h0, T.h1, T.h2, T.h3)[lv], (T.kc, T.k1, T.k2, T.k3)[lv], lv % 2
-            d, last, tmp, hk, sk = T.dd[:, 0:2 * n], lv == 3, s[:, 1 - r, 128:128 + n], "H%d" % lv, "s%d" % lv
-            out += [tt(T.pp[:, 0:n], h[:, b], s[:, r, a], OP.mult, [hk, bk, sk], ["pp"]),
-                    tt(tmp, h[:, a], s[:, r, b], OP.mult, [hk, bk, sk], ["tmp"]),
+            d, last, tmp, gk, hk = T.dd[:, 0:2 * n], lv == 3, s[:, 1 - r, 128:128 + n], "G%d" % lv, "H%d" % lv
+            out += [tt(T.pp[:, 0:n], h[:, a], s[:, r, b], OP.mult, [gk, bk, hk], ["pp"]),
+                    tt(tmp, h[:, b], s[:, r, a], OP.mult, [gk, bk, hk], ["tmp"]),
                     tt(T.dd[:, 1:2 * n:2], T.pp[:, 0:n], tmp, OP.subtract, ["pp", "tmp", bk], ["dd"]),
-                    scan(So[lv], d, s[:, r, every], OP.max, OP.min, ["dd", bk, sk], ["fs%d" % c if last else "s%d" % (lv + 1)]),
+                    scan(Go[lv], d, s[:, r, every], OP.max, OP.min, ["dd", bk, gk], ["fg%d" % c if last else "G%d" % (lv + 1)]),
                     scan(Ho[lv], d, h[:, every], OP.max, OP.min, ["dd", hk], ["fh%d" % c if last else "H%d" % (lv + 1)]),
-                    scan(Ko[lv], d, k[:, every], OP.max, OP.min, ["dd", "kc", "K%d" % lv], ["kb%d" % c if last else "K%d" % (lv + 1)], 0.5)]
-        return out + send(t, c, "g", T["RG%d%d" % (t, c)][:], T.fin[:, c], ["fs%d" % c, "fh%d" % c], "RG%d%d" % (t, c), 32)
+                    scan(Ko[lv], d, k[:, every], OP.max, OP.min, ["dd", "kc", "K%d" % lv], ["kb%d" % c if last else "K%d" % (lv + 1)])]
+            if c and lv == 1:
+                out += [cp(T.four[:, 0], s[:, 0, 1:128:2], [bk, "G2"], ["cg"]), cp(T.four[:, 1], T.h2[:, 1::2], ["H2"], ["ch"])]
+                out += send(t, c, "g", T["RG%d1" % t][:], T.four[:], ["cg", "ch"], "RG%d1" % t)
+        return out + ([] if c else send(t, c, "g", T["RG%d0" % t][:], T.fin[:, 0], ["fg0", "fh0"], "RG%d0" % t))
+
+    def spread(name, out, i, cols, bk):
+        return [mm(name, out, T.sb[:, i, 7 - j:71 - j, :], cols(j), False, j == 7, ["sb%d" % i, "r8", "ro0", "ro1", "ro2"], bk) for j in range(8)]
 
     def profile(t, c):
         k = "y%d" % c
-        return [mm(T.LL[:, 0:16], T.idf[:], T.cy[:], True, False, ["idf", "cy"], ["LL"], 4)] \
-            + [cp(T.sb[:, 3, 14 + b:142:16], T.k4[:, c, 16 * b + 1:16 * b + 16:2], ["kb%d" % c], ["sb3%d" % b]) for b in range(2)] \
-            + [mm(T.LL[:, 0:16], T.sb[:, 3, 14 - 2 * j:142 - 2 * j], T.r8[:, 16 * j:16 * j + 16], False, j == 7, ["sb30", "sb31", "r8"], ["LL"]) for j in range(8)] \
+        return [mm("ly%d" % c, T.LL[:, 0:16], T.idf[:], T.cy[:], True, False, ["idf", "cy"], "LL"),
+                cp(T.sb[:, 3, 7::8, :], T.k4[:, c, 1::2], ["kb%d" % c], ["sb3"])] \
+            + spread("sy%d" % c, T.LL[:, 0:16], 3, lambda j: T.r8[:, 16 * j:16 * j + 16], "LL") \
             + [cp(T.oy[:, 16 * c:16 * c + 16], T.LL[:, 0:16], ["LL"], ["oy%d" % c]),
-               act(T.yy[:, ln(c)], T.pg[:, 4096 * c:4096 * (c + 1)].indirect(T.oy[:, 16 * c:16 * c + 16]), AF.Copy,
-                   ["pg%d" % i for i in range(8 * c, 8 * c + 8)] + ["oy%d" % c], [k], r=GATHER)] \
-            + send(t, c, "y", T["RY%d%d" % (t, c)][:], T.yy[:, ln(c)], [k], "RY%d%d" % (t, c), 64) \
-            + [mm(T.DZ[:, 256:512], T.idb[:], T.vv[:, ln(c)], True, False, ["idb", "vv"], ["DZ"]),
-               mm(T.DZ[:, 256:512], T.idb[:], T.yy[:, ln(c)], False, True, [k], ["DZ"]),
-               mm(T.DZ[:, 0:256], idx(2), T.z[:, ln(c)], True, False, ["id2", "z%d" % c], ["DZ"]),
-               mm(T.DZ[:, 0:256], idx(-2), T.yy[:, ln(c)], False, True, ["id-2", k], ["DZ"]),
+               act(T.yy[:, ln(c)], T.pg[:, 4096 * c:4096 * (c + 1)].indirect(T.oy[:, 16 * c:16 * c + 16]), AF.Abs,
+                   ["pg%d" % i for i in range(4096 * c // PW, 4096 * (c + 1) // PW)] + ["oy%d" % c], [k])] \
+            + send(t, c, "y", T["RY%d%d" % (t, c)][:], T.yy[:, ln(c)], [k], "RY%d%d" % (t, c)) \
+            + [mm("dv%d" % c, T.DZ[:, 256:512], T.idb[:], T.vv[:, ln(c)], True, False, ["idb", "vv"], "DZ"),
+               mm("dv%d" % c, T.DZ[:, 0:256], idx(2), T.z[:, ln(c)], False, False, ["id2", "z%d" % c], "DZ"),
+               mm("dy%d" % c, T.DZ[:, 256:512], T.idb[:], T.yy[:, ln(c)], False, False, [k], "DZ"),
+               mm("dy%d" % c, T.DZ[:, 0:256], idx(-2), T.yy[:, ln(c)], False, True, ["id-2", k], "DZ"),
                act(T.cz[:, c, 256:768], T.DZ[:], AF.Identity, ["DZ"], ["nv%d" % c], 191.75, 0.5)]
 
     def columns():
-        return [mm(T.LL[:, 64:96], T.qw[:, 15 - a:143 - a], T.z[:, a::16], a == 0, a == 15, ["qw", "z0", "z1"], ["LL"]) for a in range(16)] \
+        return [mm("col", T.LL[:, 64:96], T.qw[:, 15 - a:143 - a], T.z[:, a::16], a == 0, a == 15, ["qw", "z0", "z1"], "LL") for a in range(16)] \
             + [cp(T.ri[:], T.LL[:, 64:96], ["LL"], ["ri"]), ts(T.ri[:], T.ri[:], 7, OP.bitwise_and, ["ri"], ["ri"]),
-               tt(T.cm[:, 1::4, :], T.ri[:], T.c8[:], OP.add, ["ri", "c80", "c81"], ["cm1", "cm5"], 2),
+               tt(T.cm[:, 1::4, :], T.ri[:], T.c8[:], OP.add, ["ri", "c80", "c81"], ["cm1", "cm5"]),
                cp(T.cu[:, 0:32], T.cm[:, 1::4, :], ["cm1", "cm5"], ["cu"]),
-               act(T.vv[:], REC.indirect(T.cu[:, 0:32]), AF.Copy, XK + ["cu"], ["vv"], r=GATHER)]
+               act(T.vv[:], REC.indirect(T.cu[:, 0:32]), AF.Copy, XK + ["cu"], ["vv"])]
 
     def meet(t, c):
         r, k, f = T["RG%d%d" % (t, c)], "RG%d%d" % (t, c), 48 * c
-        out = [mm(T.LL[:, 32:64], T.idf[:], T.cm[:, 3 * c + 1:3 * c + 3, :], True, False, ["idf"] + ["cm%d" % j for j in (1, 2, 4, 5)], ["LL"], 4),
-               mm(T.Z1[:, 0:16], T.idf[:], T.cm[:, 0, :], True, False, ["idf", "cm0"], ["Z1"], 4)]
+        out = [mm("lm%d" % c, T.LL[:, 32:64], T.idf[:], T.cm[:, 3 * c + 1:3 * c + 3, :], True, False, ["idf"] + ["cm%d" % j for j in (1, 2, 4, 5)], "LL")]
         if t == 2 and c:
-            out.append(mm(T.LL[:, 48:64], T.idf[:], T.adj[:], False, False, ["adj"], ["LL"], 4))
-        out += [tt(T.wa[:], T.fin[:, c, :, 1::2], r[:, ::-1, 1::2], OP.mult, ["fs%d" % c, "fh%d" % c, k], ["wa"], 2)]
-        out += [tt(T.sb[:, 2, 14 + b:142:16], T.wa[:, 16 + 8 * b:24 + 8 * b], T.wa[:, 8 * b:8 * b + 8], OP.is_ge if rank < (rank ^ STEPS[t]) else OP.is_gt,
-                   ["wa"], ["sb2%d" % b], 2) for b in range(2)]
-        out += [tt(T.sb[:, c, 14 + b:142:16], T.sb[:, 2, 14 + b:142:16], T.k4[:, c, 16 * b + 1:16 * b + 16:2], OP.mult, ["sb2%d" % b, "kb%d" % c],
-                   ["sb%d%d" % (c, b)], 2) for b in range(2)]
-        sig = ["sb%d0" % c, "sb%d1" % c]
-        out += [mm(T.LL[:, 32:64], T.sb[:, 2, 14 - 2 * j:142 - 2 * j], T.ro[:, 48 * j + 16 * c:48 * j + 16 * c + 32], False, j == 7,
-                   ["sb20", "sb21", "ro"], ["LL"]) for j in range(8)] + [cp(T.ou[:, f + 16:f + 48], T.LL[:, 32:64], ["LL"], ["ou%d" % c])]
-        out += [mm(T.Z1[:, 0:16], T.sb[:, c, 14 - 2 * j:142 - 2 * j], T.ro[:, 48 * j + 16:48 * j + 32], False, j == 7,
-                   sig + ["ro"], ["Z1"]) for j in range(8)] + [cp(T.ou[:, f:f + 16], T.Z1[:, 0:16], ["Z1"], ["oj%d" % c])]
+            out.append(mm("lm1", T.LL[:, 48:64], T.idf[:], T.adj[:], False, False, ["adj"], "LL"))
+        beats = OP.is_ge if rank < (rank ^ STEPS[t]) else OP.is_gt
+        if c == 0:
+            out += [tt(T.wa[:], T.fin[:, 0, :, 1::2], r[:, ::-1, 1::2], OP.mult, ["fg0", "fh0", k], ["wa"]),
+                    tt(T.sb[:, 2, 7::8, :], T.wa[:, 0:16], T.wa[:, 16:32], beats, ["wa"], ["sb2"]),
+                    tt(T.sb[:, 0, 7::8, :], T.sb[:, 2, 7::8, :], T.k4[:, 0, 1::2], OP.mult, ["sb2", "kb0"], ["sb0"])]
+        else:
+            out += [cp(T.ks[:, 0::5], T.k4[:, 1, 1::2], ["kb1", "kz"], ["ks"])]
+            out += [tt(T.wb[:, :, 1 + i::5], T.fin[:, 1, :, 1::2], r[:, ::-1, i::4], OP.mult, ["fg1", "fh1", k, "wz"], ["wb%d" % i]) for i in range(4)]
+            out += [tt(T.fl[:], T.wb[:, 0], T.wb[:, 1], beats, ["wb%d" % i for i in range(4)], ["fl"]),
+                    scan(T.wk[:], T.fl[:], T.ks[:], OP.mult, OP.add, ["fl", "ks"], ["wk"]),
+                    ts(T.sb[:, 2, 7::8, :], T.wk[:, 4::5], 0.0, OP.is_gt, ["wk"], ["sb2"]),
+                    cp(T.sb[:, 1, 7::8, :], T.wk[:, 4::5], ["wk"], ["sb1"])]
+        out += spread("sm%d" % c, T.LL[:, 32:64], 2, lambda j: T.ro[:, j, c:c + 2, :], "LL")
+        out.append(cp(T.ou[:, f + 16:f + 48], T.LL[:, 32:64], ["LL"], ["ou%d" % c]))
         if t < 2:
-            out += [mm(T.HH[:, 1, 0, 0, 8 * c:8 * c + 8], T.o32[:], T.sb[:, c, 14 + b:142:16], b == 0, b == 1, ["o32"] + sig, ["HH"]) for b in range(2)]
-            if c:
-                out.append(vec(lambda q: q.tensor_reduce(T.a32[:], T.HH[:, 1, 0, 0, :], AX.X, OP.add), 16, ["HH"], ["a32"]))
-        return out
+            out.append(mm("ac%d" % c, T.HH[:, 1, 0, 16 * c:16 * c + 16], T.o32[:], T.wk[:, 4::5] if c else T.sb[:, 0, 7::8, :], True, True,
+                          ["o32", "wk" if c else "sb0"], "HH"))
+        if t < 2 and c:
+            out.append(o("v", lambda q: q.tensor_reduce(T.a32[:], T.HH[:, 1, 0, :], AX.X, OP.add), ["HH"], ["a32"]))
+        out.append(mm("lj%d" % c, T.Z1[:, 0:16], T.idf[:], T.cm[:, 0, :], True, False, ["idf", "cm0"], "Z1"))
+        out += spread("sj%d" % c, T.Z1[:, 0:16], c, lambda j: T.ro[:, j, 1, :], "Z1")
+        return out + [cp(T.ou[:, f:f + 16], T.Z1[:, 0:16], ["Z1"], ["oj%d" % c])]
 
     def scatter(c):
         win = T.X[:, SP + 2048:SP + 6144] if c else T.X[:, 0:SP + 2048]
-        return [tt(win.indirect(T.ou[:, OS[c]:OS[c] + 16]), T.cz[:, c, 512:768], T.m192[:], OP.add, ["nv%d" % c, "m192", "ou%d" % c], [XK[c]], SCATTER)]
+        return [tt(win.indirect(T.ou[:, OS[c] + 8 * h:OS[c] + 8 * h + 8]), T.cz[:, c, 512 + 128 * h:640 + 128 * h], T.m192[:], OP.add,
+                   ["nv%d" % c, "m192", "ou%d" % c], [XK[c]]) for h in range(2)]
 
     def demand(t, c):
-        out = [mm(T.S0[:, 0], T.idb[:], T.z[:, ln(c)], True, False, ["z%d" % c], ["S0"]),
-               mm(T.S0[:, 0], T.idb[:], T["RY%d%d" % (t, c)][:], False, True, ["RY%d%d" % (t, c)], ["S0"]),
-               act(T.cz[:, c, 0:256], T.S0[:, 0], AF.Identity, ["S0"], ["cl%d" % c], 191.75, 0.5),
+        s, bk = T["S%d" % c], "S%d" % c
+        out = [mm("zy%d" % c, s[:, 1], T.idb[:], T.z[:, ln(c)], True, False, ["z%d" % c], bk),
+               mm("zr%d" % c, s[:, 1], T.idb[:], T["RY%d%d" % (t, c)][:], False, True, ["RY%d%d" % (t, c)], bk),
+               act(T.cz[:, c, 0:256], s[:, 1], AF.Identity, [bk], ["cl%d" % c], 191.75, 0.5),
                act(T.za[:, ln(c)], T.cz[:, c, 0:512].indirect(T.ou[:, OZ[c]:OZ[c] + 16]), AF.Abs,
-                   ["nv%d" % c, "cl%d" % c, "ou%d" % c], ["za%d" % c], -192.0, r=GATHER),
-               ts(T.z[:, ln(c)], T.za[:, ln(c)], 1.0, OP.max, ["za%d" % c], ["z%d" % c], r=0.5)]
-        return out + (factor(c) if t < 2 else [dma("y", T.yz[:, ln(c)], T.z[:, ln(c)], ["z%d" % c], [], "sz%d" % c, 64)])
+                   ["nv%d" % c, "cl%d" % c, "ou%d" % c], ["za%d" % c], -192.0),
+               ts(T.z[:, ln(c)], T.za[:, ln(c)], 1.0, OP.max, ["za%d" % c], ["z%d" % c])]
+        return out + (factor(c) if t < 2 else [dma("y", "oz%d" % c, T.yz[:, ln(c)], T.z[:, ln(c)], ["z%d" % c], [], "sz%d" % c)])
 
     def names(t, c):
         k = "%d%d" % (t, c)
         src, rd = W(t, c)[:].indirect(T.ou[:, OJ[c]:OJ[c] + 16]), ["J" + k, "Jr" + k, "Wt" + k, "oj%d" % c]
         if t < 2:
-            return [act(W(t + 1, c)[:, 0:256], src, AF.Copy, rd, ["J%d%d" % (t + 1, c)], r=GATHER)]
-        return [act(T.jo[:, ln(c)], src, AF.Copy, rd, ["jo%d" % c], r=GATHER), dma("y", T.yj[:, ln(c)], T.jo[:, ln(c)], ["jo%d" % c], [], "sj%d" % c, 128)]
+            return [act(W(t + 1, c)[:, 0:256], src, AF.Copy, rd, ["J%d%d" % (t + 1, c)], name="j%d" % c)]
+        return [act(T.jo[:, ln(c)], src, AF.Copy, rd, ["jo%d" % c], name="j%d" % c),
+                dma("y", "oj%d" % c, T.yj[:, ln(c)], T.jo[:, ln(c)], ["jo%d" % c], [], "sj%d" % c)]
 
     def output(c):
         if c == 0:
-            return [ts(T.yo[:, SP:SP + 2048], T.X[:, SP + 2048:SP + 4096], 16.0, OP.mult, XK, ["Yp"], r=0.5),
-                    o("g", lambda q: q.dma_start(T.yo[:, SP:SP + 2048], T.X[:, SP:SP + 2048], accum_op=OP.add), XK + ["Yp"], ["Yp"],
-                      1000.0, 3000.0, ("pk", 16)),
-                    act(T.yv[:, 0:256], T.X[:, SP + 2048:SP + 4096].indirect(T.cu[:, 0:16]), AF.Identity, XK + ["cu"], ["e0"], -192.0, 16.0, GATHER),
-                   tt(T.yo[:, 0:SP + 2048].indirect(T.ou[:, OS[0]:OS[0] + 16]), T.cz[:, 0, 512:768], T.yv[:, 0:256], OP.add,
-                      ["nv0", "e0", "ou0", "Yp"], ["Y"], SCATTER)]
+            out = []
+            for i in range(4):
+                a, bk = SP + 512 * i, ("UU", "Z0")[i % 2]
+                out += [mm("pa%d" % i, T[bk][:], T.idb[:], T.X[:, a:a + 512], True, False, XK + ["idb"], bk),
+                        mm("pa%d" % i, T[bk][:], idx(16), T.X[:, a + 2048:a + 2560], False, True, XK + ["id16"], bk),
+                        act(T.yo[:, a:a + 512], T[bk][:], AF.Copy, [bk], ["Yp%d" % i])]
+            return out + [act(T.yv[:, 0:256], T.X[:, SP + 2048:SP + 4096].indirect(T.cu[:, 0:16]), AF.Identity, XK + ["cu"], ["e0"], -192.0, 16.0)] \
+                + [tt(T.yo[:, 0:SP + 2048].indirect(T.ou[:, OS[0] + 8 * h:OS[0] + 8 * h + 8]), T.cz[:, 0, 512 + 128 * h:640 + 128 * h], T.yv[:, 128 * h:128 * h + 128],
+                      OP.add, ["nv0", "e0", "ou0"] + ["Yp%d" % i for i in range(4)], ["Y"]) for h in range(2)]
         out = [ts(T.cu[:, 32:48], T.cm[:, 5, :], -2048.0, OP.add, ["cm5"], ["cu2"]),
-               act(T.nb[:, 0:256], T.yo[:, SP:SP + 2048].indirect(T.cu[:, 32:48]), AF.Copy, ["Y", "Yb", "cu2"], ["nb0"], r=GATHER),
-               mm(T.UU[:, 0:256], T.idb[:], T.nb[:, 0:256], True, False, ["nb0"], ["UU"]),
-               mm(T.UU[:, 0:256], idx(-16), T.vv[:, 256:512], False, False, ["vv", "id-16"], ["UU"]),
-               mm(T.UU[:, 0:256], idx(16), T.cz[:, 1, 512:768], False, True, ["nv1"], ["UU"]),
+               act(T.nb[:, 0:256], T.yo[:, SP:SP + 2048].indirect(T.cu[:, 32:48]), AF.Copy, ["Y", "Yb", "cu2"], ["nb0"]),
+               mm("pk", T.UU[:, 0:256], T.idb[:], T.nb[:, 0:256], True, False, ["nb0"], "UU"),
+               mm("pk", T.UU[:, 0:256], idx(-16), T.vv[:, 256:512], False, False, ["vv", "id-16"], "UU"),
+               mm("pk", T.UU[:, 0:256], idx(16), T.cz[:, 1, 512:768], False, True, ["nv1", "id16"], "UU"),
                act(T.yv[:, 256:512], T.UU[:, 0:256], AF.Identity, ["UU"], ["e1"], -3072.0)]
         for h in range(2):
             out += [cp(T.yo[:, SP + 1024 * h:SP + 4096].indirect(T.ou[:, OS[1] + 8 * h:OS[1] + 8 * h + 8]), T.yv[:, 256 + 128 * h:384 + 128 * h],
-                       ["e1", "ou1", "Y"], ["Yb"] + ["Yh%d" % j for j in range(h, 2)], SCATTER * 128),
-                    dma("y" if h else "s", T.yx[:, 1024 * h:1024 * h + 1024], T.yo[:, SP + 1024 * h:SP + 1024 * h + 1024], ["Yh%d" % h], [], "sy%d" % h, 256)]
+                       ["e1", "ou1", "Y"], ["Yb"] + ["Yh%d" % j for j in range(h, 2)]),
+                    dma("y", "oy%d" % h, T.yx[:, 1024 * h:1024 * h + 1024], T.yo[:, SP + 1024 * h:SP + 1024 * h + 1024],
+                        ["Yh%d" % h], [], "sy%d" % h)]
         return out
 
-    setup = len(ops)
-    ops += [cp(W(0, c)[:, 0:256], T.ji[:, ln(c)], ["ji%d" % c], ["J0%d" % c]) for c in range(2)] + tables(0, 0) + tables(0, 1)
+    ops += [cp(W(0, c)[:, 0:256], T.ji[:, ln(c)], ["ji%d" % c], ["J0%d" % c], "J%d" % c) for c in range(2)] + tables(0, 0) + tables(0, 1)
     ops += factor(0) + prod(0, 0) + factor(1)
     for t in range(3):
-        ops += hops(t, 0, 128) + (demand(t - 1, 1) if t else []) + quarter(0) + prod(t, 1) + hops(t, 1, 256) + columns() + quarter(1)
-        ops += search(t, 0) + quarter(2) + quarter(3) + profile(t, 0) + meet(t, 0) + names(t, 0) + demand(t, 0)
+        ops += hops(t, 0, 128) + (demand(t - 1, 1) if t else []) + quarter(t, 0)
+        ops += prod(t, 1) + hops(t, 1, 256) + columns() + quarter(t, 1)
+        ops += search(t, 0) + quarter(t, 2) + quarter(t, 3) + profile(t, 0) + meet(t, 0) + names(t, 0) + demand(t, 0)
         ops += (scatter(0) + prod(t + 1, 0) if t < 2 else output(0))
         ops += search(t, 1) + profile(t, 1) + meet(t, 1) + names(t, 1)
         ops += scatter(1) + tables(t + 1, 0) + tables(t + 1, 1) if t < 2 else output(1) + demand(t, 1)
-    scalar = scalar_line(0) + scalar_line(1) + scalar_line(2)
-    vector = "pi0 pi1 pi0 pi1 hu0 hu1".split() + vector_line(0) + vector_line(1) + vector_line(2)
-    emit(g, T, order(ops, setup, {"s": scalar, "y": ["z0", "Xl", "ji1"], "v": vector}))
+    emit(g, T, order(ops))

from concourse.bass import DstId, RemoteDMATransfer
from concourse.mybir import AluOpType as OP, AxisListType as AX, ActivationFunctionType as AF

STEPS = (5, 2, 7)
F, B, I, U = "float32", "bfloat16", "int32", "uint16"
SP = 2560
BIG = 4096.0
LIFT = 1.0 / 16
SCAN = (1, 3)
HELP = False
ZS = 3
PARTS = 4
PW = 512
VPICK = (64, 64, 64)

SCRATCH = {
    "X": ("sbuf", [128, SP + 6144], B), "yo": ("sbuf", [128, SP + 4096], B),
    "xg": ("sbuf", [128, 8192], B), "mg": ("sbuf", [128, 8192], B), "pg": ("sbuf", [128, 8192], B),
    "m0": ("sbuf", [128, 384], B), "zl": ("sbuf", [128, 3, 128], B), "zr": ("sbuf", [128, 6144], B), "rw": ("sbuf", [128, 3, 8, 32], B),
    "ji": ("sbuf", [128, 512], I), "z": ("sbuf", [128, 512], B), "za": ("sbuf", [128, 512], B), "w": ("sbuf", [128, 1], F),
    "jo": ("sbuf", [128, 512], F), "pi": ("sbuf", [128, 512], I), "hu": ("sbuf", [128, 512], U),
    "yy": ("sbuf", [128, 512], B), "vv": ("sbuf", [128, 512], B), "nb": ("sbuf", [128, 512], B),
    "cz": ("sbuf", [128, 2, 768], B), "yv": ("sbuf", [128, 512], B),
    "h0": ("sbuf", [128, 256], F), "h1": ("sbuf", [128, 256], F), "h2": ("sbuf", [128, 128], F), "h3": ("sbuf", [128, 64], F),
    "k1": ("sbuf", [128, 256], B), "k2": ("sbuf", [128, 128], B), "k3": ("sbuf", [128, 64], B),
    "pp": ("sbuf", [128, 128], F), "dd": ("sbuf", [128, 256], B), "fin": ("sbuf", [128, 2, 2, 32], F), "wa": ("sbuf", [128, 32], F),
    "four": ("sbuf", [128, 2, 64], F), "wb": ("sbuf", [128, 2, 80], F), "fl": ("sbuf", [128, 80], B), "ks": ("sbuf", [128, 80], B), "wk": ("sbuf", [128, 80], B),
    "k4": ("sbuf", [128, 2, 32], B), "sb": ("sbuf", [128, 4, 71, 2], B),
    "oy": ("sbuf", [128, 32], U), "ou": ("sbuf", [128, 96], U), "ri": ("sbuf", [128, 32], I), "cu": ("sbuf", [128, 48], U),
    "one": ("sbuf", [128, 256], B), "idb": ("sbuf", [128, 128], B), "ids": ("sbuf", [128, 6, 128], B),
    "idf": ("sbuf", [128, 128], F), "o32": ("sbuf", [128, 128], B),
    "bd": ("sbuf", [128, 128], B), "bd4": ("sbuf", [128, 2, 8, 16], B), "f4": ("sbuf", [128, 128], B), "kc": ("sbuf", [128, 256], B),
    "bdw": ("sbuf", [128, 128], B), "bdw2": ("sbuf", [128, 128], B), "qw": ("sbuf", [128, 144], B),
    "cst": ("sbuf", [128, 128], B), "mp": ("sbuf", [128, PW], B), "mr": ("sbuf", [128, PW], B), "m192": ("sbuf", [128, 128], B),
    "r8": ("sbuf", [128, 128], B), "ro": ("sbuf", [128, 8, 3, 16], B), "cm": ("sbuf", [128, 6, 16], F), "cy": ("sbuf", [128, 16], F),
    "c8": ("sbuf", [128, 32], F), "adj": ("sbuf", [128, 16], F), "i3": ("sbuf", [128, 16], I), "i4": ("sbuf", [128, 2], I),
    "pc": ("sbuf", [128, 2], F), "a1": ("sbuf", [128, 1], F), "a32": ("sbuf", [128, 1], F),
    "Z0": ("psum", [128, 512], F), "Z1": ("psum", [128, 512], F), "S0": ("psum", [128, 2, 256], F), "S1": ("psum", [128, 2, 256], F),
    "HH": ("psum", [128, 2, 8, 32], F), "UU": ("psum", [128, 512], F), "DZ": ("psum", [128, 512], F), "LL": ("psum", [128, 512], F),
}
SEMAPHORES = ["cv", "cs", "cp", "cg", "ldx", "ldj", "ldz", "ldw", "sy0", "sy1", "sj0", "sj1", "sz0", "sz1", "lt"]
for _t in range(3):
    for _c in range(2):
        SCRATCH["W%d%d" % (_t, _c)] = ("sbuf", [128, 17 * 256], F)
        SCRATCH["D%d%d" % (_t, _c)] = ("dram", [8, 32, 256], F)
        SCRATCH["RG%d%d" % (_t, _c)] = ("sbuf", [128, 2, 32 + 32 * _c], F)
        SCRATCH["RY%d%d" % (_t, _c)] = ("sbuf", [128, 256], B)
        for _k in ("aj", "ao", "ag", "ay", "lj", "lg", "ly", "do", "dt"):
            SEMAPHORES.append("%s%d%d" % (_k, _t, _c))
    SEMAPHORES += ["dp%d%d" % (_t, _p) for _p in range(PARTS)]
BANKS = ("Z0", "Z1", "S0", "S1", "HH", "UU", "DZ", "LL")
ESEM = {"v": "cv", "s": "cs", "p": "cp", "g": "cg"}
IDS = (16.0, -16.0, -2048.0, 2.0, -2.0, -1.0)

HEAD = {
    "v": "one cst0 zz qw i4a mr mp mr i4b bdw cst1 bd5 zl1 bd4 bdw2 id-2048 rw mr qw J0 pc mp zl3 pi0 pi1 pi0 cm0 rw1 hu0 pi1 J1 c80 rw0 id-1 "
         "pi2 pi3 hu1 c81 pi2 f4 rw2 ri hu2 ri",
    "s": "w ji nb0 zs nb1 zs zs",
    "p": "us0 uc0 us1 uz0 uq0 rq1 uc1 uz1 uq1 col ig0 ih0 rq0",
    "g": "i4 bd bd idb kc i3 sj0 zr0 zr0 zr0 sj1 " + "zr0 " * 9,
    "y": "z0 Xl",
}
ROUND = {
    "v": "pi1:12 idf:0 pi1:12 z1:12 hu1:12 x1 u00 sb0:0 ri:12 zl3:12 pi2:12 id2:0 u10 a1:0 pi3:12 u01 pi2:12 id-2:0 pg3 pi2:12 u11 hu2:12 "
         "n2 pg2 m3 m2 f2 pg0 pg5 pg4 pg6 ro2:0 cy:0 G0 pg8:01 ri:12 dd:0 "
         "pp tmp pg1 ro0:0 dd cm1 ro1:0 adj:0 H1 G1 K1 m20 m192:0 pp tmp m21 dd m22 H2 G2 m23 n6 pp tmp K2 pg10:2 m6 dd f6 n7 G3 H3 f7 m7 K3 "
         "pp tmp pg7 dd cu cm4:0 kb0 pg9:2 pg12:01 sb3 G0 fh0 fg0 "
         "pp tmp oy0 id-16:0 cu2:2 dd wz:0 pg8:2 kz:0 G1 H1 K1 pp tmp pg11:01 pg12:2 dd pg15 G2 H2 K2 cg pp tmp wa ch dd cm2:0 pg11:2 sb2 H3 G3 sb0 K3 "
         "pp tmp pg14 dd pg13:2 pg9:01 kb1 ou0 fg1 sb3 fh1 "
         "Y:2 ks:2 oy1:2 wb3:2 oj0:2 wb1:2 Y:2 wb0:2 wb2:2 z0:2 fl:2 wk:2 sb2:2 ou1:2 sb1:2 Yb:2 oj1:2 Yb:2 z1:2 "
         "pg13:01 wz:0 oj0:01 pg10:01 oy1:01 z0:01 wb3:01 wb2:01 wb0:01 wb1:01 o32:0 ks:01 fl:01 zl1:01 wk:01 X0:01 sb2:01 sb1:01 X0:01 "
         "pi0:01 a32:01 ou1:01 pi1:01 pi0:01 oj1:01 X1:01 pi0:01 X1:01 hu0:01 id16:0",
    "s": "cl1:12 za1:12 x0 nb1:12 x2 x3 x4 H0 x5 x6 x7 H0 vv Yp0:2 y0 e0:2 Yp1:2 nv0 Yp2:2 Yp3:2 cl0 za0 y1 j0 nb0:01 zs:01 nb0:2 nv1 e1:2 cl1:2 "
         "zs:01 za1:2 zs:01 j1",
    "p": "us1:12 uc1:12 uz1:12 col:12 uq1:12 hx0 gm00 rz1 hx1 hz1 gm01 gm1 ih1 rp2 ig1 rz3 pa0:2 gm20 ly0 hx2 gm21 gm22 lj0 gm23 hx3 hz3 gm3 sy0 "
         "dv0 pa1:2 pa2:2 dy0 uc0:01 zy0 lm0 pa3:2 sm0 zr0 sj0 ly1 sy1 dv1 lm1 us0:01 uz0:01 ac0:01 dy1 lj1 ac1:01 uq0:01 sm1 sj1:01 pk:2 zy1 zr1:01 "
         "ih0:01 sj1:2 rq0:01 zr1:2 ig0:01 rq1:01",
    "g": "r8:0 sj1:12 " + "zr0:12 " * 6 + "zr1 " * 15 + "sg0 sy0 sg1 sy1 " + "zr0:01 " * 5 + "sj0:01 zr0:01",
    "y": "do0 do1 dr0 dr1 wa0 wb0 wc0 wa1 wb1 wc1 oj0:2 oz0:2 oy0:2 oy1:2 oz1:2 oj1:2",
}


def line(eng):
    out = HEAD[eng].split()
    for t in range(3):
        out += [k.split(":")[0] for k in ROUND[eng].split() if ":" not in k or str(t) in k.split(":")[1]]
    return out


def order(ops):
    pred, lastw, readers, named = [set() for _ in ops], {}, {}, {}
    for i, (eng, fn, rd, wr, tok, name) in enumerate(ops):
        wr = wr + [k for k in rd if k in BANKS]
        for k in rd + wr:
            pred[i].update(lastw.get(k, []))
        for k in wr:
            pred[i].update(readers.get(k, []))
        for k in rd:
            readers.setdefault(k, []).append(i)
        for k in wr:
            lastw[k], readers[k] = [i], []
        pred[i].discard(i)
        if fn is None or eng in "py" and ops[i - 1][0] == eng and ops[i - 1][5] == name:
            group.append(i)
        else:
            group = [i]
            named.setdefault((eng, name), []).append(group)
    queue = {e: [i for k in line(e) for i in named[e, k].pop(0)] for e in HEAD}
    assert not any(named.values())
    out, done, at = [], set(), {e: 0 for e in queue}
    while len(out) < len(ops):
        n = len(out)
        for e, q in queue.items():
            while at[e] < len(q) and pred[q[at[e]]] <= done:
                done.add(q[at[e]])
                out.append(ops[q[at[e]]])
                at[e] += 1
        assert len(out) > n, [(e, at[e], ops[q[at[e]]][5], [ops[j][5] for j in pred[q[at[e]]] - done]) for e, q in queue.items() if at[e] < len(q)]
    return out


def emit(g, T, ops):
    Q = {"v": g.vector, "s": g.scalar, "p": g.tensor, "g": g, "y": g.sync}
    cnt = {e: 0 for e in ESEM}
    know = {e: {} for e in Q}
    clock = {}
    lastw, readers, bank, total, seen = {}, {}, {}, {}, {}
    for eng, fn, rd, wr, tok, _ in ops:
        deps = []
        for k in rd:
            if k not in BANKS:
                deps += lastw.get(k, [])
        for k in wr:
            if k not in BANKS:
                deps += lastw.get(k, []) + readers.get(k, [])
        for k in rd + wr:
            if k in BANKS:
                deps += [t for e, t in bank.get(k, {}).items() if e != eng]
        if eng == "p":
            deps = [d for d in deps if d[0] != "cp"]
        if fn is not None:
            kn = know[eng]
            for d in sorted(set(deps), key=lambda d: -d[1]):
                if kn.get(d[0], 0) < d[1] and d != tok:
                    Q[eng].wait_ge(T.sem[d[0]], d[1])
                    kn[d[0]] = d[1]
                    seen[d[0]] = max(seen.get(d[0], 0), d[1])
                    for s, v in clock.get(d, {}).items():
                        kn[s] = max(kn.get(s, 0), v)
            ins = fn(Q[eng])
            if tok is None:
                cnt[eng] += 1
                tok = (ESEM[eng], cnt[eng])
                ins.then_inc(T.sem[tok[0]], 1)
            elif ins is not None:
                ins.then_inc(T.sem[tok[0]], 16)
            ck = clock.setdefault(tok, {})
            for s, v in kn.items():
                ck[s] = max(ck.get(s, 0), v)
        total[tok[0]] = max(total.pop(tok[0], 0), tok[1])
        for k in rd:
            if k not in BANKS:
                readers.setdefault(k, []).append(tok)
        for k in wr:
            if k not in BANKS:
                lastw[k] = [tok]
                readers[k] = []
        for k in rd + wr:
            if k in BANKS:
                bank.setdefault(k, {})[eng] = tok
    for s, v in total.items():
        if seen.get(s, 0) < v:
            g.wait_ge(T.sem[s], v)


def helpers(T, topo, core):
    return [h for h in topo.cores_of(core) if topo.die(h) == topo.die(core) and h not in T.cores]


def hand_on(g, core, T, topo, rank, c):
    home = T.cores[rank]
    rid, pid, _ = topo.addr(home)
    for t in range(3):
        k = "%d%d" % (t, c)
        w, d, far = T["W" + k], T["D" + k], len(topo.engines(T.cores[rank ^ STEPS[t]], core))
        g.scalar.wait_ge(T.sem["ao" + k], len(topo.engines(home, core)) - far)
        g.scalar.dma_start(d[:, 0:16, :], w[:, 0:256]).then_inc(T.sem["do" + k], 16)
        g.sync.wait_ge(T.sem["aj" + k], far)
        g.sync.dma_start(d[:, 16:32, :], w[:, 4096:4352]).then_inc(T.sem["do" + k], 16)
        g.sync.wait_ge(T.sem["do" + k], 32)
        for s in range(1, 16):
            g.sync.dma_start(w[:, 256 * s:256 * s + 256], d[:, s:s + 16, :]).then_inc(T.sem["dp%d%d" % (t, (s - 1) * PARTS // 16)], 16)
        for p in range(PARTS):
            a, b = 1 + 16 * p // PARTS, 1 + 16 * (p + 1) // PARTS
            g.wait_ge(T.sem["dp%d%d" % (t, p)], 16 * (min(b, 16) - a))
            g.remote_dma(w[:, 256 * a:256 * b], w[:, 256 * a:256 * b], T.sem["dt" + k], T.sem["lt"], pid, rid, topo.mask(core, home))
    g.wait_ge(T.sem["lt"], 3 * PARTS * len(topo.engines(core, home)))


def rank_program(g, core, T, topo):
    rank = T.rank_of(core)
    if rank is None:
        for r, home in enumerate(T.cores):
            if HELP and core in helpers(T, topo, home)[0:2]:
                hand_on(g, core, T, topo, r, helpers(T, topo, home).index(core))
        return
    ops = []

    def o(eng, fn, rd, wr, name=None, tok=None):
        return (eng, fn, list(rd), list(wr), tok, name or wr[0])

    def tt(out, a, b, op, rd, wr):
        return o("v", lambda q: q.tensor_tensor(out, a, b, op), rd, wr)

    def ts(out, a, s1, op0, rd, wr, s2=None, op1=None):
        if op1 is None:
            return o("v", lambda q: q.tensor_scalar(out, a, s1, None, op0), rd, wr)
        return o("v", lambda q: q.tensor_scalar(out, a, s1, s2, op0, op1), rd, wr)

    def cp(out, a, rd, wr, name=None):
        return o("v", lambda q: q.tensor_copy(out, a), rd, wr, name)

    def ms(ap, c, wr):
        return o("v", lambda q: q.memset(ap, c), [], wr)

    def scan(out, a, b, op0, op1, rd, wr, first=0.0):
        return o("v", lambda q: q.tensor_tensor_scan(out, a, b, first, op0, op1), rd, wr)

    def act(out, a, fn, rd, wr, bias=0.0, scale=1.0, name=None):
        return o("s", lambda q: q.activation(out, a, fn, bias=bias, scale=scale), rd, wr, name)

    def mm(name, out, l, r, st, sp, rd, bk):
        return o("p", lambda q: q.matmul(out, l, r, st, sp), rd, [bk], name)

    def dma(eng, name, out, a, rd, wr, sem, n=1):
        return o(eng, lambda q: q.dma_start(out, a), rd, wr, name, (sem, 16 * n))

    def send(t, c, kind, dst, src, rd, land):
        peer = T.cores[rank ^ STEPS[t]]
        assert topo.may_write(core, peer)
        rid, pid, _ = topo.addr(peer)
        n = len(topo.engines(core, peer))
        back = len(topo.engines(peer, core))
        a, l, name = "a%s%d%d" % (kind, t, c), "l%s%d%d" % (kind, t, c), "s%s%d" % (kind, c)

        def f(q):
            q.remote_dma(dst, src, T.sem[a], T.sem[l], pid, rid, topo.mask(core, peer))
        return [o("g", f, rd, [], name, (l, n)), o("g", None, [], [land], name, (a, back))]

    def iota(out, pat, base, cm, wr, **kw):
        return o("g", lambda q: q.iota(out, pat, base, cm, **kw), [], wr)

    def asel(out, a, pat, cmp, base, cm, rd, wr, name=None):
        return o("g", lambda q: q.affine_select(out, a, pat, cmp, 0.0, base, cm), rd, wr, name)

    def W(t, c):
        return T["W%d%d" % (t, c)]

    def ln(c):
        return slice(256 * c, 256 * c + 256)

    def idx(v):
        return T.ids[:, IDS.index(v), :]

    REC = T.X[:, SP:SP + 4096]
    XK = ["X0", "X1", "Xl"]
    OJ, OS, OZ = (0, 48), (16, 80), (32, 64)

    ops += [dma("s", "w", T.w[:], T.wt[:], [], ["w"], "ldw"), dma("y", "z0", T.z[:], T.zd[:], [], ["z0", "z1"], "ldz"),
            dma("s", "ji", T.ji[:], T.jn[:], [], ["ji0", "ji1"], "ldj"), dma("y", "Xl", REC, T.xt[:], [], ["Xl"], "ldx")]
    small = dict(allow_small_or_imprecise_dtypes=True)
    ops += [ms(T.one[:], 1.0, ["one"]),
            asel(T.bd[:], T.one[:, 0:128], [[-16, 8], [0, 16]], OP.is_ge, 0, 1, ["one"], ["bd"]),
            asel(T.bd[:], T.bd[:], [[16, 8], [0, 16]], OP.is_ge, 15, -1, ["bd"], ["bd"]),
            asel(T.idb[:], T.one[:, 0:128], [[-1, 128]], OP.is_equal, 0, 1, ["one"], ["idb"]),
            iota(T.i3[:], [[16, 16]], 0, 0, ["i3"]), iota(T.i4[:], [[0, 2]], 0, 1, ["i4"]),
            iota(T.kc[:], [[0, 16], [1, 16]], 1, 0, ["kc"], **small),
            asel(T.r8[:], T.one[:, 0:128], [[-1, 8], [-8, 16]], OP.is_equal, 0, 1, ["one"], ["r8"]),
            ms(T.cst[0:64, :], 6144.0, ["cst0"]), ms(T.cst[64:128, :], 33.0 / 64, ["cst1"]),
            ms(T.mp[:], 1.0, ["mp"]), ms(T.dd[:], BIG * BIG, ["dd"]),
            ms(T.sb[:], 0.0, ["sb%d" % i for i in range(4)]), ms(T.mp[:, 0::16], 0.0, ["mp"]),
            ms(T.mr[:], 1.0, ["mr"]), ms(T.mr[:, 0::16], -1024.0, ["mr"]), ms(T.mr[:, 1::16], -1.0, ["mr"]),
            ms(T.zr[:, 0::16], 0.0, ["zz"]), ms(T.ks[:], 0.0, ["kz"]), ms(T.wb[:, 0], 0.0, ["wz"]), ms(T.wb[:, 1], 1.0, ["wz"]),
            ms(T.rw[0:1, 0], -1.0, ["rw0"]), ms(T.rw[0:1, 1:3], 0.0, ["rw"]), ms(T.rw[0:1, 1, :, 16:32], -1.0, ["rw1", "rw"]),
            cp(T.rw[0:1, 2, :, 0:16], T.kc[0:1, 0:128], ["kc", "rw"], ["rw2"]),
            ms(T.qw[:], 0.0, ["qw"]), ms(T.m192[:], -192.0, ["m192"]), ms(T.o32[:], 32.0, ["o32"]), ms(T.f4[0:1, :], BIG, ["f4"]),
            ts(T.bdw[:], T.bd[:], T.w[:], OP.mult, ["bd", "w"], ["bdw"]),
            ts(T.bdw2[:], T.bd[:], T.w[:], OP.mult, ["bd", "w"], ["bdw2"], 2.0, OP.mult),
            ts(T.bd4[:, 0], T.bd[:], BIG, OP.mult, ["bd"], ["bd4"]), ts(T.bd4[:, 1], T.bd[:], -BIG, OP.mult, ["bd"], ["bd5"]),
            cp(T.idf[:], T.idb[:], ["idb"], ["idf"]), cp(T.qw[:, 15:143:16], T.bdw[:, 0::16], ["bdw", "qw"], ["qw"]),
            ts(T.i4[:, 0:1], T.i4[:, 0:1], 15, OP.bitwise_and, ["i4"], ["i4a"]),
            ts(T.i4[:, 1:2], T.i4[:, 1:2], 1, OP.bitwise_and, ["i4"], ["i4b"]),
            cp(T.pc[:], T.i4[:], ["i4a", "i4b"], ["pc"]),
            ts(T.a1[:], T.pc[:, 1:2], 2040.0, OP.mult, ["pc"], ["a1"], -1.0, OP.add)]
    ops += [ts(idx(v), T.idb[:], v, OP.mult, ["idb"], ["id%d" % v]) for v in IDS]
    ops += [ts(T.ro[:, :, i, :], T.r8[:], v, OP.mult, ["r8"], ["ro%d" % i]) for i, v in enumerate((1.0 * SP, 256.0, 512.0 - SP))]
    ops += [ts(T.cm[:, j, :], T.i3[:], T.pc[:, 0:1], OP.add, ["i3", "pc"], ["cm%d" % j]) for j in (0, 2, 4)]
    ops += [ts(T.cy[:], T.cm[:, 0, :], 8.0, OP.mult, ["cm0", "a1"], ["cy"], T.a1[:], OP.add),
            ts(T.c8[:, 0:16], T.cm[:, 0, :], 8.0, OP.mult, ["cm0"], ["c80"]),
            ts(T.c8[:, 16:32], T.cm[:, 0, :], 8.0, OP.mult, ["cm0"], ["c81"], 2048.0, OP.add),
            ts(T.adj[:], T.i3[:], 128.0, OP.is_ge, ["i3"], ["adj"], -1024.0, OP.mult)]

    def tables(t, c):
        w, k = W(t, c), "%d%d" % (t, c)
        if not HELP:
            d, last = T["D" + k], ["RY%d1" % (t - 1)]
            out = send(t, c, "j", w[:, 4096:4352], w[:, 0:256], ["J" + k] + last, "Jr" + k)
            out += [dma("y", "do%d" % c, d[:, 0:16, :], w[:, 0:256], ["J" + k] + last, ["Do" + k], "do" + k),
                    dma("y", "dr%d" % c, d[:, 16:32, :], w[:, 4096:4352], ["Jr" + k], ["Dr" + k], "ao" + k)]
            return out + [dma("y", "w%s%d" % ("abc"[(s - 1) // 5], c), w[:, 256 * s:256 * s + 256], d[:, s:s + 16, :], ["Do" + k, "Dr" + k], ["Wt" + k],
                              "dt" + k, 15) for s in range(1, 16)]
        far, near = helpers(T, topo, T.cores[rank ^ STEPS[t]])[c], helpers(T, topo, core)[c]
        assert topo.may_write(core, far)
        mask = topo.mask(core, far)
        go = [RemoteDMATransfer(dst_ids=[DstId(rid=topo.addr(h)[0], pnc=topo.addr(h)[1])], dma_engine_mask=m, remote_sem=T.sem[s + k], src=w[:, 0:256], dst=dst)
              for h, m, s, dst in ((far, mask, "aj", w[:, 4096:4352]), (near, topo.mask(core, near) & ~mask, "ao", w[:, 0:256]))]

        def f(q):
            q.remote_dma_fused(go, local_sem=T.sem["lj" + k])
        return [o("g", f, ["J" + k] + ["RY%d1" % (t - 1)] * c, [], "sj%d" % c, ("lj" + k, len(topo.engines(core, near)))),
                o("g", None, [], ["Wt" + k], "sj%d" % c, ("dt" + k, PARTS * len(topo.engines(near, core))))]

    def factor(c):
        z, s, bk = "z%d" % c, T["S%d" % c], "S%d" % c
        return repeat(c) \
            + [mm("us%d" % c, s[:, 0], T.bdw[:], T.z[:, ln(c)], True, True, ["bdw", z], bk),
               act(T.nb[:, ln(c)], s[:, 0], AF.Identity, [bk], ["nb%d" % c], 191.5 + 1.0 / 2048, 1.0 / 1024),
               mm("uc%d" % c, T.UU[:, ln(c)], T.cst[:], T.one[:], True, False, ["cst0", "cst1", "one"], "UU"),
               mm("uz%d" % c, T.UU[:, ln(c)], T.bdw2[:], T.z[:, ln(c)], False, False, ["bdw2", z], "UU"),
               mm("uq%d" % c, T.UU[:, ln(c)], idx(-2048), T.nb[:, ln(c)], False, True, ["id-2048", "nb%d" % c], "UU")]

    def prod(t, c):
        src, k = (T.ji[:, ln(c)], "ji%d" % c) if t == 0 else (W(t, c)[:, 0:256], "J%d%d" % (t, c))
        return [tt(T.pi[:, 256 * c + 128 * b:256 * c + 128 * b + 128], src[:, b:256:2], T.UU[:, 256 * c + b:256 * c + 256:2], OP.mult,
                   [k, "UU"], ["pi%d" % (2 * c + b)]) for b in range(2)]

    def hops(t, c, w):
        out = []
        for a in range(256 * c, 256 * c + 256, w):
            sl, qs = slice(a, a + w), range(a // 128, (a + w) // 128)
            k = ["pi%d" % q for q in qs]
            if t > 0:
                out.append(ts(T.pi[:, sl], T.pi[:, sl], T.a32[:], OP.add, k + ["a32"], k))
            out.append(ts(T.pi[:, sl], T.pi[:, sl], 5, OP.arith_shift_right, k, k, 4095, OP.bitwise_and))
            out.append(cp(T.hu[:, sl], T.pi[:, sl], k, ["hu%d" % q for q in qs]))
        return out

    def xk(j):
        return ["x%d" % j] + ["w1"] * (j == 1)

    def pick(t, j):
        out, cut = [], VPICK[t] if j == 1 else 0
        for a, b in ((0, cut), (cut, 64)):
            if a < b:
                dst, src = T.xg[:, 1024 * j + 16 * a:1024 * j + 16 * b], REC.indirect(T.hu[:, 64 * j + a:64 * j + b])
                rd = XK + ["hu%d" % (j // 2)]
                out.append(act(dst, src, AF.Identity, rd, [xk(j)[-1]], LIFT * (j // 2 in SCAN)) if b > cut else ts(dst, src, LIFT * (0 in SCAN), OP.add, rd, ["x%d" % j]))
        return out

    def repeat(c):
        qs = [q for q in SCAN if q // 2 == c]
        a, b, k = SCAN.index(qs[0]), SCAN.index(qs[-1]) + 1, ["zl%d" % q for q in qs]
        return [ts(T.zl[:, SCAN.index(q)], T.z[:, 256 * c + q % 2:256 * c + 256:2], LIFT, OP.add, ["z%d" % c], ["zl%d" % q]) for q in qs] \
            + [act(T.zr[:, 2048 * a + r:2048 * b:16], T.zl[:, a:b], AF.Copy, k, ["zr%d%d" % (c, r)], name="zs") if c == 0 and r <= ZS else
               asel(T.zr[:, 2048 * a + r:2048 * b:16], T.zl[:, a:b], [[0, 128 * (b - a)]], OP.is_equal, 0, 0, k, ["zr%d%d" % (c, r)], "zr%d" % c)
               for r in range(1, 16)]

    def under(q):
        c, a, js = q // 2, 2048 * q, (2 * q, 2 * q + 1)
        if q == 0:
            out = []
            for j in js:
                zb = "Z%d" % j
                out += [mm("rq%d" % j, T[zb][:, r::8], T.idb[:], T.z[:, 128 * j:128 * j + 128:2], True, True, ["idb", "z0"], zb) for r in range(8)]
                out += [tt(T.mg[:, 1024 * j + h:1024 * j + 1024:2], T.xg[:, 1024 * j + h:1024 * j + 1024:2], T[zb][:], OP.min, xk(j) + [zb], ["u%d%d" % (j, h)])
                        for h in range(2)]
            return out, [["u%d%d" % (j, k % 2) for j in js] for k in range(16)]
        if q not in SCAN:
            return [mm("rp%d" % q, T.Z1[:, r::4], T.idb[:], T.z[:, 256 * c + q % 2:256 * c + 256:2], True, True, ["idb", "z%d" % c], "Z1") for r in range(4)] \
                + [tt(T.mg[:, a + h:a + 2048:4], T.xg[:, a + h:a + 2048:4], T.Z1[:], OP.min, xk(js[0]) + xk(js[1]) + ["Z1"], ["m%d%d" % (q, h)]) for h in range(4)], \
                [["m%d%d" % (q, k % 4)] for k in range(16)]
        i, out = SCAN.index(q), []
        out.append(mm("rz%d" % q, T.Z0[:, 128 * i:128 * i + 128], idx(-1), T.zl[:, i], True, True, ["id-1", "zl%d" % q], "Z0"))
        parts = [(js, 0, 128)] if c == 0 else [(js[0:1], 0, 64), (js[1:2], 64, 128)]
        for ps, lo, hi in parts:
            first, k = T.xg[:, a + 16 * lo:a + 16 * hi:16], [x for j in ps for x in xk(j)]
            n = ["n%d" % j for j in ps]
            out += [ts(first, first, -1.0, OP.mult, k, n),
                    tt(T.m0[:, 128 * i + lo:128 * i + hi], first, T.Z0[:, 128 * i + lo:128 * i + hi], OP.max, k + n + ["Z0"], ["f%d" % j for j in ps])]
        out += [scan(T.mg[:, 1024 * j:1024 * j + 1024], T.zr[:, 2048 * i + 1024 * (j % 2):2048 * i + 1024 * (j % 2) + 1024], T.xg[:, 1024 * j:1024 * j + 1024],
                     OP.max, OP.min, xk(j) + ["zz", "n%d" % j] + ["zr%d%d" % (c, r) for r in range(1, 16)], ["m%d" % j]) for j in js]
        return out, [["%s%d" % ("m" if k else "f", j) for j in js] for k in range(16)]

    def quarter(t, q):
        c, b, up = q // 2, q % 2, q in SCAN
        s, bk = T["S%d" % c], "S%d" % c
        mins, keys = under(q)
        out = pick(t, 2 * q) + pick(t, 2 * q + 1) + mins
        if b == 0:
            out.append(mm("ig%d" % c, s[:, 1], T.f4[0:1, :], T.rw[0:1, int(not up)], True, False, ["f4", "rw0", "rw1"], bk))
        if not up:
            out.append(mm("ih%d" % c, T.HH[:, 0], T.f4[0:1, :], T.rw[0:1, 2], True, False, ["f4", "rw2"], "HH"))
        out += [mm("hx%d" % q if k or not up else "hz%d" % q, T.HH[:, 0, :, 16 * b + k:16 * b + 16], T.xg[:, 2048 * q + k:2048 * q + 2048:16],
                   T.bd4[:, int(up and k == 0), :, k:16], False, b == 1 and k == 0,
                   xk(2 * q) + xk(2 * q + 1) + ["bd4"] + ["bd5", "n%d" % (2 * q), "n%d" % (2 * q + 1)] * (up and k == 0), "HH") for k in range(15, -1, -1)]
        ks = sorted(range(16), key=lambda k: keys[k])
        out += [mm("gm%d%s" % (q, "" if up else keys[k][0][-1]), s[:, 1, 16 * b + k::32],
                   T.m0[:, 128 * SCAN.index(q):128 * SCAN.index(q) + 128] if up and k == 0 else T.mg[:, 2048 * q + k:2048 * q + 2048:16],
                   T.bd4[:, int(up and k == 0), :, 0], False, b == 1 and k == ks[-1], keys[k], bk) for k in ks]
        if b:
            out += [act(T.h0[:], T.HH[:, 0], AF.Copy, ["HH"], ["H0"]), scan(s[:, 0], T.mp[:, 0:256], s[:, 1], OP.mult, OP.add, ["mp", bk], ["G0"])]
        return out + [scan(T.pg[:, PW * i:PW * i + PW], (T.mr if up else T.mp)[:], T.xg[:, PW * i:PW * i + PW], OP.mult, OP.max, ["mr" if up else "mp", "n%d" % (i * PW // 1024)] + xk(i * PW // 1024),
                           ["pg%d" % i], 1.0 * up) for i in range(2048 * q // PW, 2048 * (q + 1) // PW)]

    def search(t, c):
        s, bk = T["S%d" % c], "S%d" % c
        Go = [s[:, 1, :], s[:, 0, 0:128], s[:, 1, 0:64], T.fin[:, c, 0, :]]
        Ho = [T.h1[:], T.h2[:], T.h3[:], T.fin[:, c, 1, :]]
        Ko = [T.k1[:], T.k2[:], T.k3[:], T.k4[:, c, :]]
        out = []
        for lv in range(4):
            n, w = 128 >> lv, min(lv, 1) + 1
            every, a, b = slice(w - 1, 2 * n * w, w), slice(w - 1, 2 * n * w, 2 * w), slice(2 * w - 1, 2 * n * w, 2 * w)
            h, k, r = (T.h0, T.h1, T.h2, T.h3)[lv], (T.kc, T.k1, T.k2, T.k3)[lv], lv % 2
            d, last, tmp, gk, hk = T.dd[:, 0:2 * n], lv == 3, s[:, 1 - r, 128:128 + n], "G%d" % lv, "H%d" % lv
            out += [tt(T.pp[:, 0:n], h[:, a], s[:, r, b], OP.mult, [gk, bk, hk], ["pp"]),
                    tt(tmp, h[:, b], s[:, r, a], OP.mult, [gk, bk, hk], ["tmp"]),
                    tt(T.dd[:, 1:2 * n:2], T.pp[:, 0:n], tmp, OP.subtract, ["pp", "tmp", bk], ["dd"]),
                    scan(Go[lv], d, s[:, r, every], OP.max, OP.min, ["dd", bk, gk], ["fg%d" % c if last else "G%d" % (lv + 1)]),
                    scan(Ho[lv], d, h[:, every], OP.max, OP.min, ["dd", hk], ["fh%d" % c if last else "H%d" % (lv + 1)]),
                    scan(Ko[lv], d, k[:, every], OP.max, OP.min, ["dd", "kc", "K%d" % lv], ["kb%d" % c if last else "K%d" % (lv + 1)])]
            if c and lv == 1:
                out += [cp(T.four[:, 0], s[:, 0, 1:128:2], [bk, "G2"], ["cg"]), cp(T.four[:, 1], T.h2[:, 1::2], ["H2"], ["ch"])]
                out += send(t, c, "g", T["RG%d1" % t][:], T.four[:], ["cg", "ch"], "RG%d1" % t)
        return out + ([] if c else send(t, c, "g", T["RG%d0" % t][:], T.fin[:, 0], ["fg0", "fh0"], "RG%d0" % t))

    def spread(name, out, i, cols, bk):
        return [mm(name, out, T.sb[:, i, 7 - j:71 - j, :], cols(j), False, j == 7, ["sb%d" % i, "r8", "ro0", "ro1", "ro2"], bk) for j in range(8)]

    def profile(t, c):
        k = "y%d" % c
        return [mm("ly%d" % c, T.LL[:, 0:16], T.idf[:], T.cy[:], True, False, ["idf", "cy"], "LL"),
                cp(T.sb[:, 3, 7::8, :], T.k4[:, c, 1::2], ["kb%d" % c], ["sb3"])] \
            + spread("sy%d" % c, T.LL[:, 0:16], 3, lambda j: T.r8[:, 16 * j:16 * j + 16], "LL") \
            + [cp(T.oy[:, 16 * c:16 * c + 16], T.LL[:, 0:16], ["LL"], ["oy%d" % c]),
               act(T.yy[:, ln(c)], T.pg[:, 4096 * c:4096 * (c + 1)].indirect(T.oy[:, 16 * c:16 * c + 16]), AF.Abs,
                   ["pg%d" % i for i in range(4096 * c // PW, 4096 * (c + 1) // PW)] + ["oy%d" % c], [k])] \
            + send(t, c, "y", T["RY%d%d" % (t, c)][:], T.yy[:, ln(c)], [k], "RY%d%d" % (t, c)) \
            + [mm("dv%d" % c, T.DZ[:, 256:512], T.idb[:], T.vv[:, ln(c)], True, False, ["idb", "vv"], "DZ"),
               mm("dv%d" % c, T.DZ[:, 0:256], idx(2), T.z[:, ln(c)], False, False, ["id2", "z%d" % c], "DZ"),
               mm("dy%d" % c, T.DZ[:, 256:512], T.idb[:], T.yy[:, ln(c)], False, False, [k], "DZ"),
               mm("dy%d" % c, T.DZ[:, 0:256], idx(-2), T.yy[:, ln(c)], False, True, ["id-2", k], "DZ"),
               act(T.cz[:, c, 256:768], T.DZ[:], AF.Identity, ["DZ"], ["nv%d" % c], 191.75, 0.5)]

    def columns():
        return [mm("col", T.LL[:, 64:96], T.qw[:, 15 - a:143 - a], T.z[:, a::16], a == 0, a == 15, ["qw", "z0", "z1"], "LL") for a in range(16)] \
            + [cp(T.ri[:], T.LL[:, 64:96], ["LL"], ["ri"]), ts(T.ri[:], T.ri[:], 7, OP.bitwise_and, ["ri"], ["ri"]),
               tt(T.cm[:, 1::4, :], T.ri[:], T.c8[:], OP.add, ["ri", "c80", "c81"], ["cm1", "cm5"]),
               cp(T.cu[:, 0:32], T.cm[:, 1::4, :], ["cm1", "cm5"], ["cu"]),
               act(T.vv[:], REC.indirect(T.cu[:, 0:32]), AF.Copy, XK + ["cu"], ["vv"])]

    def meet(t, c):
        r, k, f = T["RG%d%d" % (t, c)], "RG%d%d" % (t, c), 48 * c
        out = [mm("lm%d" % c, T.LL[:, 32:64], T.idf[:], T.cm[:, 3 * c + 1:3 * c + 3, :], True, False, ["idf"] + ["cm%d" % j for j in (1, 2, 4, 5)], "LL")]
        if t == 2 and c:
            out.append(mm("lm1", T.LL[:, 48:64], T.idf[:], T.adj[:], False, False, ["adj"], "LL"))
        beats = OP.is_ge if rank < (rank ^ STEPS[t]) else OP.is_gt
        if c == 0:
            out += [tt(T.wa[:], T.fin[:, 0, :, 1::2], r[:, ::-1, 1::2], OP.mult, ["fg0", "fh0", k], ["wa"]),
                    tt(T.sb[:, 2, 7::8, :], T.wa[:, 0:16], T.wa[:, 16:32], beats, ["wa"], ["sb2"]),
                    tt(T.sb[:, 0, 7::8, :], T.sb[:, 2, 7::8, :], T.k4[:, 0, 1::2], OP.mult, ["sb2", "kb0"], ["sb0"])]
        else:
            out += [cp(T.ks[:, 0::5], T.k4[:, 1, 1::2], ["kb1", "kz"], ["ks"])]
            out += [tt(T.wb[:, :, 1 + i::5], T.fin[:, 1, :, 1::2], r[:, ::-1, i::4], OP.mult, ["fg1", "fh1", k, "wz"], ["wb%d" % i]) for i in range(4)]
            out += [tt(T.fl[:], T.wb[:, 0], T.wb[:, 1], beats, ["wb%d" % i for i in range(4)], ["fl"]),
                    scan(T.wk[:], T.fl[:], T.ks[:], OP.mult, OP.add, ["fl", "ks"], ["wk"]),
                    ts(T.sb[:, 2, 7::8, :], T.wk[:, 4::5], 0.0, OP.is_gt, ["wk"], ["sb2"]),
                    cp(T.sb[:, 1, 7::8, :], T.wk[:, 4::5], ["wk"], ["sb1"])]
        out += spread("sm%d" % c, T.LL[:, 32:64], 2, lambda j: T.ro[:, j, c:c + 2, :], "LL")
        out.append(cp(T.ou[:, f + 16:f + 48], T.LL[:, 32:64], ["LL"], ["ou%d" % c]))
        if t < 2:
            out.append(mm("ac%d" % c, T.HH[:, 1, 0, 16 * c:16 * c + 16], T.o32[:], T.wk[:, 4::5] if c else T.sb[:, 0, 7::8, :], True, True,
                          ["o32", "wk" if c else "sb0"], "HH"))
        if t < 2 and c:
            out.append(o("v", lambda q: q.tensor_reduce(T.a32[:], T.HH[:, 1, 0, :], AX.X, OP.add), ["HH"], ["a32"]))
        out.append(mm("lj%d" % c, T.Z1[:, 0:16], T.idf[:], T.cm[:, 0, :], True, False, ["idf", "cm0"], "Z1"))
        out += spread("sj%d" % c, T.Z1[:, 0:16], c, lambda j: T.ro[:, j, 1, :], "Z1")
        return out + [cp(T.ou[:, f:f + 16], T.Z1[:, 0:16], ["Z1"], ["oj%d" % c])]

    def scatter(c):
        win = T.X[:, SP + 2048:SP + 6144] if c else T.X[:, 0:SP + 2048]
        return [tt(win.indirect(T.ou[:, OS[c] + 8 * h:OS[c] + 8 * h + 8]), T.cz[:, c, 512 + 128 * h:640 + 128 * h], T.m192[:], OP.add,
                   ["nv%d" % c, "m192", "ou%d" % c], [XK[c]]) for h in range(2)]

    def demand(t, c):
        s, bk = T["S%d" % c], "S%d" % c
        out = [mm("zy%d" % c, s[:, 1], T.idb[:], T.z[:, ln(c)], True, False, ["z%d" % c], bk),
               mm("zr%d" % c, s[:, 1], T.idb[:], T["RY%d%d" % (t, c)][:], False, True, ["RY%d%d" % (t, c)], bk),
               act(T.cz[:, c, 0:256], s[:, 1], AF.Identity, [bk], ["cl%d" % c], 191.75, 0.5),
               act(T.za[:, ln(c)], T.cz[:, c, 0:512].indirect(T.ou[:, OZ[c]:OZ[c] + 16]), AF.Abs,
                   ["nv%d" % c, "cl%d" % c, "ou%d" % c], ["za%d" % c], -192.0),
               ts(T.z[:, ln(c)], T.za[:, ln(c)], 1.0, OP.max, ["za%d" % c], ["z%d" % c])]
        return out + (factor(c) if t < 2 else [dma("y", "oz%d" % c, T.yz[:, ln(c)], T.z[:, ln(c)], ["z%d" % c], [], "sz%d" % c)])

    def names(t, c):
        k = "%d%d" % (t, c)
        src, rd = W(t, c)[:].indirect(T.ou[:, OJ[c]:OJ[c] + 16]), ["J" + k, "Jr" + k, "Wt" + k, "oj%d" % c]
        if t < 2:
            return [act(W(t + 1, c)[:, 0:256], src, AF.Copy, rd, ["J%d%d" % (t + 1, c)], name="j%d" % c)]
        return [act(T.jo[:, ln(c)], src, AF.Copy, rd, ["jo%d" % c], name="j%d" % c),
                dma("y", "oj%d" % c, T.yj[:, ln(c)], T.jo[:, ln(c)], ["jo%d" % c], [], "sj%d" % c)]

    def output(c):
        if c == 0:
            out = []
            for i in range(4):
                a, bk = SP + 512 * i, ("UU", "Z0")[i % 2]
                out += [mm("pa%d" % i, T[bk][:], T.idb[:], T.X[:, a:a + 512], True, False, XK + ["idb"], bk),
                        mm("pa%d" % i, T[bk][:], idx(16), T.X[:, a + 2048:a + 2560], False, True, XK + ["id16"], bk),
                        act(T.yo[:, a:a + 512], T[bk][:], AF.Copy, [bk], ["Yp%d" % i])]
            return out + [act(T.yv[:, 0:256], T.X[:, SP + 2048:SP + 4096].indirect(T.cu[:, 0:16]), AF.Identity, XK + ["cu"], ["e0"], -192.0, 16.0)] \
                + [tt(T.yo[:, 0:SP + 2048].indirect(T.ou[:, OS[0] + 8 * h:OS[0] + 8 * h + 8]), T.cz[:, 0, 512 + 128 * h:640 + 128 * h], T.yv[:, 128 * h:128 * h + 128],
                      OP.add, ["nv0", "e0", "ou0"] + ["Yp%d" % i for i in range(4)], ["Y"]) for h in range(2)]
        out = [ts(T.cu[:, 32:48], T.cm[:, 5, :], -2048.0, OP.add, ["cm5"], ["cu2"]),
               act(T.nb[:, 0:256], T.yo[:, SP:SP + 2048].indirect(T.cu[:, 32:48]), AF.Copy, ["Y", "Yb", "cu2"], ["nb0"]),
               mm("pk", T.UU[:, 0:256], T.idb[:], T.nb[:, 0:256], True, False, ["nb0"], "UU"),
               mm("pk", T.UU[:, 0:256], idx(-16), T.vv[:, 256:512], False, False, ["vv", "id-16"], "UU"),
               mm("pk", T.UU[:, 0:256], idx(16), T.cz[:, 1, 512:768], False, True, ["nv1", "id16"], "UU"),
               act(T.yv[:, 256:512], T.UU[:, 0:256], AF.Identity, ["UU"], ["e1"], -3072.0)]
        for h in range(2):
            out += [cp(T.yo[:, SP + 1024 * h:SP + 4096].indirect(T.ou[:, OS[1] + 8 * h:OS[1] + 8 * h + 8]), T.yv[:, 256 + 128 * h:384 + 128 * h],
                       ["e1", "ou1", "Y"], ["Yb"] + ["Yh%d" % j for j in range(h, 2)]),
                    dma("y", "oy%d" % h, T.yx[:, 1024 * h:1024 * h + 1024], T.yo[:, SP + 1024 * h:SP + 1024 * h + 1024],
                        ["Yh%d" % h], [], "sy%d" % h)]
        return out

    ops += [cp(W(0, c)[:, 0:256], T.ji[:, ln(c)], ["ji%d" % c], ["J0%d" % c], "J%d" % c) for c in range(2)] + tables(0, 0) + tables(0, 1)
    ops += factor(0) + prod(0, 0) + factor(1)
    for t in range(3):
        ops += hops(t, 0, 128) + (demand(t - 1, 1) if t else []) + quarter(t, 0)
        ops += prod(t, 1) + hops(t, 1, 256) + columns() + quarter(t, 1)
        ops += search(t, 0) + quarter(t, 2) + quarter(t, 3) + profile(t, 0) + meet(t, 0) + names(t, 0) + demand(t, 0)
        ops += (scatter(0) + prod(t + 1, 0) if t < 2 else output(0))
        ops += search(t, 1) + profile(t, 1) + meet(t, 1) + names(t, 1)
        ops += scatter(1) + tables(t + 1, 0) + tables(t + 1, 1) if t < 2 else output(1) + demand(t, 1)
    emit(g, T, order(ops))
